import numpy as np, ml_dtypes
CORES = [1,5,17,21,33,37,49,53]
N = 8
import mx_ref
BF = ml_dtypes.bfloat16
def gentries(a):
    return np.ascontiguousarray(a.reshape(8, 16, -1).transpose(0, 2, 1)).reshape(8, -1)
def gtable(e):
    e = np.asarray(e); return np.ascontiguousarray(e.reshape(8, -1, 16).transpose(0, 2, 1)).reshape(128, -1).astype(np.int32)
def gcols(t, e):
    v = np.concatenate([t.reshape(8, 16, -1, 4), np.zeros((8, 16, 1, 4), BF)], axis=2)
    return np.ascontiguousarray(np.stack([v[g][:, e[g]] for g in range(8)])).reshape(128, -1)
def tile(rs):
    return np.stack(rs, axis=2).reshape(128, -1).astype(BF)
def cut(t, i, w=512):
    return t[:, w * i:w * i + w]
def pick(q, e):
    c = np.concatenate([q[0].reshape(128, -1, 4), np.zeros((128, 1, 4), np.uint8)], axis=1); s = np.concatenate([q[1], np.ones((16, 1), np.uint8)], axis=1)
    return (np.ascontiguousarray(c[:, e].reshape(128, -1)), np.ascontiguousarray(s[:, e]))
def join(*qs):
    return (np.concatenate([q[0] for q in qs], axis=1), np.concatenate([q[1] for q in qs], axis=1))
def put(q, e, v):
    c, s = q[0].reshape(128, -1, 4).copy(), q[1].copy(); c[:, e] = v[0].reshape(128, -1, 4); s[:, e] = v[1]
    return (c.reshape(128, -1), s)
def pk(c, s):
    return (np.ascontiguousarray(c), mx_ref.live(s))
def emit(q):
    return q[0], q[1]
def packed(v, rng):
    q = [mx_ref.quantize(np.ascontiguousarray(v[r])) for r in range(N)]
    return np.stack([a for a, b in q]), np.stack([mx_ref.plane(b, rng) for a, b in q])
def values_of_codes():
    e, c = np.zeros((128, 128, 4), np.float32), np.zeros((128, 2, 4), np.uint8)
    e[np.arange(128), np.arange(128), 0] = 1
    c[:127, :, 0] = np.arange(256).reshape(2, 128).T[:127]
    return mx_ref.matmul(mx_ref.quantize(e.reshape(128, 512).astype(BF)), (c.reshape(128, 8), np.full((16, 2), 127, np.uint8))).T.reshape(-1).astype(np.float64)
CODE_VALUE, SCALE_VALUE = values_of_codes(), 2.0 ** (np.arange(256) - 127.0)
def decode(q):
    return (CODE_VALUE[q[0]].reshape(16, 8, -1, 4) * SCALE_VALUE[q[1]][:, None, :, None] + 0.0).reshape(128, -1).astype(np.float32)
def f(rng, *shape):
    return mx_ref.flush((rng.standard_normal(shape, dtype=np.float32) * np.exp2(rng.integers(-2, 3, shape[:-1] + (1,)))).astype(BF))
def wide(rng, *shape, cols=0):
    v = rng.standard_normal(shape, dtype=np.float32) * np.exp2(rng.integers(-12, 13, shape)).astype(np.float32)
    if cols: v *= np.repeat(np.exp2(rng.integers(-cols, cols + 1, shape[:-2] + (1, shape[-1] // 4))) * (rng.random(shape[:-2] + (1, shape[-1] // 4)) > 0.0625), 4, axis=-1).astype(np.float32)
    return mx_ref.flush(v.astype(BF))
C, V, L, K, R = 256, 4, 4, 64, 3
def order(s, names):
    by = np.argsort(np.argsort(-s, axis=1, kind="stable"), axis=1)
    place = np.where(by == 0, 0, C)
    for t in range(L):
        first = np.min(np.take_along_axis(place, names.reshape(8, -1), axis=1).reshape(8, C, V), axis=2)
        new = (place == C) & (first < C)
        key = np.where(new, first * C + by, C * C)
        n = np.sum(place < C, axis=1)
        place = np.where(new, n[:, None] + np.argsort(np.argsort(key, axis=1, kind="stable"), axis=1), place)
    return np.argsort(place, axis=1, kind="stable")
def big(v):
    v = v.astype(np.float32)
    v[np.abs(v) < np.float32(2.0 ** -16)] = 0
    return v.astype(BF)
def numbers_of(rng):
    return {"x": big(f(rng, N, 128, 4 * C)), "u": np.array(f(rng, N, 128, 512)), "v": np.array(f(rng, N, 128, 512))}
def names_of(rng):
    return rng.integers(0, C, (N, 8, C, V))
def stored(l):
    return {"nb": np.stack([gtable(e.reshape(8, -1)) for e in l])}
def weights(rng, w):
    c, p = packed(w, rng)
    return {"wc": c, "ws": p}
def still(rng):
    w = np.zeros((N, 128, 4, 128, 4), np.float32)
    i = np.arange(128)
    for b in range(4): w[:, i, b, i, b] = 32
    return weights(rng, w.reshape(N, 128, 2048).astype(BF))
def signs(rng):
    return np.stack([rng.permutation(8) % 2 * 2.0 - 1.0 for r in range(N)])
def setup_inputs(rng):
    return {**numbers_of(rng), **stored(names_of(rng)), **weights(rng, f(rng, N, 128, 2048))}
def setup_inputs_ties(rng):
    d = numbers_of(rng)
    e = rng.permutation(N)
    x = d["x"].reshape(N, 8, 16, C, 4)
    for r in range(N):
        k = np.zeros(C, int) if r == e[0] else rng.permutation(C) % 3
        a = x[r][:, :8, :3].copy()
        a[:, :, 2] = 0
        x[r][:, :8] = a[:, :, k]
    x[e[1]] = 0
    u = d["u"].reshape(N, 8, 16, 128, 4)
    u[:, :, 8:, ::16] = 0
    w = np.array(f(rng, N, 128, 2048)).reshape(N, 8, 16, 4, 8, 16, 4)
    w[:, :, 8:, :, :, :8] = 0
    return {"x": x.reshape(N, 128, 4 * C), "u": u.reshape(N, 128, 512), "v": d["v"], **stored(names_of(rng)), **weights(rng, w.reshape(N, 128, 2048))}
def setup_inputs_near(rng):
    d, l = numbers_of(rng), names_of(rng)
    x = d["x"].astype(np.float32).reshape(N, 8, 16, C, 4)
    s = np.arange(C) // 2
    g = ((s[:, None] >> np.arange(8)) & 1) * np.exp2(np.arange(8) - 23.0)
    x[:, :, 0] = 0
    x[:, :, 0, :, 0] = 1
    x[:, :, 8] = g[:, :4]
    x[:, :, 9] = g[:, 4:]
    x[:, :, 10:] = rng.integers(4, 8, (N, 8, 6, C, 4)) * rng.choice([-1.0, 1.0], (N, 8, 6, C, 4)) * 2.0 ** -20
    u = d["u"].reshape(N, 128, 128, 4)
    k = np.where(rng.permutation(N) < N // 2, 2.0 ** -30, 1.0)
    a = k[:, None] * signs(rng)
    a[np.ix_(np.flatnonzero(k < 1), rng.permutation(8)[:2])] = 0
    a = a.astype(np.float32).astype(BF)
    k = k.astype(np.float32).astype(BF)
    u[:, :, ::16] = 0
    for h in range(0, 128, 16):
        u[:, h, h, 0] = a[:, h // 16]
        u[:, h + 8:h + 10, h] = k[:, None, None]
    l[:, :, :C // 4, 0] = C - 2
    l[:, :, 1::2] = l[:, :, ::2]
    return {"x": x.reshape(N, 128, 4 * C).astype(BF), "u": u.reshape(N, 128, 512), "v": d["v"], **stored(l), **still(rng)}
def setup_inputs_huge(rng):
    d = numbers_of(rng)
    x = 2.0 ** 30 * (0.6 + 0.4 * rng.random((N, 128, C, 4)))
    c = np.stack([rng.permutation(C) % 2 * 2.0 - 1.0 for r in range(N)])
    c[rng.permutation(N) < N // 2] = 1
    x *= c[:, None, :, None]
    u = d["u"].reshape(N, 128, 128, 4)
    a = 2.0 ** 30 * (1 - 0.25 * rng.random((N, 128, 8, 4))) * signs(rng)[:, None, :, None]
    u[:, :, ::16] = a.astype(np.float32).astype(BF)
    return {"x": x.astype(np.float32).reshape(N, 128, 4 * C).astype(BF), "u": u.reshape(N, 128, 512), "v": d["v"], **stored(names_of(rng)), **still(rng)}
def setup_inputs_graphs(rng):
    d, l = numbers_of(rng), names_of(rng)
    o = rng.permutation(N)
    x = d["x"].reshape(N, 8, 16, C, 4)
    u = d["u"].reshape(N, 128, 128, 4)
    u[:, ::16, ::16, 0] = np.eye(8, dtype=np.float32).astype(BF)
    for r in range(N):
        for g in range(8):
            e = rng.permutation(C)
            x[r, g, 0, e[0], 0] = 16384
            if o[r] % 4 == 0: l[r, g] = np.arange(C)[:, None]
            if o[r] % 4 == 1: l[r, g] = e[0]
            if o[r] % 4 == 2: l[r, g, e] = np.roll(e, 1)[:, None]
            if o[r] % 4 == 3:
                m = L if g % 2 else 2
                l[r, g] = e[m - 1 + rng.integers(0, 2, (C, V))]
                l[r, g, e[m - 1:m + 1]] = e[m - 2]
                for j in range(1, m - 1): l[r, g, e[j]] = e[j - 1]
    return {"x": x.reshape(N, 128, 4 * C), "u": u.reshape(N, 128, 512), "v": d["v"], **stored(l), **weights(rng, f(rng, N, 128, 2048))}
def setup_inputs_spread(rng):
    d = setup_inputs(rng)
    d["x"] = big(wide(rng, N, 128, 4 * C, cols=6))
    return d
def check_inputs(d):
    b = []
    for k in ("x", "u", "v"):
        a = np.abs(d[k].astype(np.float32))
        if not (np.isfinite(a).all() and ((a == 0) | (a >= 2.0 ** -30) & (a <= 2.0 ** 30)).all()): b.append("a value of " + k)
    if ((d["nb"] < 0) | (d["nb"] >= C)).any(): b.append("an entry of nb")
    if (d["wc"] % 128 == 127).any(): b.append("wc: a code that is no number")
    for r in range(N):
        a = np.abs(decode(pk(d["wc"][r], d["ws"][r])))
        if not ((a == 0) | (a >= 2.0 ** -30) & (a <= 2.0 ** 30)).all(): b.append("a number that wc and ws stand for")
    return b
def reference(x, u, v, nb, wc, ws):
    qu = [mx_ref.quantize(u[r]) for r in range(N)]
    lay = [pk(wc[r], ws[r]) for r in range(N)]
    now = [x[r] for r in range(N)]
    names = [gentries(nb[r]).astype(np.int64).reshape(8, C, V) for r in range(N)]
    for t in range(R):
        sent = []
        for r in range(N):
            p = mx_ref.matmul(qu[r], mx_ref.quantize(now[r]))
            l = order(p[::16] + np.float32(0.0), names[r])[:, ::-1]
            i = np.argsort(l, axis=1)
            sent.append(mx_ref.quantize(gcols(now[r], l)))
            e = np.take_along_axis(names[r], l[:, :, None], axis=1).reshape(8, -1)
            names[r] = np.take_along_axis(i, e, axis=1).reshape(8, C, V)
        came = decode(join(*sent))
        for r in range(N):
            e = np.concatenate([cut(came, (r + N - 1) % N, 4 * C)[:, 4 * (C - K):], cut(came, r, 4 * C)], axis=1)
            q = mx_ref.quantize(np.ascontiguousarray(((e[:, 4 * K:] + e[:, :4 * C]) * np.float32(0.5)).astype(BF)))
            now[r] = tile([np.maximum(mx_ref.matmul(pick(lay[r], np.arange(128 * b, 128 * b + 128)), q), np.float32(0.0)) * np.float32(0.03125) for b in range(4)])
    y, on = np.zeros((N, 128, C), np.float32), np.zeros((N, 8, V * C), np.float32)
    oc, osc = np.zeros((N, 128, 4 * C), np.uint8), np.zeros((N, 16, C), np.uint8)
    for r in range(N):
        q = mx_ref.quantize(now[r])
        y[r] = mx_ref.matmul(mx_ref.quantize(v[r]), q)
        on[r] = names[r].reshape(8, -1)
        oc[r], osc[r] = emit(q)
    return {"y": y, "on": on, "oc": oc, "osc": osc}

@@ -1,0 +1,508 @@
+from concourse.mybir import dt, AluOpType as A, AxisListType, ActivationFunctionType as F
+
+C, K, R = 256, 64, 3
+M = C - K
+NB = (8, 7)
+NV = 8
+NE, NF = 4, 1
+BEHIND = (4, 2)
+BF, FP, U16, I32, Q4, U8 = "bfloat16", "float32", "uint16", "int32", "float8_e4m3fn_x4", "uint8"
+SIZES = {
+    BF: "X 1024 ub 512 vb 512 eb 2048 TT 512 Z 1024 DX 1024 EH 768 kk 32 cc 80 mk 256 nm 256 c16 256 c4 256 i1 256 i0 256 t1 512 tp 512 "
+        "r3 768 NR 1024 NA 1024 NC 1024 eq 256 co 256 nf 256 p1 256 p2 128 rt 256 ce 2304 ceo 1152 cb 4096 cbo 2048 sg 4096 q1 256 pp 256 "
+        "nr 256 mj 16 byh 16 gb 768 mb 768 tb 256 vb2 256 lr 256 lc 256 ir 256",
+    FP: "cr 8 ln 16 r3f 768 nlf 80 ON 1024 ms 256 H 256 mx 4 nn 80 n2 64 ag 16 at 16 al 16 ab 16 e1 16 e2 16 ee 16 by 32 bys 16 un 2 "
+        "k3 256 kr 256 kl 16 gf 768 mf 768 tf 256 vf 256 ys 256",
+    U16: "nbu 64 oa 16 ou 8 nl 64 byu 32 pl 16 npl 16 l4 64 ku 256",
+    I32: "nbi 64 di 48 dj 64",
+    Q4: "qu 128 qur 128 qv 128 qw 512 qe 512 qx 256 qz 192 qh 128 qt0 128 qt1 128 qt2 128 lq 320",
+    U8: "su 128 sur 128 sv 128 sw 512 se 512 sx 256 sz 192 sh 128 st0 128 st1 128 st2 128 ls 320",
+}
+SCRATCH = {n: ("sbuf", [128, int(w)], d) for d, s in SIZES.items() for n, w in zip(s.split()[0::2], s.split()[1::2])}
+SCRATCH.update({n: ("psum", [128, w], FP) for n, w in (("pw", 2048), ("pa", 512), ("pb", 512), ("pc", 512), ("pd", 512))})
+SEMAPHORES = ["V", "S", "P", "G", "ldx", "ldu", "ldn", "ldw", "ldv", "out", "sent", "arr0", "arr1", "arr2"]
+BANKS = ("pw0", "pw1", "pw2", "pw3", "pa", "pb", "pc", "pd")
+
+
+def rank_program(g, core, T, topo):
+    rank = T.rank_of(core)
+    if rank is None:
+        return
+    n_ranks = len(T.cores)
+    nxt, prv = T.cores[(rank + 1) % n_ranks], T.cores[(rank - 1) % n_ranks]
+    rid, pid = topo.addr(nxt)[:2]
+    n_out, n_in = len(topo.engines(core, nxt)), len(topo.engines(prv, core))
+
+    queue = {"V": g.vector, "S": g.scalar, "P": g.tensor, "G": g, "Y": g.sync}
+    count = {s: 0 for s in SEMAPHORES}
+    known = {e: {} for e in queue}
+    clock, writer, readers = {}, {}, {}
+
+    def wait(e, ev):
+        if known[e].get(ev[0], 0) >= ev[1]:
+            return
+        queue[e].wait_ge(T.sem[ev[0]], ev[1])
+        for s, n in clock[ev].items():
+            known[e][s] = max(known[e].get(s, 0), n)
+
+    def note(e, ev, r, w):
+        clock[ev] = dict(known[e])
+        clock[ev][ev[0]] = ev[1]
+        for t in r:
+            readers.setdefault(t, []).append(ev)
+        for t in w:
+            writer[t], readers[t] = ev, []
+
+    def before(e, r, w):
+        need = [writer[t] for t in r + w if t in writer]
+        for t in w:
+            need += readers.get(t, [])
+        for t in r:
+            if t in BANKS:
+                need += [ev for ev in readers.get(t, []) if ev[0] != e]
+        for ev in sorted(set(need), key=lambda ev: -ev[1]):
+            wait(e, ev)
+
+    def op(e, r, w, fn):
+        r, w = r.split(), w.split()
+        before(e, r, w)
+        count[e] += 1
+        fn(queue[e]).then_inc(T.sem[e], 1)
+        note(e, (e, count[e]), r, w)
+
+    def dma(e, sem, r, w, out, in_, last=True):
+        r, w = r.split(), w.split()
+        before(e, r, w)
+        count[sem] += 16
+        queue[e].dma_start(out, in_).then_inc(T.sem[sem], 16)
+        if last:
+            note(e, (sem, count[sem]), r, w)
+
+    def ts(r, w, out, in0, s1, op0, s2=None, op1=None):
+        if op1 is None:
+            op("V", r, w, lambda q: q.tensor_scalar(out, in0, s1, None, op0))
+        else:
+            op("V", r, w, lambda q: q.tensor_scalar(out, in0, s1, s2, op0, op1))
+
+    def tt(r, w, out, a, b, o):
+        op("V", r, w, lambda q: q.tensor_tensor(out, a, b, o))
+
+    def cp(r, w, out, a):
+        op("V", r, w, lambda q: q.tensor_copy(out, a))
+
+    def scan(r, w, out, a, b, init, o0, o1):
+        op("V", r, w, lambda q: q.tensor_tensor_scan(out, a, b, init, o0, o1))
+
+    def total(r, w, out, src, at, n, init=0.0):
+        scan(r, w, out, src[:, at:at + n // 2], src[:, at + n // 2:at + n], init, A.add, A.add)
+
+    def fill(w, out, c):
+        op("V", "", w, lambda q: q.memset(out, c))
+
+    def act(r, w, out, a, f, **kw):
+        op("S", r, w, lambda q: q.activation(out, a, f, **kw))
+
+    def quant(r, w, q_, s_, a):
+        op("V", r, w, lambda q: q.quantize_mx(q_, s_, a))
+
+    def mm(r, w, out, lq, ls, l0, rq, rs, r0, n):
+        op("P", r, w, lambda q: q.matmul_mx(out, lq[:, l0:l0 + 128], ls[:, l0:l0 + 128], rq[:, r0:r0 + n], rs[:, r0:r0 + n], True, True))
+
+    def table(w, out, pat, base):
+        op("G", "", w, lambda q: q.iota(out, pat, base, 0, allow_small_or_imprecise_dtypes=True))
+
+    def bank(b, n):
+        return T.pw[:, 512 * b:512 * b + n]
+
+    def names(fmt, rows):
+        return " ".join(fmt % i for i in rows)
+
+    def pick(e, r, w, out, win):
+        if e == "V":
+            cp(r, w, out, win)
+        else:
+            act(r, w, out, win, F.Copy)
+
+    BIG = 2.0 ** 30
+    XS = "Xh Xm0 Xm1 Xm2 Xm3"
+    NRS = "NR0 NR1 NR2 NR3"
+    T1 = "t1a t1b t1c"
+    dma("Y", "ldn", "", "nbi", T.nbi[:], T.nb[:])
+    dma("S", "ldx", "", XS, T.X[:], T.x[:])
+    dma("Y", "ldu", "", "ub", T.ub[:], T.u[:])
+    dma("Y", "ldw", "ub Xh", "", T.qw[:].bitcast(dt.uint8), T.wc[:], last=False)
+    dma("Y", "ldw", "", "qw", T.sw[:], T.ws[:])
+    dma("Y", "ldv", "", "vb", T.vb[:], T.v[:])
+    op("G", "", "di0", lambda q: q.iota(T.di[:, 0:16], [[1, 16]], 128, -1))
+    op("G", "", "di2", lambda q: q.iota(T.di[:, 32:48], [[0, 16]], 0, 1))
+    table("ln", T.ln[:], [[16, 16]], 16)
+    op("G", "", "di1", lambda q: q.iota(T.di[:, 16:32], [[4, 16]], 131, -1))
+    table("i1", T.i1[:], [[1, C]], 1)
+    table("i0", T.i0[:], [[1, C]], 0)
+    table("t1a", T.t1[:, 1:C], [[256, C - 1]], 256)
+    table("eb", T.eb[:], [[0, 2048]], 0)
+    op("G", "eb", "eb", lambda q: q.affine_select(T.eb[:], T.eb[:], [[1, 4], [-1, 512]], A.not_equal, 0.5, 0, 4))
+    table("r3f", T.r3f[:], [[512, C], [0, 3]], 2 ** 24 - 1)
+    op("G", "r3f", "r3f", lambda q: q.affine_select(T.r3f[:], T.r3f[:], [[0, C], [1, 3]], A.is_equal, 1.0, 0, 0))
+    fill("r3", T.r3[:], 1.0)
+    ts("di0", "dj0", T.dj[:, 0:16], T.di[:, 0:16], 15, A.bitwise_and)
+    fill("at15", T.at[:, 15:16], 0.0)
+    ts("di2", "dj2", T.dj[:, 32:48], T.di[:, 32:48], 15, A.bitwise_and)
+    ts("dj0", "cc0", T.cc[:, 0:16], T.dj[:, 0:16], 0.0, A.is_equal)
+    cp("dj2", "oa", T.oa[:], T.dj[:, 32:48])
+    ts("di1", "dj1", T.dj[:, 16:32], T.di[:, 16:32], 2, A.arith_shift_right, 3, A.bitwise_and)
+    ts("ln", "ou", T.ou[:], T.ln[:, 0:8], -16.0, A.add)
+    ts("dj0 dj1", "cc1", T.cc[:, 16:48], T.dj[:, 0:32], 0.0, A.not_equal)
+    ts("di2", "dj3", T.dj[:, 48:49], T.di[:, 32:33], 3, A.bitwise_and)
+    act("cc0 oa", "mk", T.mk[:], T.cc[:, 0:16].indirect(T.oa[:]), F.Copy)
+    act("cc1 oa", "nm", T.nm[:], T.cc[:, 16:32].indirect(T.oa[:]), F.Copy)
+    ts("dj0 dj1", "kk", T.kk[:], T.dj[:, 0:32], 1.0, A.is_equal, BIG, A.mult)
+    ts("dj0", "cr0", T.cr[:, 0:1], T.dj[:, 15:16], 0.0, A.is_equal, 1 / BIG, A.max)
+    ts("dj1", "cr1", T.cr[:, 1:2], T.dj[:, 19:20], 0.0, A.is_equal, 1 / BIG, A.max)
+    tt("kk cc1", "cc2", T.cc[:, 48:80], T.kk[:], T.cc[:, 16:48], A.max)
+    ts("dj0", "cr7", T.cr[:, 7:8], T.dj[:, 15:16], 0.0, A.not_equal, BIG, A.mult)
+    ts("dj3", "cr3", T.cr[:, 3:4], T.dj[:, 48:49], -4.0, A.add)
+    ts("dj2", "cr4", T.cr[:, 4:5], T.dj[:, 32:33], -16.0, A.add)
+    ts("cr1", "cr2", T.cr[:, 2:3], T.cr[:, 1:2], 4.0, A.mult)
+    ts("cr7", "cr5", T.cr[:, 5:6], T.cr[:, 7:8], 1.0, A.max)
+    ts("cr7", "cr6", T.cr[:, 6:7], T.cr[:, 7:8], 1.0, A.max, -1.0, A.mult)
+    ts("ln cr4", "pos", T.nlf[:, 64:80], T.ln[:], T.cr[:, 4:5], A.add)
+    act("cc2 oa", "c16", T.c16[:], T.cc[:, 48:64].indirect(T.oa[:]), F.Copy)
+    fill("r3", T.r3[:, 0:768:3], 2.0 ** 25)
+    cp("nbi", "nbu", T.nbu[:], T.nbi[:])
+    fill("al0", T.al[:], 0.0)
+    for p in range(2):
+        pick("VS"[p], "i1 nbu", "NR%d" % p, T.NR[:, 256 * p:256 * p + 256], T.i1[:].indirect(T.nbu[:, 16 * p:16 * p + 16]))
+    quant("ub", "qu", T.qu[:], T.su[:], T.ub[:])
+    act("qu ou", "sur", T.sur[:], T.su[:].indirect(T.ou[:]), F.Copy)
+    op("V", "qu ou", "qur", lambda q: q.tensor_copy(T.qur[:].bitcast(dt.uint32), T.qu[:].bitcast(dt.uint32).indirect(T.ou[:])))
+    quant(XS, "qxh qxo qxm", T.qx[:], T.sx[:], T.X[:])
+    act("i1 nbu", "NR2 NR3", T.NR[:, 512:1024], T.i1[:].indirect(T.nbu[:, 32:64]), F.Copy)
+    fill("t1b", T.t1[:, C:2 * C], 2.0 ** 17)
+    fill("t1c", T.t1[:, 0:1], 1.0)
+    fill("TTz", T.TT[:, 256:512], 0.0)
+
+    def names_to_lists(part):
+        for e in (2 * part, 2 * part + 1):
+            scan("c16 " + NRS, "NC%d" % e, T.NC[:, C * e:C * e + C], T.c16[:], T.NR[:, e:1024:4], 0.0, A.mult, A.max)
+        if part:
+            ts("NC0 NC1 NC2 NC3 cr0", "nlf", T.nlf[:, 0:64], T.NC[:, 15:1024:16], T.cr[:, 0:1], A.mult, -1.0, A.add)
+            ts("NC0 NC1 NC2 NC3 cr0", "nl", T.nl[:], T.NC[:, 15:1024:16], T.cr[:, 0:1], A.mult, -1.0, A.add)
+
+    def own(i):
+        return T.H[:, 16 * i + 15:16 * i + 16]
+
+    def s_rows(rows, src, name, c0, hs):
+        def sign(i):
+            act(name + " " + hs, "sg%d sh%d sj%d" % (i, i, i) + (" si%d" % i if c0 == 0 else ""), T.sg[:, C * i + c0:C * i + C], src[:, 0:C - c0], F.Sign,
+                bias=own(i), scale=-1.0)
+
+        for n, i in enumerate(rows):
+            if n == 0:
+                sign(i)
+            if n + 1 < len(rows):
+                sign(rows[n + 1])
+            a, b = C * i, 16 * i + 16
+            if i < 15:
+                act("sg%d" % i, "sh%d at%d" % (i, i), T.sg[:, a + b:a + C], T.sg[:, a + b:a + C], F.Relu, scale=-1.0, accum_out=T.at[:, i:i + 1])
+            act("sg%d" % i, "sj%d ag%d" % (i, i), T.sg[:, a + c0:a + b], T.sg[:, a + c0:a + b], F.Relu, accum_out=T.ag[:, i:i + 1])
+
+    def to_list(src, name, c0, n, tag, m):
+        tt(name + " mk", "ms" + tag, T.ms[:, c0:c0 + n], src[:, 0:n], T.mk[:, 0:n], A.mult)
+        op("V", name, "mx%d" % m, lambda q: q.tensor_reduce(T.mx[:, m:m + 1], src[:, 0:n], AxisListType.X, A.max))
+        scan("nm ms" + tag, "H" + tag, T.H[:, c0:c0 + n], T.nm[:, 0:n], T.ms[:, c0:c0 + n], 0.0, A.mult, A.add)
+
+    def equal(src, name, c0, n, tag):
+        tt("H%s %s" % (tag, name), "eq" + tag, T.eq[:, c0:c0 + n], T.H[:, c0:c0 + n], src[:, 0:n], A.is_equal)
+
+    def ties(c0, n, tag):
+        scan("nm eq" + tag, "co" + tag, T.co[:, c0:c0 + n], T.nm[:, 0:n], T.eq[:, c0:c0 + n], 0.0, A.mult, A.add)
+
+    def early():
+        mm("qur sur qxo qxm", "pa", T.pa[:, 0:M], T.qur, T.sur, 0, T.qx, T.sx, K, M)
+        mm("qur sur qxo qxm", "pb", T.pb[:, 0:M], T.qur, T.sur, 0, T.qx, T.sx, K, M)
+        to_list(T.pa, "pa", K, M, "m", 0)
+        lo, h = 4 + NE, M // 2
+        s_rows(list(range(lo, 16 - NF)), T.pb, "pb", K, "Hm")
+
+        def v_sum(i):
+            total("ce%d cf%d" % (i, i), "ceo%d" % i, T.ceo[:, h * (i - 4):h * (i - 3)], T.ce, M * (i - 4), M, float(K))
+
+        def v_row(i):
+            a, b = M * (i - 4), 16 * i + 16 - K
+            ts("pa Hm", "ce%d" % i, T.ce[:, a:a + b], T.pa[:, 0:b], own(i), A.is_ge)
+            if i > 4:
+                v_sum(i - 1)
+            ts("pa Hm", "cf%d" % i, T.ce[:, a + b:a + M], T.pa[:, b:M], own(i), A.is_gt)
+
+        def last():
+            equal(T.pa, "pa", K, M, "m")
+            v_sum(lo - 1)
+            ties(K, M, "m")
+
+        return [lambda: names_to_lists(0), lambda: names_to_lists(1)] + [lambda i=i: v_row(i) for i in range(4, lo)] + [last]
+
+    def late_scores():
+        mm("qur sur qxh qxo qxm", "pc", T.pc[:, 0:C], T.qur, T.sur, 0, T.qx, T.sx, 0, C)
+        mm("qur sur qxh qxo qxm", "pd", T.pd[:, 0:C], T.qur, T.sur, 0, T.qx, T.sx, 0, C)
+
+    def late(t):
+        nv, n0, lo = (NV, C, NV) if t == 0 else (4, K, 4 + NE)
+        h = M // 2
+        com = "coh" if t == 0 else "com"
+
+        def row(i, part):
+            a, b = C * i, 16 * i + 16
+            if part == 0:
+                ts("pc Hh", "cb%d" % i, T.cb[:, a:a + b], T.pc[:, 0:b], own(i), A.is_ge)
+            elif part == 1:
+                ts("pc Hh", "cd%d" % i, T.cb[:, a + b:a + C], T.pc[:, b:C], own(i), A.is_gt)
+            else:
+                total("cb%d cd%d" % (i, i), "cbo%d" % i, T.cbo[:, 128 * i:128 * i + 128], T.cb, a, C)
+
+        def short(i, part):
+            if part == 0:
+                act("pd Hm", "si%d" % i, T.sg[:, C * i:C * i + K], T.pd[:, 0:K], F.Sign, bias=own(i), scale=-1.0)
+            else:
+                act("si%d al0" % i, "si%d al%d" % (i, i), T.sg[:, C * i:C * i + K], T.sg[:, C * i:C * i + K], F.Relu, accum_out=T.al[:, i:i + 1])
+
+        to_list(T.pc, "pc", 0, n0, "h", 1 if t else 2)
+        if t:
+            tt("mx0 mx1", "mx2", T.mx[:, 2:3], T.mx[:, 0:1], T.mx[:, 1:2], A.max)
+            short(4, 0)
+        act("pd mx2", "nf", T.nf[:], T.pd[:, 0:C], F.Sign, bias=T.mx[:, 2:3], scale=-1.0)
+        if t:
+            for i in range(5, 17 - NF):
+                if i < 16 - NF:
+                    short(i, 0)
+                short(i - 1, 1)
+            s_rows(list(range(16 - NF, 16)), T.pd, "pd", 0, "Hm")
+        else:
+            s_rows(list(range(nv, 16)), T.pd, "pd", 0, "Hh")
+        srows = range(lo, 16)
+        small = [
+            lambda: equal(T.pc, "pc", 0, n0, "h"),
+            lambda: ties(0, n0, "h"),
+            lambda: scan("nf", "p1", T.p1[:], T.nf[:], T.nf[:], 1.0, A.mult, A.mult),
+            lambda: total("p1", "p2", T.p2[:], T.p1, 0, C),
+            lambda: ts("nlf pos p2", "nn", T.nn[:], T.nlf[:], T.p2[:, 127:128], A.not_equal, 256.0, A.mult),
+            lambda: tt("nn", "n2a", T.n2[:, 0:32], T.nn[:, 0:32], T.nn[:, 32:64], A.min),
+            lambda: tt("n2a", "n2b", T.n2[:, 32:48], T.n2[:, 0:16], T.n2[:, 16:32], A.min),
+            lambda: tt("n2b nn", "n2c", T.n2[:, 48:64], T.n2[:, 32:48], T.nn[:, 64:80], A.min),
+        ]
+        if t == 0:
+            small = [lambda: None] * (2 * nv - 10) + [lambda: names_to_lists(0), lambda: names_to_lists(1)] + small
+        for i in range(nv):
+            for part in range(2):
+                row(i, part)
+                small.pop(0)()
+        tt("ln " + com, "e2", T.e2[:, lo:16], T.ln[:, lo:16], T.co[:, 16 * lo + 15:C:16], A.subtract)
+        if t:
+            tt(names("ceo%d", range(4, lo)) + " com", "eev", T.ee[:, 4:lo], T.ceo[:, h - 1:h * (lo - 4):h], T.co[:, K + 15:16 * lo:16], A.subtract)
+        for i in range(nv):
+            row(i, 2)
+        ts("i0 p2", "rt", T.rt[:], T.i0[:], T.p2[:, 127:128], A.not_equal, 2.0 ** 25, A.mult)
+        tt(names("cbo%d", range(nv)) + " coh", "byb", T.by[:, 0:nv], T.cbo[:, 127:128 * nv:128], T.co[:, 15:16 * nv:16], A.subtract)
+        if t:
+            tt("e2 " + names("al%d", range(lo, 16 - NF)), "e3", T.e2[:, lo:16], T.e2[:, lo:16], T.al[:, lo:16], A.subtract)
+            tt("eev " + names("al%d", range(4, lo)), "byd", T.by[:, 4:lo], T.ee[:, 4:lo], T.al[:, 4:lo], A.subtract)
+        tt("e2 e3 " + names("at%d", srows), "e1", T.e1[:, lo:16], T.e2[:, lo:16], T.at[:, lo:16], A.add)
+        tt("e1 " + names("ag%d", srows), "bya", T.by[:, lo:16], T.e1[:, lo:16], T.ag[:, lo:16], A.subtract)
+        tt("bya byb byd n2c", "byc", T.by[:, 16:32], T.by[:, 0:16], T.n2[:, 48:64], A.add)
+        ts("bya byb byd cr5", "bys", T.bys[:], T.by[:, 0:16], T.cr[:, 5:6], A.mult)
+        cp("bya byb byc byd", "byu", T.byu[:], T.by[:])
+        cp("bya byb byd", "byh", T.byh[:], T.by[:, 0:16])
+        for p in (1, 0):
+            pick("VS"[p], T1 + " byu", "q1%d" % p, T.q1[:, 128 * p:128 * p + 128], T.t1[:].indirect(T.byu[:, 16 + 8 * p:24 + 8 * p]))
+
+    def least(tab, name, gg, mo, tmp, rst, rname):
+        act(name + " nl", "g1", gg[:, 1:768:3], tab[:].indirect(T.nl[:, 32:48]), F.Copy)
+        act(name + " nl", "g2", gg[:, 2:768:3], tab[:].indirect(T.nl[:, 48:64]), F.Copy)
+        tt(name + " nl rt", "tmp", tmp[:], tab[:].indirect(T.nl[:, 0:16]), T.rt[:], A.min)
+        tt(name + " nl tmp", "g0", gg[:, 0:768:3], tab[:].indirect(T.nl[:, 16:32]), tmp[:], A.min)
+        scan("g0 g1 g2 " + rname, "mo", mo[:], rst[:], gg[:], 0.0, A.max, A.min)
+
+    def keys(mo, conv):
+        scan("mo c16", "conv", conv[:], T.c16[:], mo[:, 2:768:3], 0.0, A.mult, A.max)
+        tt("i0 byu mo", "kr", T.kr[:], T.i0[:].indirect(T.byu[:, 0:16]), mo[:, 2:768:3], A.add)
+        tt("conv bys", "kl", T.kl[:], conv[:, 15:C:16], T.bys[:], A.add)
+
+    def ranking(nb, narrow, out, name, c0, c1, c2, between=None):
+        ns = 16 - nb
+        for i in range(ns):
+            act("kr kl cr6", "sg%d sh%d si%d sj%d ab%d" % (i, i, i, i, i), T.sg[:, C * i:C * i + C], T.kr[:], F.Sign, bias=T.kl[:, i:i + 1],
+                scale=T.cr[:, 6:7], accum_out=T.ab[:, i:i + 1])
+        if narrow:
+            ts("conv cr0", "mj", T.mj[:], T.vb2[:, 15:C:16], T.cr[:, 0:1], A.mult)
+            cp("kr", "ku", T.ku[:], T.kr[:])
+        for i in range(ns, 17):
+            if i < 16 and narrow:
+                ts("ku mj byh", "cb%d cd%d" % (i, i), T.cb[:, C * i:C * i + C], T.ku[:], T.mj[:, i:i + 1], A.subtract, T.byh[:, i:i + 1], A.is_lt)
+            elif i < 16:
+                ts("kr kl cr5", "cb%d cd%d" % (i, i), T.cb[:, C * i:C * i + C], T.kr[:], T.cr[:, 5:6], A.mult, T.kl[:, i:i + 1], A.is_gt)
+            if i > ns:
+                total("cb%d" % (i - 1), "cbo%d" % (i - 1), T.cbo[:, 128 * i - 128:128 * i], T.cb, C * (i - 1), C)
+        ts(names("cbo%d", range(ns, 16)) + " un0", name + "a", out[:, ns:16], T.cbo[:, 128 * ns + 127:2048:128], c0, A.add)
+        if between:
+            between()
+        ts(names("ab%d", range(ns)) + " un1", name + "b", out[:, 0:ns], T.ab[:, 0:ns], c1, A.mult, c2, A.add)
+
+    def unpack():
+        for b in range(4):
+            mm("qe qxh qxo qxm", "pw%d" % b, bank(b, C), T.qe, T.se, 128 * b, T.qx, T.sx, 0, C)
+
+    def halves(b):
+        act("pw%d" % b, "DX%d" % b, T.DX[:, b:1024:4], bank(b, C), F.Copy)
+
+    CUT = 16 - NB[1] + NB[1] % 2
+
+    def order(t):
+        if t > 0:
+            unpack()
+        least(T.q1, "q10 q11", T.gb, T.mb, T.tb, T.r3, "r3")
+        if t > 0:
+            halves(0)
+        else:
+            act(T1, "tp", T.tp[:], T.t1[:], F.Copy, scale=256.0)
+        act("mo", "nr un0", T.nr[:], T.mb[:, 2:768:3], F.Relu, bias=-1.0, scale=2.0 ** -16, accum_out=T.un[:, 0:1])
+        act("un0", "un1", T.un[:, 1:2], T.un[:, 0:1], F.Identity, bias=127.5)
+        keys(T.mb, T.vb2)
+        ranking(NB[0], True, T.pl, "pl", T.un[:, 0:1], 0.5, T.un[:, 1:2])
+        for p in (0, 1):
+            pick("SV"[p], "tp pla plb", "pp%d" % p, T.pp[:, 128 * p:128 * p + 128], T.tp[:].indirect(T.pl[:, 8 * p:8 * p + 8]))
+        least(T.pp, "pp0 pp1", T.gb, T.mb, T.tb, T.r3, "r3")
+        if t == 0:
+            act("cc2 oa", "c4", T.c4[:], T.cc[:, 64:80].indirect(T.oa[:]), F.Copy)
+        else:
+            halves(1)
+        tt(T1 + " byu mo", "k3", T.k3[:], T.t1[:].indirect(T.byu[:, 0:16]), T.mb[:, 2:768:3], A.add)
+        if t == 0:
+            quant("eb", "qe", T.qe[:], T.se[:], T.eb[:])
+            unpack()
+        least(T.k3, "k3", T.gf, T.mf, T.tf, T.r3f, "r3f")
+        for b in (range(4) if t == 0 else (2, 3)):
+            halves(b)
+        keys(T.mf, T.vf)
+        ranking(NB[1], False, T.npl, "npl", 0.0, -0.5, 127.5,
+                lambda: cp("i1 npla", "lr", T.lr[:].indirect(T.npl[:, CUT:16]), T.i1[:, 16 * CUT:C]))
+
+    def relu(b, n, c0, w):
+        out, a = T.X[:, 4 * c0 + b:4 * (c0 + n):4], bank(b, n)
+        if b % 2:
+            ts("pw%d" % b, w, out, a, 0.0, A.max, 0.03125, A.mult)
+        else:
+            act("pw%d" % b, w, out, a, F.Relu, scale=0.03125)
+
+    def main_codes():
+        quant("Xm0 Xm1 Xm2 Xm3", "qxo qxm", T.qx[:, K:C], T.sx[:, K:C], T.X[:, 4 * K:1024])
+
+    def move(t):
+        qt, st = T["qt%d" % t], T["st%d" % t]
+        dxs = "DX0 DX1 DX2 DX3 l4"
+
+        def name(e):
+            act("ir nl", "NA%d" % e, T.NA[:, e:1024:4], T.ir[:].indirect(T.nl[:, 16 * e:16 * e + 16]), F.Copy)
+
+        def renamed(e, p):
+            if t < R - 1:
+                pick(e, "NA0 NA1 NA2 NA3 l4", "NR%d" % p, T.NR[:, 256 * p:256 * p + 256], T.NA[:].indirect(T.l4[:, 16 * p:16 * p + 16]))
+
+        act("i1 npla nplb", "ir", T.ir[:], T.i1[:].indirect(T.npl[:]), F.Copy)
+        name(0)
+        cp("i1 npla nplb", "lr", T.lr[:].indirect(T.npl[:, 0:CUT]), T.i1[:, 0:16 * CUT])
+        scan("c4 lr", "lc", T.lc[:], T.c4[:], T.lr[:], 0.0, A.mult, A.max)
+        ts("lc cr2 cr3", "l4", T.l4[:], T.lc[:, 3:C:4], T.cr[:, 2:3], A.mult, T.cr[:, 3:4], A.add)
+        if t < R - 1:
+            cp(XS + " l4", "TT0 TT1", T.TT[:, 0:256], T.X[:].indirect(T.l4[:, 48:64]))
+        else:
+            for p in (1, 0):
+                pick("VS"[p], XS + " l4", "TT%d" % p, T.TT[:, 128 * p:128 * p + 128], T.X[:].indirect(T.l4[:, 48 + 8 * p:56 + 8 * p]))
+        quant("TT0 TT1 TTz", "qt", qt[:], st[:], T.TT[:])
+        before("G", ["qt"], [])
+        at = 128 + K * t
+        arr = T.sem["arr%d" % t]
+        g.remote_dma(T.lq[:, at:at + K].bitcast(dt.uint8), qt[:, 0:K].bitcast(dt.uint8), arr, T.sem["sent"], pid, rid, topo.mask(core, nxt))
+        g.remote_dma(T.ls[:, at:at + K], st[:, 0:K], arr, T.sem["sent"], pid, rid, topo.mask(core, nxt))
+        count["sent"] += 2 * n_out
+        count["arr%d" % t] = 2 * n_in
+        ev = ("arr%d" % t, 2 * n_in)
+        clock[ev], writer["land%d" % t] = {ev[0]: ev[1]}, ev
+        for p in range(3):
+            act(dxs, "EH%d" % p, T.EH[:, 256 * p:256 * p + 256], T.DX[:].indirect(T.l4[:, 16 * p:16 * p + 16]), F.Copy)
+            tt(dxs + " EH%d" % p, "Z%d" % (p + 1), T.Z[:, 256 * p + 256:256 * p + 512], T.DX[:].indirect(T.l4[:, 16 * p + 16:16 * p + 32]),
+               T.EH[:, 256 * p:256 * p + 256], A.add)
+        quant("Z1 Z2 Z3", "qz", T.qz[:], T.sz[:], T.Z[:, 256:1024])
+        for b in range(4):
+            mm("qw qz", "pw%d" % b, bank(b, M), T.qw, T.sw, 128 * b, T.qz, T.sz, 0, M)
+        for e in (1, 2, 3):
+            name(e)
+        if t == 0:
+            quant(XS, "lq", T.lq[:, 0:128], T.ls[:, 0:128], T.X[:, 0:512])
+        if t == R - 1:
+            quant("vb", "qv", T.qv[:], T.sv[:], T.vb[:])
+        relu(0, M, K, "Xm0")
+        relu(1, M, K, "Xm1")
+        renamed("V", 0)
+        relu(2, M, K, "Xm2")
+        relu(3, M, K, "Xm3")
+        renamed("S", 2)
+        renamed("S", 3)
+        if t < R - 1:
+            main_codes()
+        renamed("V", 1)
+
+    def mix(t):
+        if t == R - 1:
+            to = [(n, T[n][:, 0:128], T[n][:, K:128]) for n in BANKS[4:]]
+        else:
+            to = [(BANKS[b], bank(b, 128), T.pw[:, 512 * b + K:512 * b + 128]) for b in range(4)]
+        for b in range(4):
+            mm("qe lq land%d" % t, to[b][0], to[b][1], T.qe, T.se, 128 * b, T.lq, T.ls, K + K * t, 128)
+        for b in range(4):
+            tt(to[b][0] + " EH0", "Z0%d" % b, T.Z[:, b:256:4], to[b][2], T.EH[:, b:256:4], A.add)
+        quant("Z00 Z01 Z02 Z03 Z1", "qh", T.qh[:], T.sh[:], T.Z[:, 0:512])
+        for b in range(4):
+            mm("qw qh", "pw%d" % b, bank(b, 128), T.qw, T.sw, 128 * b, T.qh, T.sh, 0, 128)
+
+    def layer():
+        for b in range(4):
+            ts("pw%d" % b, "Xh%d" % b + (" Xh" if b == 0 else ""), T.X[:, b:4 * K:4], bank(b, K), 0.0, A.max, 0.03125, A.mult)
+        quant("Xh0 Xh1 Xh2 Xh3 Xm0 Xm1 Xm2 Xm3", "qxh qxo Xh", T.qx[:, 0:128], T.sx[:, 0:128], T.X[:, 0:512])
+
+    def run(todo, left):
+        while len(todo) > left:
+            todo.pop(0)()
+
+    for t in range(R):
+        if t == 0:
+            late_scores()
+        else:
+            todo = early()
+            run(todo, BEHIND[0])
+            mix(t - 1)
+            run(todo, BEHIND[1])
+            layer()
+            late_scores()
+            run(todo, 0)
+        late(t)
+        order(t)
+        move(t)
+
+    act("NA0 NA1 NA2 NA3 l4", "ON", T.ON[:], T.NA[:].indirect(T.l4[:]), F.Identity, bias=-1.0)
+    dma("S", "out", "ON", "", T.on[:], T.ON[0:128:16, :], last=False)
+    mix(R - 1)
+    main_codes()
+    mm("qv qxm", "pa", T.pa[:, 0:128], T.qv, T.sv, 0, T.qx, T.sx, 128, 128)
+    dma("Y", "out", "qxm", "", T.oc[:, 512:1024], T.qx[:, 128:C].bitcast(dt.uint8), last=False)
+    act("pa", "ym", T.ys[:, 128:C], T.pa[:, 0:128], F.Copy)
+    dma("S", "out", "ym", "", T.y[:, 128:C], T.ys[:, 128:C], last=False)
+    layer()
+    mm("qv qxh qxo", "pc", T.pc[:, 0:128], T.qv, T.sv, 0, T.qx, T.sx, 0, 128)
+    dma("Y", "out", "qxh qxo", "", T.oc[:, 0:512], T.qx[:, 0:128].bitcast(dt.uint8), last=False)
+    for k in range(4):
+        dma("S" if k else "Y", "out", "qxh qxo qxm", "", T.osc[4 * k:4 * k + 4, :], T.sx[32 * k:32 * k + 4, :], last=False)
+    cp("pc", "yh", T.ys[:, 0:128], T.pc[:, 0:128])
+    dma("Y", "out", "yh", "", T.y[:, 0:128], T.ys[:, 0:128], last=False)
+    for s in SEMAPHORES:
+        if count[s]:
+            g.wait_ge(T.sem[s], count[s])

@@ -2,10 +2,11 @@ from concourse.mybir import dt, AluOpType as A, AxisListType, ActivationFunction
 
 C, K, R = 256, 64, 3
 M = C - K
-NB = (8, 7)
-NV = 8
-NE, NF = 4, 1
-BEHIND = (4, 2)
+NB = (9, 6)
+NV = 9
+NE = 4
+WAKE, TRAVEL = 200.0, 3500.0
+SOONER = {"msh": 300.0, "pla": -200.0, "eqh": 300.0, "cbo0": 200.0}
 BF, FP, U16, I32, Q4, U8 = "bfloat16", "float32", "uint16", "int32", "float8_e4m3fn_x4", "uint8"
 SIZES = {
     BF: "X 1024 ub 512 vb 512 eb 2048 TT 512 Z 1024 DX 1024 EH 768 kk 32 cc 80 mk 256 nm 256 c16 256 c4 256 i1 256 i0 256 t1 512 tp 512 "
@@ -20,7 +21,7 @@ SIZES = {
 }
 SCRATCH = {n: ("sbuf", [128, int(w)], d) for d, s in SIZES.items() for n, w in zip(s.split()[0::2], s.split()[1::2])}
 SCRATCH.update({n: ("psum", [128, w], FP) for n, w in (("pw", 2048), ("pa", 512), ("pb", 512), ("pc", 512), ("pd", 512))})
-SEMAPHORES = ["V", "S", "P", "G", "ldx", "ldu", "ldn", "ldw", "ldv", "out", "sent", "arr0", "arr1", "arr2"]
+SEMAPHORES = ["V", "S", "P", "G", "ldx", "ldu", "ldn", "ldw", "lds", "ldv", "out", "sent", "arr0", "arr1", "arr2"]
 BANKS = ("pw0", "pw1", "pw2", "pw3", "pa", "pb", "pc", "pd")
 
 
@@ -36,47 +37,72 @@ def rank_program(g, core, T, topo):
     queue = {"V": g.vector, "S": g.scalar, "P": g.tensor, "G": g, "Y": g.sync}
     count = {s: 0 for s in SEMAPHORES}
     known = {e: {} for e in queue}
-    clock, writer, readers = {}, {}, {}
+    calls, first, writer, readers = [], [], {}, {}
 
-    def wait(e, ev):
-        if known[e].get(ev[0], 0) >= ev[1]:
-            return
-        queue[e].wait_ge(T.sem[ev[0]], ev[1])
-        for s, n in clock[ev].items():
-            known[e][s] = max(known[e].get(s, 0), n)
-
-    def note(e, ev, r, w):
-        clock[ev] = dict(known[e])
-        clock[ev][ev[0]] = ev[1]
-        for t in r:
-            readers.setdefault(t, []).append(ev)
+    def record(e, r, w, fn, cost, late, sem, n):
+        r, w = r.split(), w.split()
+        first.append(sum(float(t) for t in r if t[0] == "+") + SOONER.get(w[0] if w else "", 0.0))
+        need = {writer[t] for t in r + w if t in writer}
         for t in w:
-            writer[t], readers[t] = ev, []
-
-    def before(e, r, w):
-        need = [writer[t] for t in r + w if t in writer]
-        for t in w:
-            need += readers.get(t, [])
+            need.update(readers.get(t, []))
         for t in r:
             if t in BANKS:
-                need += [ev for ev in readers.get(t, []) if ev[0] != e]
-        for ev in sorted(set(need), key=lambda ev: -ev[1]):
-            wait(e, ev)
+                need.update(i for i in readers.get(t, []) if calls[i][0] != e)
+        for t in r:
+            readers.setdefault(t, []).append(len(calls))
+        for t in w:
+            writer[t], readers[t] = len(calls), []
+        calls.append((e, need, fn, cost, late, sem, n))
 
     def op(e, r, w, fn):
-        r, w = r.split(), w.split()
-        before(e, r, w)
-        count[e] += 1
-        fn(queue[e]).then_inc(T.sem[e], 1)
-        note(e, (e, count[e]), r, w)
+        cost = 55.0
+        if r[:1] == "@":
+            c, r = (r + " ").split(" ", 1)
+            cost = 55 + {"g": 1.3, "s": 3.2}[c[1]] * int(c[2:]) if c[1] in "gs" else max(55.0, 0.87 * int(c[1:]))
+        record(e, r, w, lambda: fn(queue[e]).then_inc(T.sem[e], 1), cost, 0.0, e, 1)
 
-    def dma(e, sem, r, w, out, in_, last=True):
-        r, w = r.split(), w.split()
-        before(e, r, w)
-        count[sem] += 16
-        queue[e].dma_start(out, in_).then_inc(T.sem[sem], 16)
-        if last:
-            note(e, (sem, count[sem]), r, w)
+    def dma(e, sem, r, w, out, in_):
+        record(e, r, w, lambda: queue[e].dma_start(out, in_).then_inc(T.sem[sem], 16), 60.0, 2200.0, sem, 16)
+
+    def issue():
+        n = len(calls)
+        after = [[] for _ in calls]
+        for i, c in enumerate(calls):
+            for j in c[1]:
+                after[j].append(i)
+        rest = [0.0] * n
+        for i in range(n - 1, -1, -1):
+            rest[i] = first[i] + calls[i][3] + calls[i][4] + max([WAKE + rest[j] for j in after[i]] + [0.0])
+        left, ready, free = [len(c[1]) for c in calls], [0.0] * n, {e: 0.0 for e in queue}
+        can = [i for i in range(n) if not left[i]]
+        event, clock = {}, {}
+        while can:
+            i = min(can, key=lambda k: (max(ready[k], free[calls[k][0]]), -rest[k], k))
+            e = calls[i][0]
+            until = max(ready[i], free[e]) + calls[i][3]
+            for k in can:
+                if calls[k][0] == e and rest[k] > rest[i]:
+                    ti, tk = max(ready[i], free[e]), max(ready[k], free[e])
+                    if tk < until and max(tk + rest[k], tk + calls[k][3] + rest[i]) < max(ti + rest[i], ti + calls[i][3] + rest[k]):
+                        i = k
+            can.remove(i)
+            _, need, fn, cost, late, sem, inc = calls[i]
+            for ev in sorted({event[j] for j in need}, key=lambda ev: (-ev[1], ev[0])):
+                if known[e].get(ev[0], 0) < ev[1]:
+                    queue[e].wait_ge(T.sem[ev[0]], ev[1])
+                    for s, v in clock[ev].items():
+                        known[e][s] = max(known[e].get(s, 0), v)
+            fn()
+            count[sem] += inc
+            event[i] = (sem, count[sem])
+            clock[event[i]] = dict(known[e]) if sem[:3] != "arr" else {}
+            clock[event[i]][sem] = count[sem]
+            free[e] = max(ready[i], free[e]) + cost
+            for j in after[i]:
+                ready[j] = max(ready[j], free[e] + late + WAKE)
+                left[j] -= 1
+                if not left[j]:
+                    can.append(j)
 
     def ts(r, w, out, in0, s1, op0, s2=None, op1=None):
         if op1 is None:
@@ -96,20 +122,21 @@ def rank_program(g, core, T, topo):
     def total(r, w, out, src, at, n, init=0.0):
         scan(r, w, out, src[:, at:at + n // 2], src[:, at + n // 2:at + n], init, A.add, A.add)
 
-    def fill(w, out, c):
-        op("V", "", w, lambda q: q.memset(out, c))
+    def fill(r, w, out, c):
+        op("V", r, w, lambda q: q.memset(out, c))
 
     def act(r, w, out, a, f, **kw):
         op("S", r, w, lambda q: q.activation(out, a, f, **kw))
 
-    def quant(r, w, q_, s_, a):
-        op("V", r, w, lambda q: q.quantize_mx(q_, s_, a))
+    def quant(n, r, w, q_, s_, a):
+        op("V", "@%d " % (n + 20) + r, w, lambda q: q.quantize_mx(q_, s_, a))
 
     def mm(r, w, out, lq, ls, l0, rq, rs, r0, n):
-        op("P", r, w, lambda q: q.matmul_mx(out, lq[:, l0:l0 + 128], ls[:, l0:l0 + 128], rq[:, r0:r0 + n], rs[:, r0:r0 + n], True, True))
+        op("P", "@%d " % (3 * n // 2) + r, w,
+           lambda q: q.matmul_mx(out, lq[:, l0:l0 + 128], ls[:, l0:l0 + 128], rq[:, r0:r0 + n], rs[:, r0:r0 + n], True, True))
 
-    def table(w, out, pat, base):
-        op("G", "", w, lambda q: q.iota(out, pat, base, 0, allow_small_or_imprecise_dtypes=True))
+    def table(n, w, out, pat, base):
+        op("G", "@%d" % (150 + 2 * n), w + " gq", lambda q: q.iota(out, pat, base, 0, allow_small_or_imprecise_dtypes=True))
 
     def bank(b, n):
         return T.pw[:, 512 * b:512 * b + n]
@@ -125,28 +152,31 @@ def rank_program(g, core, T, topo):
 
     BIG = 2.0 ** 30
     XS = "Xh Xm0 Xm1 Xm2 Xm3"
-    NRS = "NR0 NR1 NR2 NR3"
     T1 = "t1a t1b t1c"
-    dma("Y", "ldn", "", "nbi", T.nbi[:], T.nb[:])
     dma("S", "ldx", "", XS, T.X[:], T.x[:])
     dma("Y", "ldu", "", "ub", T.ub[:], T.u[:])
-    dma("Y", "ldw", "ub Xh", "", T.qw[:].bitcast(dt.uint8), T.wc[:], last=False)
-    dma("Y", "ldw", "", "qw", T.sw[:], T.ws[:])
-    dma("Y", "ldv", "", "vb", T.vb[:], T.v[:])
-    op("G", "", "di0", lambda q: q.iota(T.di[:, 0:16], [[1, 16]], 128, -1))
-    op("G", "", "di2", lambda q: q.iota(T.di[:, 32:48], [[0, 16]], 0, 1))
-    table("ln", T.ln[:], [[16, 16]], 16)
-    op("G", "", "di1", lambda q: q.iota(T.di[:, 16:32], [[4, 16]], 131, -1))
-    table("i1", T.i1[:], [[1, C]], 1)
-    table("i0", T.i0[:], [[1, C]], 0)
-    table("t1a", T.t1[:, 1:C], [[256, C - 1]], 256)
-    table("eb", T.eb[:], [[0, 2048]], 0)
-    op("G", "eb", "eb", lambda q: q.affine_select(T.eb[:], T.eb[:], [[1, 4], [-1, 512]], A.not_equal, 0.5, 0, 4))
-    table("r3f", T.r3f[:], [[512, C], [0, 3]], 2 ** 24 - 1)
-    op("G", "r3f", "r3f", lambda q: q.affine_select(T.r3f[:], T.r3f[:], [[0, C], [1, 3]], A.is_equal, 1.0, 0, 0))
-    fill("r3", T.r3[:], 1.0)
+    dma("Y", "ldn", "", "nbi", T.nbi[:], T.nb[:])
+    dma("Y", "ldw", "ub Xh", "qw", T.qw[:].bitcast(dt.uint8), T.wc[:])
+    dma("Y", "lds", "ub Xh", "sw", T.sw[:], T.ws[:])
+    dma("Y", "ldv", "qw", "vb", T.vb[:], T.v[:])
+    op("G", "@180", "di0", lambda q: q.iota(T.di[:, 0:16], [[1, 16]], 128, -1))
+    op("G", "@180", "di2", lambda q: q.iota(T.di[:, 32:48], [[0, 16]], 0, 1))
+    op("G", "@180", "ln", lambda q: q.iota(T.ln[:], [[16, 16]], 16, 0, allow_small_or_imprecise_dtypes=True))
+    op("G", "@180", "di1 gq", lambda q: q.iota(T.di[:, 16:32], [[4, 16]], 131, -1))
+    table(C, "i1", T.i1[:], [[1, C]], 1)
+    table(C, "i0", T.i0[:], [[1, C]], 0)
+    table(C, "t1a", T.t1[:, 1:C], [[256, C - 1]], 256)
+    op("G", "@4250 di0 di2 ln", "eb gq", lambda q: q.iota(T.eb[:], [[0, 2048]], 0, 0, allow_small_or_imprecise_dtypes=True))
+    op("G", "@4300 eb", "eb gq", lambda q: q.affine_select(T.eb[:], T.eb[:], [[1, 4], [-1, 512]], A.not_equal, 0.5, 0, 4))
+    table(768, "r3f", T.r3f[:], [[512, C], [0, 3]], 2 ** 24 - 1)
+    op("G", "@1750 r3f", "r3f", lambda q: q.affine_select(T.r3f[:], T.r3f[:], [[0, C], [1, 3]], A.is_equal, 1.0, 0, 0))
+    fill("@384", "r3", T.r3[:], 1.0)
+    fill("@128", "r3", T.r3[:, 0:768:3], 2.0 ** 25)
+    fill("", "at15", T.at[:, 15:16], 0.0)
+    fill("@128", "t1b", T.t1[:, C:2 * C], 2.0 ** 17)
+    fill("", "t1c", T.t1[:, 0:1], 1.0)
+    fill("@128", "TTz", T.TT[:, 256:512], 0.0)
     ts("di0", "dj0", T.dj[:, 0:16], T.di[:, 0:16], 15, A.bitwise_and)
-    fill("at15", T.at[:, 15:16], 0.0)
     ts("di2", "dj2", T.dj[:, 32:48], T.di[:, 32:48], 15, A.bitwise_and)
     ts("dj0", "cc0", T.cc[:, 0:16], T.dj[:, 0:16], 0.0, A.is_equal)
     cp("dj2", "oa", T.oa[:], T.dj[:, 32:48])
@@ -154,8 +184,8 @@ def rank_program(g, core, T, topo):
     ts("ln", "ou", T.ou[:], T.ln[:, 0:8], -16.0, A.add)
     ts("dj0 dj1", "cc1", T.cc[:, 16:48], T.dj[:, 0:32], 0.0, A.not_equal)
     ts("di2", "dj3", T.dj[:, 48:49], T.di[:, 32:33], 3, A.bitwise_and)
-    act("cc0 oa", "mk", T.mk[:], T.cc[:, 0:16].indirect(T.oa[:]), F.Copy)
-    act("cc1 oa", "nm", T.nm[:], T.cc[:, 16:32].indirect(T.oa[:]), F.Copy)
+    act("@g256 cc0 oa", "mk", T.mk[:], T.cc[:, 0:16].indirect(T.oa[:]), F.Copy)
+    act("@g256 cc1 oa", "nm", T.nm[:], T.cc[:, 16:32].indirect(T.oa[:]), F.Copy)
     ts("dj0 dj1", "kk", T.kk[:], T.dj[:, 0:32], 1.0, A.is_equal, BIG, A.mult)
     ts("dj0", "cr0", T.cr[:, 0:1], T.dj[:, 15:16], 0.0, A.is_equal, 1 / BIG, A.max)
     ts("dj1", "cr1", T.cr[:, 1:2], T.dj[:, 19:20], 0.0, A.is_equal, 1 / BIG, A.max)
@@ -167,289 +197,198 @@ def rank_program(g, core, T, topo):
     ts("cr7", "cr5", T.cr[:, 5:6], T.cr[:, 7:8], 1.0, A.max)
     ts("cr7", "cr6", T.cr[:, 6:7], T.cr[:, 7:8], 1.0, A.max, -1.0, A.mult)
     ts("ln cr4", "pos", T.nlf[:, 64:80], T.ln[:], T.cr[:, 4:5], A.add)
-    act("cc2 oa", "c16", T.c16[:], T.cc[:, 48:64].indirect(T.oa[:]), F.Copy)
-    fill("r3", T.r3[:, 0:768:3], 2.0 ** 25)
+    act("@g256 cc2 oa", "c16", T.c16[:], T.cc[:, 48:64].indirect(T.oa[:]), F.Copy)
+    act("@g256 cc2 oa", "c4", T.c4[:], T.cc[:, 64:80].indirect(T.oa[:]), F.Copy)
+    act("@512 " + T1, "tp", T.tp[:], T.t1[:], F.Copy, scale=256.0)
+    quant(512, "eb +5000", "qe", T.qe[:], T.se[:], T.eb[:])
+    quant(128, "vb", "qv", T.qv[:], T.sv[:], T.vb[:])
     cp("nbi", "nbu", T.nbu[:], T.nbi[:])
-    fill("al0", T.al[:], 0.0)
-    for p in range(2):
-        pick("VS"[p], "i1 nbu", "NR%d" % p, T.NR[:, 256 * p:256 * p + 256], T.i1[:].indirect(T.nbu[:, 16 * p:16 * p + 16]))
-    quant("ub", "qu", T.qu[:], T.su[:], T.ub[:])
-    act("qu ou", "sur", T.sur[:], T.su[:].indirect(T.ou[:]), F.Copy)
-    op("V", "qu ou", "qur", lambda q: q.tensor_copy(T.qur[:].bitcast(dt.uint32), T.qu[:].bitcast(dt.uint32).indirect(T.ou[:])))
-    quant(XS, "qxh qxo qxm", T.qx[:], T.sx[:], T.X[:])
-    act("i1 nbu", "NR2 NR3", T.NR[:, 512:1024], T.i1[:].indirect(T.nbu[:, 32:64]), F.Copy)
-    fill("t1b", T.t1[:, C:2 * C], 2.0 ** 17)
-    fill("t1c", T.t1[:, 0:1], 1.0)
-    fill("TTz", T.TT[:, 256:512], 0.0)
+    for p in range(4):
+        pick("VSSS"[p], "@g256 i1 nbu", "NR%d" % p, T.NR[:, 256 * p:256 * p + 256], T.i1[:].indirect(T.nbu[:, 16 * p:16 * p + 16]))
+    quant(128, "ub", "qu", T.qu[:], T.su[:], T.ub[:])
+    act("@g128 qu ou", "sur", T.sur[:], T.su[:].indirect(T.ou[:]), F.Copy)
+    op("V", "@g128 qu ou", "qur", lambda q: q.tensor_copy(T.qur[:].bitcast(dt.uint32), T.qu[:].bitcast(dt.uint32).indirect(T.ou[:])))
+    quant(C, XS, "qxh qxo qxm", T.qx[:], T.sx[:], T.X[:])
+    quant(128, XS, "lq", T.lq[:, 0:128], T.ls[:, 0:128], T.X[:, 0:512])
 
-    def names_to_lists(part):
-        for e in (2 * part, 2 * part + 1):
-            scan("c16 " + NRS, "NC%d" % e, T.NC[:, C * e:C * e + C], T.c16[:], T.NR[:, e:1024:4], 0.0, A.mult, A.max)
-        if part:
-            ts("NC0 NC1 NC2 NC3 cr0", "nlf", T.nlf[:, 0:64], T.NC[:, 15:1024:16], T.cr[:, 0:1], A.mult, -1.0, A.add)
-            ts("NC0 NC1 NC2 NC3 cr0", "nl", T.nl[:], T.NC[:, 15:1024:16], T.cr[:, 0:1], A.mult, -1.0, A.add)
+    def names_to_lists():
+        for e in range(4):
+            scan("@128 c16 NR0 NR1 NR2 NR3", "NC%d" % e, T.NC[:, C * e:C * e + C], T.c16[:], T.NR[:, e:1024:4], 0.0, A.mult, A.max)
+        ts("NC0 NC1 NC2 NC3 cr0", "nlf", T.nlf[:, 0:64], T.NC[:, 15:1024:16], T.cr[:, 0:1], A.mult, -1.0, A.add)
+        ts("NC0 NC1 NC2 NC3 cr0", "nl", T.nl[:], T.NC[:, 15:1024:16], T.cr[:, 0:1], A.mult, -1.0, A.add)
 
     def own(i):
         return T.H[:, 16 * i + 15:16 * i + 16]
 
     def s_rows(rows, src, name, c0, hs):
-        def sign(i):
-            act(name + " " + hs, "sg%d sh%d sj%d" % (i, i, i) + (" si%d" % i if c0 == 0 else ""), T.sg[:, C * i + c0:C * i + C], src[:, 0:C - c0], F.Sign,
-                bias=own(i), scale=-1.0)
-
-        for n, i in enumerate(rows):
-            if n == 0:
-                sign(i)
-            if n + 1 < len(rows):
-                sign(rows[n + 1])
+        for i in rows:
             a, b = C * i, 16 * i + 16
+            act("@%d %s %s +%d" % (C - c0, name, hs, 3000 if c0 else 0), "sg%d sh%d sj%d" % (i, i, i) + (" si%d" % i if c0 == 0 else ""),
+                T.sg[:, a + c0:a + C], src[:, 0:C - c0], F.Sign, bias=own(i), scale=-1.0)
             if i < 15:
-                act("sg%d" % i, "sh%d at%d" % (i, i), T.sg[:, a + b:a + C], T.sg[:, a + b:a + C], F.Relu, scale=-1.0, accum_out=T.at[:, i:i + 1])
-            act("sg%d" % i, "sj%d ag%d" % (i, i), T.sg[:, a + c0:a + b], T.sg[:, a + c0:a + b], F.Relu, accum_out=T.ag[:, i:i + 1])
+                act("@%d sg%d" % (max(64, C - b) + 24, i), "sh%d at%d" % (i, i), T.sg[:, a + b:a + C], T.sg[:, a + b:a + C], F.Relu, scale=-1.0,
+                    accum_out=T.at[:, i:i + 1])
+            act("@%d sg%d" % (max(64, b - c0) + 24, i), "sj%d ag%d" % (i, i), T.sg[:, a + c0:a + b], T.sg[:, a + c0:a + b], F.Relu,
+                accum_out=T.ag[:, i:i + 1])
 
     def to_list(src, name, c0, n, tag, m):
-        tt(name + " mk", "ms" + tag, T.ms[:, c0:c0 + n], src[:, 0:n], T.mk[:, 0:n], A.mult)
-        op("V", name, "mx%d" % m, lambda q: q.tensor_reduce(T.mx[:, m:m + 1], src[:, 0:n], AxisListType.X, A.max))
-        scan("nm ms" + tag, "H" + tag, T.H[:, c0:c0 + n], T.nm[:, 0:n], T.ms[:, c0:c0 + n], 0.0, A.mult, A.add)
-
-    def equal(src, name, c0, n, tag):
-        tt("H%s %s" % (tag, name), "eq" + tag, T.eq[:, c0:c0 + n], T.H[:, c0:c0 + n], src[:, 0:n], A.is_equal)
-
-    def ties(c0, n, tag):
-        scan("nm eq" + tag, "co" + tag, T.co[:, c0:c0 + n], T.nm[:, 0:n], T.eq[:, c0:c0 + n], 0.0, A.mult, A.add)
+        tt("@%d %s mk" % (n, name), "ms" + tag, T.ms[:, c0:c0 + n], src[:, 0:n], T.mk[:, 0:n], A.mult)
+        op("V", "@%d %s" % (n, name), "mx%d" % m, lambda q: q.tensor_reduce(T.mx[:, m:m + 1], src[:, 0:n], AxisListType.X, A.max))
+        scan("@%d nm ms%s" % (n, tag), "H" + tag, T.H[:, c0:c0 + n], T.nm[:, 0:n], T.ms[:, c0:c0 + n], 0.0, A.mult, A.add)
+        tt("@%d H%s %s" % (n, tag, name), "eq" + tag, T.eq[:, c0:c0 + n], T.H[:, c0:c0 + n], src[:, 0:n], A.is_equal)
+        scan("@%d nm eq%s" % (n // 2, tag), "co" + tag, T.co[:, c0:c0 + n], T.nm[:, 0:n], T.eq[:, c0:c0 + n], 0.0, A.mult, A.add)
 
     def early():
         mm("qur sur qxo qxm", "pa", T.pa[:, 0:M], T.qur, T.sur, 0, T.qx, T.sx, K, M)
         mm("qur sur qxo qxm", "pb", T.pb[:, 0:M], T.qur, T.sur, 0, T.qx, T.sx, K, M)
         to_list(T.pa, "pa", K, M, "m", 0)
         lo, h = 4 + NE, M // 2
-        s_rows(list(range(lo, 16 - NF)), T.pb, "pb", K, "Hm")
-
-        def v_sum(i):
-            total("ce%d cf%d" % (i, i), "ceo%d" % i, T.ceo[:, h * (i - 4):h * (i - 3)], T.ce, M * (i - 4), M, float(K))
-
-        def v_row(i):
+        s_rows(range(lo, 16), T.pb, "pb", K, "Hm")
+        for i in range(4, lo):
             a, b = M * (i - 4), 16 * i + 16 - K
-            ts("pa Hm", "ce%d" % i, T.ce[:, a:a + b], T.pa[:, 0:b], own(i), A.is_ge)
-            if i > 4:
-                v_sum(i - 1)
-            ts("pa Hm", "cf%d" % i, T.ce[:, a + b:a + M], T.pa[:, b:M], own(i), A.is_gt)
-
-        def last():
-            equal(T.pa, "pa", K, M, "m")
-            v_sum(lo - 1)
-            ties(K, M, "m")
-
-        return [lambda: names_to_lists(0), lambda: names_to_lists(1)] + [lambda i=i: v_row(i) for i in range(4, lo)] + [last]
-
-    def late_scores():
-        mm("qur sur qxh qxo qxm", "pc", T.pc[:, 0:C], T.qur, T.sur, 0, T.qx, T.sx, 0, C)
-        mm("qur sur qxh qxo qxm", "pd", T.pd[:, 0:C], T.qur, T.sur, 0, T.qx, T.sx, 0, C)
+            ts("@%d pa Hm" % b, "ce%d" % i, T.ce[:, a:a + b], T.pa[:, 0:b], own(i), A.is_ge)
+            ts("@%d pa Hm" % (M - b), "cf%d" % i, T.ce[:, a + b:a + M], T.pa[:, b:M], own(i), A.is_gt)
+            total("ce%d cf%d" % (i, i), "ceo%d" % i, T.ceo[:, h * (i - 4):h * (i - 3)], T.ce, a, M, float(K))
 
     def late(t):
         nv, n0, lo = (NV, C, NV) if t == 0 else (4, K, 4 + NE)
         h = M // 2
         com = "coh" if t == 0 else "com"
-
-        def row(i, part):
-            a, b = C * i, 16 * i + 16
-            if part == 0:
-                ts("pc Hh", "cb%d" % i, T.cb[:, a:a + b], T.pc[:, 0:b], own(i), A.is_ge)
-            elif part == 1:
-                ts("pc Hh", "cd%d" % i, T.cb[:, a + b:a + C], T.pc[:, b:C], own(i), A.is_gt)
-            else:
-                total("cb%d cd%d" % (i, i), "cbo%d" % i, T.cbo[:, 128 * i:128 * i + 128], T.cb, a, C)
-
-        def short(i, part):
-            if part == 0:
-                act("pd Hm", "si%d" % i, T.sg[:, C * i:C * i + K], T.pd[:, 0:K], F.Sign, bias=own(i), scale=-1.0)
-            else:
-                act("si%d al0" % i, "si%d al%d" % (i, i), T.sg[:, C * i:C * i + K], T.sg[:, C * i:C * i + K], F.Relu, accum_out=T.al[:, i:i + 1])
-
+        mm("qur sur qxh qxo qxm", "pc", T.pc[:, 0:C], T.qur, T.sur, 0, T.qx, T.sx, 0, C)
+        mm("qur sur qxh qxo qxm", "pd", T.pd[:, 0:C], T.qur, T.sur, 0, T.qx, T.sx, 0, C)
         to_list(T.pc, "pc", 0, n0, "h", 1 if t else 2)
         if t:
             tt("mx0 mx1", "mx2", T.mx[:, 2:3], T.mx[:, 0:1], T.mx[:, 1:2], A.max)
-            short(4, 0)
-        act("pd mx2", "nf", T.nf[:], T.pd[:, 0:C], F.Sign, bias=T.mx[:, 2:3], scale=-1.0)
-        if t:
-            for i in range(5, 17 - NF):
-                if i < 16 - NF:
-                    short(i, 0)
-                short(i - 1, 1)
-            s_rows(list(range(16 - NF, 16)), T.pd, "pd", 0, "Hm")
-        else:
-            s_rows(list(range(nv, 16)), T.pd, "pd", 0, "Hh")
-        srows = range(lo, 16)
-        small = [
-            lambda: equal(T.pc, "pc", 0, n0, "h"),
-            lambda: ties(0, n0, "h"),
-            lambda: scan("nf", "p1", T.p1[:], T.nf[:], T.nf[:], 1.0, A.mult, A.mult),
-            lambda: total("p1", "p2", T.p2[:], T.p1, 0, C),
-            lambda: ts("nlf pos p2", "nn", T.nn[:], T.nlf[:], T.p2[:, 127:128], A.not_equal, 256.0, A.mult),
-            lambda: tt("nn", "n2a", T.n2[:, 0:32], T.nn[:, 0:32], T.nn[:, 32:64], A.min),
-            lambda: tt("n2a", "n2b", T.n2[:, 32:48], T.n2[:, 0:16], T.n2[:, 16:32], A.min),
-            lambda: tt("n2b nn", "n2c", T.n2[:, 48:64], T.n2[:, 32:48], T.nn[:, 64:80], A.min),
-        ]
+            for i in range(4, 16):
+                act("pd Hm", "si%d" % i, T.sg[:, C * i:C * i + K], T.pd[:, 0:K], F.Sign, bias=own(i), scale=-1.0)
+                act("@88 si%d" % i, "si%d al%d" % (i, i), T.sg[:, C * i:C * i + K], T.sg[:, C * i:C * i + K], F.Relu, accum_out=T.al[:, i:i + 1])
+        act("@256 pd mx2", "nf", T.nf[:], T.pd[:, 0:C], F.Sign, bias=T.mx[:, 2:3], scale=-1.0)
         if t == 0:
-            small = [lambda: None] * (2 * nv - 10) + [lambda: names_to_lists(0), lambda: names_to_lists(1)] + small
+            s_rows(range(nv, 16), T.pd, "pd", 0, "Hh")
+        srows = range(lo, 16)
+        scan("@128 nf", "p1", T.p1[:], T.nf[:], T.nf[:], 1.0, A.mult, A.mult)
+        total("p1", "p2", T.p2[:], T.p1, 0, C)
+        ts("@80 nlf pos p2", "nn", T.nn[:], T.nlf[:], T.p2[:, 127:128], A.not_equal, 256.0, A.mult)
+        tt("nn", "n2a", T.n2[:, 0:32], T.nn[:, 0:32], T.nn[:, 32:64], A.min)
+        tt("n2a", "n2b", T.n2[:, 32:48], T.n2[:, 0:16], T.n2[:, 16:32], A.min)
+        tt("n2b nn", "n2c", T.n2[:, 48:64], T.n2[:, 32:48], T.nn[:, 64:80], A.min)
+        ts("@128 i0 p2", "rt", T.rt[:], T.i0[:], T.p2[:, 127:128], A.not_equal, 2.0 ** 25, A.mult)
         for i in range(nv):
-            for part in range(2):
-                row(i, part)
-                small.pop(0)()
+            a, b = C * i, 16 * i + 16
+            ts("@%d pc Hh" % b, "cb%d" % i, T.cb[:, a:a + b], T.pc[:, 0:b], own(i), A.is_ge)
+            ts("@%d pc Hh" % (C - b), "cd%d" % i, T.cb[:, a + b:a + C], T.pc[:, b:C], own(i), A.is_gt)
+            total("cb%d cd%d" % (i, i), "cbo%d" % i, T.cbo[:, 128 * i:128 * i + 128], T.cb, a, C)
         tt("ln " + com, "e2", T.e2[:, lo:16], T.ln[:, lo:16], T.co[:, 16 * lo + 15:C:16], A.subtract)
+        tt(names("cbo%d", range(nv)) + " coh", "byb", T.by[:, 0:nv], T.cbo[:, 127:128 * nv:128], T.co[:, 15:16 * nv:16], A.subtract)
+        tt("e2 " + names("at%d", srows), "e1", T.e1[:, lo:16], T.e2[:, lo:16], T.at[:, lo:16], A.add)
         if t:
             tt(names("ceo%d", range(4, lo)) + " com", "eev", T.ee[:, 4:lo], T.ceo[:, h - 1:h * (lo - 4):h], T.co[:, K + 15:16 * lo:16], A.subtract)
-        for i in range(nv):
-            row(i, 2)
-        ts("i0 p2", "rt", T.rt[:], T.i0[:], T.p2[:, 127:128], A.not_equal, 2.0 ** 25, A.mult)
-        tt(names("cbo%d", range(nv)) + " coh", "byb", T.by[:, 0:nv], T.cbo[:, 127:128 * nv:128], T.co[:, 15:16 * nv:16], A.subtract)
-        if t:
-            tt("e2 " + names("al%d", range(lo, 16 - NF)), "e3", T.e2[:, lo:16], T.e2[:, lo:16], T.al[:, lo:16], A.subtract)
-            tt("eev " + names("al%d", range(4, lo)), "byd", T.by[:, 4:lo], T.ee[:, 4:lo], T.al[:, 4:lo], A.subtract)
-        tt("e2 e3 " + names("at%d", srows), "e1", T.e1[:, lo:16], T.e2[:, lo:16], T.at[:, lo:16], A.add)
-        tt("e1 " + names("ag%d", srows), "bya", T.by[:, lo:16], T.e1[:, lo:16], T.ag[:, lo:16], A.subtract)
-        tt("bya byb byd n2c", "byc", T.by[:, 16:32], T.by[:, 0:16], T.n2[:, 48:64], A.add)
-        ts("bya byb byd cr5", "bys", T.bys[:], T.by[:, 0:16], T.cr[:, 5:6], A.mult)
-        cp("bya byb byc byd", "byu", T.byu[:], T.by[:])
-        cp("bya byb byd", "byh", T.byh[:], T.by[:, 0:16])
+            tt("e1 " + names("ag%d", srows), "ees", T.ee[:, lo:16], T.e1[:, lo:16], T.ag[:, lo:16], A.subtract)
+            tt("eev ees " + names("al%d", range(4, 16)), "bya", T.by[:, 4:16], T.ee[:, 4:16], T.al[:, 4:16], A.subtract)
+        else:
+            tt("e1 " + names("ag%d", srows), "bya", T.by[:, lo:16], T.e1[:, lo:16], T.ag[:, lo:16], A.subtract)
+        tt("bya byb n2c", "byc", T.by[:, 16:32], T.by[:, 0:16], T.n2[:, 48:64], A.add)
+        cp("bya byb byc", "byu", T.byu[:], T.by[:])
+        ts("bya byb cr5", "bys", T.bys[:], T.by[:, 0:16], T.cr[:, 5:6], A.mult)
+        cp("bya byb", "byh", T.byh[:], T.by[:, 0:16])
         for p in (1, 0):
-            pick("VS"[p], T1 + " byu", "q1%d" % p, T.q1[:, 128 * p:128 * p + 128], T.t1[:].indirect(T.byu[:, 16 + 8 * p:24 + 8 * p]))
+            pick("VS"[p], "@g128 byu " + T1, "q1%d" % p, T.q1[:, 128 * p:128 * p + 128], T.t1[:].indirect(T.byu[:, 16 + 8 * p:24 + 8 * p]))
 
-    def least(tab, name, gg, mo, tmp, rst, rname):
-        act(name + " nl", "g1", gg[:, 1:768:3], tab[:].indirect(T.nl[:, 32:48]), F.Copy)
-        act(name + " nl", "g2", gg[:, 2:768:3], tab[:].indirect(T.nl[:, 48:64]), F.Copy)
-        tt(name + " nl rt", "tmp", tmp[:], tab[:].indirect(T.nl[:, 0:16]), T.rt[:], A.min)
-        tt(name + " nl tmp", "g0", gg[:, 0:768:3], tab[:].indirect(T.nl[:, 16:32]), tmp[:], A.min)
-        scan("g0 g1 g2 " + rname, "mo", mo[:], rst[:], gg[:], 0.0, A.max, A.min)
+    def least(tab, name, gg, mo, tmp, rst, rname, cyc):
+        for h in range(2):
+            a, b, o, r = 384 * h, 384 * h + 384, 8 * h, "@g128 nl " + name
+            act(r, "g1%d" % h, gg[:, a + 1:b:3], tab[:].indirect(T.nl[:, 32 + o:40 + o]), F.Copy)
+            act(r, "g2%d" % h, gg[:, a + 2:b:3], tab[:].indirect(T.nl[:, 48 + o:56 + o]), F.Copy)
+            tt(r + " rt", "tmp%d" % h, tmp[:, 128 * h:128 * h + 128], tab[:].indirect(T.nl[:, o:o + 8]), T.rt[:, 128 * h:128 * h + 128], A.min)
+            tt(r + " tmp%d" % h, "g0%d" % h, gg[:, a:b:3], tab[:].indirect(T.nl[:, 16 + o:24 + o]), tmp[:, 128 * h:128 * h + 128], A.min)
+            scan("@%d g0%d g1%d g2%d %s" % (cyc, h, h, h, rname), "mo%d" % h, mo[:, a:b], rst[:, a:b], gg[:, a:b], 0.0, A.max, A.min)
 
-    def keys(mo, conv):
-        scan("mo c16", "conv", conv[:], T.c16[:], mo[:, 2:768:3], 0.0, A.mult, A.max)
-        tt("i0 byu mo", "kr", T.kr[:], T.i0[:].indirect(T.byu[:, 0:16]), mo[:, 2:768:3], A.add)
-        tt("conv bys", "kl", T.kl[:], conv[:, 15:C:16], T.bys[:], A.add)
+    def plus(out, name, tab, tname, mo):
+        for h in range(2):
+            tt("@g128 byu mo%d %s" % (h, tname), name + str(h), out[:, 128 * h:128 * h + 128], tab[:].indirect(T.byu[:, 8 * h:8 * h + 8]),
+               mo[:, 384 * h + 2:384 * h + 384:3], A.add)
 
-    def ranking(nb, narrow, out, name, c0, c1, c2, between=None):
+    def keys(mo, conv, cyc):
+        for h in range(2):
+            scan("@%d mo%d c16" % (cyc, h), "conv%d" % h, conv[:, 128 * h:128 * h + 128], T.c16[:, 0:128], mo[:, 384 * h + 2:384 * h + 384:3],
+                 0.0, A.mult, A.max)
+        plus(T.kr, "kr", T.i0, "i0", mo)
+        tt("conv0 conv1 bys", "kl", T.kl[:], conv[:, 15:C:16], T.bys[:], A.add)
+
+    def ranking(nb, narrow, out, name, c0, c1, c2):
         ns = 16 - nb
         for i in range(ns):
-            act("kr kl cr6", "sg%d sh%d si%d sj%d ab%d" % (i, i, i, i, i), T.sg[:, C * i:C * i + C], T.kr[:], F.Sign, bias=T.kl[:, i:i + 1],
-                scale=T.cr[:, 6:7], accum_out=T.ab[:, i:i + 1])
+            act("@280 kr0 kr1 kl cr6", "sg%d sh%d si%d sj%d ab%d" % (i, i, i, i, i), T.sg[:, C * i:C * i + C], T.kr[:], F.Sign,
+                bias=T.kl[:, i:i + 1], scale=T.cr[:, 6:7], accum_out=T.ab[:, i:i + 1])
         if narrow:
-            ts("conv cr0", "mj", T.mj[:], T.vb2[:, 15:C:16], T.cr[:, 0:1], A.mult)
-            cp("kr", "ku", T.ku[:], T.kr[:])
-        for i in range(ns, 17):
-            if i < 16 and narrow:
-                ts("ku mj byh", "cb%d cd%d" % (i, i), T.cb[:, C * i:C * i + C], T.ku[:], T.mj[:, i:i + 1], A.subtract, T.byh[:, i:i + 1], A.is_lt)
-            elif i < 16:
-                ts("kr kl cr5", "cb%d cd%d" % (i, i), T.cb[:, C * i:C * i + C], T.kr[:], T.cr[:, 5:6], A.mult, T.kl[:, i:i + 1], A.is_gt)
-            if i > ns:
-                total("cb%d" % (i - 1), "cbo%d" % (i - 1), T.cbo[:, 128 * i - 128:128 * i], T.cb, C * (i - 1), C)
+            ts("conv0 conv1 cr0", "mj", T.mj[:], T.vb2[:, 15:C:16], T.cr[:, 0:1], A.mult)
+            for h in range(2):
+                cp("@128 kr%d" % h, "ku%d" % h, T.ku[:, 128 * h:128 * h + 128], T.kr[:, 128 * h:128 * h + 128])
+        for i in range(ns, 16):
+            if narrow:
+                ts("@128 ku0 ku1 mj byh", "cb%d cd%d" % (i, i), T.cb[:, C * i:C * i + C], T.ku[:], T.mj[:, i:i + 1], A.subtract, T.byh[:, i:i + 1], A.is_lt)
+            else:
+                ts("@256 kr0 kr1 kl cr5", "cb%d cd%d" % (i, i), T.cb[:, C * i:C * i + C], T.kr[:], T.cr[:, 5:6], A.mult, T.kl[:, i:i + 1], A.is_gt)
+            total("cb%d" % i, "cbo%d" % i, T.cbo[:, 128 * i:128 * i + 128], T.cb, C * i, C)
         ts(names("cbo%d", range(ns, 16)) + " un0", name + "a", out[:, ns:16], T.cbo[:, 128 * ns + 127:2048:128], c0, A.add)
-        if between:
-            between()
         ts(names("ab%d", range(ns)) + " un1", name + "b", out[:, 0:ns], T.ab[:, 0:ns], c1, A.mult, c2, A.add)
 
-    def unpack():
+    def order():
         for b in range(4):
             mm("qe qxh qxo qxm", "pw%d" % b, bank(b, C), T.qe, T.se, 128 * b, T.qx, T.sx, 0, C)
-
-    def halves(b):
-        act("pw%d" % b, "DX%d" % b, T.DX[:, b:1024:4], bank(b, C), F.Copy)
-
-    CUT = 16 - NB[1] + NB[1] % 2
-
-    def order(t):
-        if t > 0:
-            unpack()
-        least(T.q1, "q10 q11", T.gb, T.mb, T.tb, T.r3, "r3")
-        if t > 0:
-            halves(0)
-        else:
-            act(T1, "tp", T.tp[:], T.t1[:], F.Copy, scale=256.0)
-        act("mo", "nr un0", T.nr[:], T.mb[:, 2:768:3], F.Relu, bias=-1.0, scale=2.0 ** -16, accum_out=T.un[:, 0:1])
+            act("@256 pw%d +1500" % b, "DX%d" % b, T.DX[:, b:1024:4], bank(b, C), F.Copy)
+        least(T.q1, "q10 q11", T.gb, T.mb, T.tb, T.r3, "r3", 192)
+        act("@280 mo0 mo1", "nr un0", T.nr[:], T.mb[:, 2:768:3], F.Relu, bias=-1.0, scale=2.0 ** -16, accum_out=T.un[:, 0:1])
         act("un0", "un1", T.un[:, 1:2], T.un[:, 0:1], F.Identity, bias=127.5)
-        keys(T.mb, T.vb2)
+        keys(T.mb, T.vb2, 64)
         ranking(NB[0], True, T.pl, "pl", T.un[:, 0:1], 0.5, T.un[:, 1:2])
         for p in (0, 1):
-            pick("SV"[p], "tp pla plb", "pp%d" % p, T.pp[:, 128 * p:128 * p + 128], T.tp[:].indirect(T.pl[:, 8 * p:8 * p + 8]))
-        least(T.pp, "pp0 pp1", T.gb, T.mb, T.tb, T.r3, "r3")
-        if t == 0:
-            act("cc2 oa", "c4", T.c4[:], T.cc[:, 64:80].indirect(T.oa[:]), F.Copy)
-        else:
-            halves(1)
-        tt(T1 + " byu mo", "k3", T.k3[:], T.t1[:].indirect(T.byu[:, 0:16]), T.mb[:, 2:768:3], A.add)
-        if t == 0:
-            quant("eb", "qe", T.qe[:], T.se[:], T.eb[:])
-            unpack()
-        least(T.k3, "k3", T.gf, T.mf, T.tf, T.r3f, "r3f")
-        for b in (range(4) if t == 0 else (2, 3)):
-            halves(b)
-        keys(T.mf, T.vf)
-        ranking(NB[1], False, T.npl, "npl", 0.0, -0.5, 127.5,
-                lambda: cp("i1 npla", "lr", T.lr[:].indirect(T.npl[:, CUT:16]), T.i1[:, 16 * CUT:C]))
-
-    def relu(b, n, c0, w):
-        out, a = T.X[:, 4 * c0 + b:4 * (c0 + n):4], bank(b, n)
-        if b % 2:
-            ts("pw%d" % b, w, out, a, 0.0, A.max, 0.03125, A.mult)
-        else:
-            act("pw%d" % b, w, out, a, F.Relu, scale=0.03125)
-
-    def main_codes():
-        quant("Xm0 Xm1 Xm2 Xm3", "qxo qxm", T.qx[:, K:C], T.sx[:, K:C], T.X[:, 4 * K:1024])
+            pick("SV"[p], "@g128 tp pla plb", "pp%d" % p, T.pp[:, 128 * p:128 * p + 128], T.tp[:].indirect(T.pl[:, 8 * p:8 * p + 8]))
+        least(T.pp, "pp0 pp1", T.gb, T.mb, T.tb, T.r3, "r3", 192)
+        plus(T.k3, "k3", T.t1, T1, T.mb)
+        least(T.k3, "k30 k31", T.gf, T.mf, T.tf, T.r3f, "r3f", 384)
+        keys(T.mf, T.vf, 128)
+        ranking(NB[1], False, T.npl, "npl", 0.0, -0.5, 127.5)
 
     def move(t):
         qt, st = T["qt%d" % t], T["st%d" % t]
-        dxs = "DX0 DX1 DX2 DX3 l4"
-
-        def name(e):
-            act("ir nl", "NA%d" % e, T.NA[:, e:1024:4], T.ir[:].indirect(T.nl[:, 16 * e:16 * e + 16]), F.Copy)
-
-        def renamed(e, p):
-            if t < R - 1:
-                pick(e, "NA0 NA1 NA2 NA3 l4", "NR%d" % p, T.NR[:, 256 * p:256 * p + 256], T.NA[:].indirect(T.l4[:, 16 * p:16 * p + 16]))
-
-        act("i1 npla nplb", "ir", T.ir[:], T.i1[:].indirect(T.npl[:]), F.Copy)
-        name(0)
-        cp("i1 npla nplb", "lr", T.lr[:].indirect(T.npl[:, 0:CUT]), T.i1[:, 0:16 * CUT])
-        scan("c4 lr", "lc", T.lc[:], T.c4[:], T.lr[:], 0.0, A.mult, A.max)
+        dxs = "@g256 DX0 DX1 DX2 DX3 l4"
+        cut = 16 - NB[1] + NB[1] % 2
+        cp("@s%d i1 npla" % (C - 16 * cut), "lr", T.lr[:].indirect(T.npl[:, cut:16]), T.i1[:, 16 * cut:C])
+        cp("@s%d i1 npla nplb" % (16 * cut), "lr", T.lr[:].indirect(T.npl[:, 0:cut]), T.i1[:, 0:16 * cut])
+        scan("@128 c4 lr", "lc", T.lc[:], T.c4[:], T.lr[:], 0.0, A.mult, A.max)
         ts("lc cr2 cr3", "l4", T.l4[:], T.lc[:, 3:C:4], T.cr[:, 2:3], A.mult, T.cr[:, 3:4], A.add)
         if t < R - 1:
-            cp(XS + " l4", "TT0 TT1", T.TT[:, 0:256], T.X[:].indirect(T.l4[:, 48:64]))
+            cp("@g256 l4 " + XS, "TT0 TT1", T.TT[:, 0:256], T.X[:].indirect(T.l4[:, 48:64]))
         else:
             for p in (1, 0):
-                pick("VS"[p], XS + " l4", "TT%d" % p, T.TT[:, 128 * p:128 * p + 128], T.X[:].indirect(T.l4[:, 48 + 8 * p:56 + 8 * p]))
-        quant("TT0 TT1 TTz", "qt", qt[:], st[:], T.TT[:])
-        before("G", ["qt"], [])
-        at = 128 + K * t
-        arr = T.sem["arr%d" % t]
-        g.remote_dma(T.lq[:, at:at + K].bitcast(dt.uint8), qt[:, 0:K].bitcast(dt.uint8), arr, T.sem["sent"], pid, rid, topo.mask(core, nxt))
-        g.remote_dma(T.ls[:, at:at + K], st[:, 0:K], arr, T.sem["sent"], pid, rid, topo.mask(core, nxt))
-        count["sent"] += 2 * n_out
-        count["arr%d" % t] = 2 * n_in
-        ev = ("arr%d" % t, 2 * n_in)
-        clock[ev], writer["land%d" % t] = {ev[0]: ev[1]}, ev
+                pick("VS"[p], "@g128 l4 " + XS, "TT%d" % p, T.TT[:, 128 * p:128 * p + 128], T.X[:].indirect(T.l4[:, 48 + 8 * p:56 + 8 * p]))
+        quant(128, "TT0 TT1 TTz", "qt%d" % t, qt[:], st[:], T.TT[:])
+        at, arr = 128 + K * t, "arr%d" % t
+
+        def send():
+            g.remote_dma(T.lq[:, at:at + K].bitcast(dt.uint8), qt[:, 0:K].bitcast(dt.uint8), T.sem[arr], T.sem["sent"], pid, rid, topo.mask(core, nxt))
+            g.remote_dma(T.ls[:, at:at + K], st[:, 0:K], T.sem[arr], T.sem["sent"], pid, rid, topo.mask(core, nxt))
+            count["sent"] += 2 * n_out
+
+        record("G", "qt%d" % t, "land%d" % t, send, 500.0, TRAVEL, arr, 2 * n_in)
         for p in range(3):
             act(dxs, "EH%d" % p, T.EH[:, 256 * p:256 * p + 256], T.DX[:].indirect(T.l4[:, 16 * p:16 * p + 16]), F.Copy)
             tt(dxs + " EH%d" % p, "Z%d" % (p + 1), T.Z[:, 256 * p + 256:256 * p + 512], T.DX[:].indirect(T.l4[:, 16 * p + 16:16 * p + 32]),
                T.EH[:, 256 * p:256 * p + 256], A.add)
-        quant("Z1 Z2 Z3", "qz", T.qz[:], T.sz[:], T.Z[:, 256:1024])
+        quant(M, "Z1 Z2 Z3", "qz", T.qz[:], T.sz[:], T.Z[:, 256:1024])
         for b in range(4):
-            mm("qw qz", "pw%d" % b, bank(b, M), T.qw, T.sw, 128 * b, T.qz, T.sz, 0, M)
-        for e in (1, 2, 3):
-            name(e)
-        if t == 0:
-            quant(XS, "lq", T.lq[:, 0:128], T.ls[:, 0:128], T.X[:, 0:512])
-        if t == R - 1:
-            quant("vb", "qv", T.qv[:], T.sv[:], T.vb[:])
-        relu(0, M, K, "Xm0")
-        relu(1, M, K, "Xm1")
-        renamed("V", 0)
-        relu(2, M, K, "Xm2")
-        relu(3, M, K, "Xm3")
-        renamed("S", 2)
-        renamed("S", 3)
-        if t < R - 1:
-            main_codes()
-        renamed("V", 1)
+            mm("qw sw qz", "pw%d" % b, bank(b, M), T.qw, T.sw, 128 * b, T.qz, T.sz, 0, M)
+            if b % 2:
+                ts("@192 pw%d" % b, "Xm%d" % b, T.X[:, 4 * K + b:1024:4], bank(b, M), 0.0, A.max, 0.03125, A.mult)
+            else:
+                act("@192 pw%d" % b, "Xm%d" % b, T.X[:, 4 * K + b:1024:4], bank(b, M), F.Relu, scale=0.03125)
+        quant(M, "Xm0 Xm1 Xm2 Xm3", "qxo qxm", T.qx[:, K:C], T.sx[:, K:C], T.X[:, 4 * K:1024])
+        act("@g256 i1 npla nplb", "ir", T.ir[:], T.i1[:].indirect(T.npl[:]), F.Copy)
+        for e in range(4):
+            act("@g256 ir nl", "NA%d" % e, T.NA[:, e:1024:4], T.ir[:].indirect(T.nl[:, 16 * e:16 * e + 16]), F.Copy)
+        for p in range(4 if t < R - 1 else 0):
+            pick("VVSS"[p], "@g256 NA0 NA1 NA2 NA3 l4", "NR%d" % p, T.NR[:, 256 * p:256 * p + 256], T.NA[:].indirect(T.l4[:, 16 * p:16 * p + 16]))
 
     def mix(t):
         if t == R - 1:
@@ -458,51 +397,36 @@ def rank_program(g, core, T, topo):
             to = [(BANKS[b], bank(b, 128), T.pw[:, 512 * b + K:512 * b + 128]) for b in range(4)]
         for b in range(4):
             mm("qe lq land%d" % t, to[b][0], to[b][1], T.qe, T.se, 128 * b, T.lq, T.ls, K + K * t, 128)
-        for b in range(4):
             tt(to[b][0] + " EH0", "Z0%d" % b, T.Z[:, b:256:4], to[b][2], T.EH[:, b:256:4], A.add)
-        quant("Z00 Z01 Z02 Z03 Z1", "qh", T.qh[:], T.sh[:], T.Z[:, 0:512])
+        quant(128, "Z00 Z01 Z02 Z03 Z1", "qh", T.qh[:], T.sh[:], T.Z[:, 0:512])
         for b in range(4):
-            mm("qw qh", "pw%d" % b, bank(b, 128), T.qw, T.sw, 128 * b, T.qh, T.sh, 0, 128)
-
-    def layer():
-        for b in range(4):
-            ts("pw%d" % b, "Xh%d" % b + (" Xh" if b == 0 else ""), T.X[:, b:4 * K:4], bank(b, K), 0.0, A.max, 0.03125, A.mult)
-        quant("Xh0 Xh1 Xh2 Xh3 Xm0 Xm1 Xm2 Xm3", "qxh qxo Xh", T.qx[:, 0:128], T.sx[:, 0:128], T.X[:, 0:512])
-
-    def run(todo, left):
-        while len(todo) > left:
-            todo.pop(0)()
+            mm("qw sw qh", "pw%d" % b, bank(b, 128), T.qw, T.sw, 128 * b, T.qh, T.sh, 0, 128)
+            ts("pw%d qt%d lq" % (b, t), "Xh%d" % b, T.X[:, b:4 * K:4], bank(b, K), 0.0, A.max, 0.03125, A.mult)
+        quant(128, "Xh0 Xh1 Xh2 Xh3 Xm0 Xm1 Xm2 Xm3", "qxh qxo Xh", T.qx[:, 0:128], T.sx[:, 0:128], T.X[:, 0:512])
 
     for t in range(R):
-        if t == 0:
-            late_scores()
-        else:
-            todo = early()
-            run(todo, BEHIND[0])
+        names_to_lists()
+        if t:
+            early()
             mix(t - 1)
-            run(todo, BEHIND[1])
-            layer()
-            late_scores()
-            run(todo, 0)
         late(t)
-        order(t)
+        order()
         move(t)
 
-    act("NA0 NA1 NA2 NA3 l4", "ON", T.ON[:], T.NA[:].indirect(T.l4[:]), F.Identity, bias=-1.0)
-    dma("S", "out", "ON", "", T.on[:], T.ON[0:128:16, :], last=False)
+    act("@g1024 NA0 NA1 NA2 NA3 l4", "ON", T.ON[:], T.NA[:].indirect(T.l4[:]), F.Identity, bias=-1.0)
+    dma("S", "out", "ON", "", T.on[:], T.ON[0:128:16, :])
     mix(R - 1)
-    main_codes()
     mm("qv qxm", "pa", T.pa[:, 0:128], T.qv, T.sv, 0, T.qx, T.sx, 128, 128)
-    dma("Y", "out", "qxm", "", T.oc[:, 512:1024], T.qx[:, 128:C].bitcast(dt.uint8), last=False)
-    act("pa", "ym", T.ys[:, 128:C], T.pa[:, 0:128], F.Copy)
-    dma("S", "out", "ym", "", T.y[:, 128:C], T.ys[:, 128:C], last=False)
-    layer()
+    dma("Y", "out", "qxm", "", T.oc[:, 512:1024], T.qx[:, 128:C].bitcast(dt.uint8))
+    act("@128 pa", "ym", T.ys[:, 128:C], T.pa[:, 0:128], F.Copy)
+    dma("S", "out", "ym", "", T.y[:, 128:C], T.ys[:, 128:C])
     mm("qv qxh qxo", "pc", T.pc[:, 0:128], T.qv, T.sv, 0, T.qx, T.sx, 0, 128)
-    dma("Y", "out", "qxh qxo", "", T.oc[:, 0:512], T.qx[:, 0:128].bitcast(dt.uint8), last=False)
+    dma("Y", "out", "qxh qxo", "", T.oc[:, 0:512], T.qx[:, 0:128].bitcast(dt.uint8))
     for k in range(4):
-        dma("S" if k else "Y", "out", "qxh qxo qxm", "", T.osc[4 * k:4 * k + 4, :], T.sx[32 * k:32 * k + 4, :], last=False)
-    cp("pc", "yh", T.ys[:, 0:128], T.pc[:, 0:128])
-    dma("Y", "out", "yh", "", T.y[:, 0:128], T.ys[:, 0:128], last=False)
+        dma("S" if k else "Y", "out", "qxh qxo qxm", "", T.osc[4 * k:4 * k + 4, :], T.sx[32 * k:32 * k + 4, :])
+    cp("@128 pc", "yh", T.ys[:, 0:128], T.pc[:, 0:128])
+    dma("Y", "out", "yh", "", T.y[:, 0:128], T.ys[:, 0:128])
+    issue()
     for s in SEMAPHORES:
         if count[s]:
             g.wait_ge(T.sem[s], count[s])

@@ -1,20 +1,22 @@
-from concourse.mybir import dt, AluOpType as A, AxisListType, ActivationFunctionType as F
+import numpy as np
+from concourse.mybir import dt, AluOpType as A, ActivationFunctionType as F
 
 C, K, R = 256, 64, 3
 M = C - K
-NB = (9, 6)
-NV = 9
-NE = 4
-WAKE, TRAVEL = 200.0, 3500.0
-SOONER = {"msh": 300.0, "pla": -200.0, "eqh": 300.0, "cbo0": 200.0}
+NV = 10
+NE = 5
+NL = 2
+NB = 7
+WAKE, TRAVEL = 200.0, 2800.0
 BF, FP, U16, I32, Q4, U8 = "bfloat16", "float32", "uint16", "int32", "float8_e4m3fn_x4", "uint8"
+SG = 272
 SIZES = {
-    BF: "X 1024 ub 512 vb 512 eb 2048 TT 512 Z 1024 DX 1024 EH 768 kk 32 cc 80 mk 256 nm 256 c16 256 c4 256 i1 256 i0 256 t1 512 tp 512 "
-        "r3 768 NR 1024 NA 1024 NC 1024 eq 256 co 256 nf 256 p1 256 p2 128 rt 256 ce 2304 ceo 1152 cb 4096 cbo 2048 sg 4096 q1 256 pp 256 "
-        "nr 256 mj 16 byh 16 gb 768 mb 768 tb 256 vb2 256 lr 256 lc 256 ir 256",
-    FP: "cr 8 ln 16 r3f 768 nlf 80 ON 1024 ms 256 H 256 mx 4 nn 80 n2 64 ag 16 at 16 al 16 ab 16 e1 16 e2 16 ee 16 by 32 bys 16 un 2 "
-        "k3 256 kr 256 kl 16 gf 768 mf 768 tf 256 vf 256 ys 256",
-    U16: "nbu 64 oa 16 ou 8 nl 64 byu 32 pl 16 npl 16 l4 64 ku 256",
+    BF: "X 1024 ub 512 vb 512 eb 2048 TT 512 Z 1024 DX 1024 EH 768 kk 32 cc 80 mk 256 nm 256 c16 256 c4 256 i1 256 i0 256 t1 512 "
+        "NR 1024 NA 1024 NC 1024 eq 256 co 256 nf 256 cs 256 one 256 rt 256 ce 2304 ceo 1152 cb 4096 cbo 2048 sg 4352 q1 256 "
+        "d2 1024 d3 1024 tb 256 lr 256 lc 256 ir 256 iq 256 cr2 256 cl 256 eqb 256 cob 256 rs 80",
+    FP: "cr 10 ln 16 nlf 80 ON 1024 ms 256 H 256 mx 256 mh 64 nn 80 n2 80 at 16 ab 16 e1 16 e2 16 e3 16 ac 16 lb 16 ci 16 rb 16 bc 16 "
+        "d4 768 cap 256 g2 1024 g4 768 m2 1024 m3 1024 m4 784 tf 256 mb 256 Hb 256 W 512 ys 256",
+    U16: "nbu 64 oa 16 ou 8 nl 64 nl4 64 bcu 16 byu 16 rl 16 npl 16 l4 64",
     I32: "nbi 64 di 48 dj 64",
     Q4: "qu 128 qur 128 qv 128 qw 512 qe 512 qx 256 qz 192 qh 128 qt0 128 qt1 128 qt2 128 lq 320",
     U8: "su 128 sur 128 sv 128 sw 512 se 512 sx 256 sz 192 sh 128 st0 128 st1 128 st2 128 ls 320",
@@ -22,7 +24,29 @@ SIZES = {
 SCRATCH = {n: ("sbuf", [128, int(w)], d) for d, s in SIZES.items() for n, w in zip(s.split()[0::2], s.split()[1::2])}
 SCRATCH.update({n: ("psum", [128, w], FP) for n, w in (("pw", 2048), ("pa", 512), ("pb", 512), ("pc", 512), ("pd", 512))})
 SEMAPHORES = ["V", "S", "P", "G", "ldx", "ldu", "ldn", "ldw", "lds", "ldv", "out", "sent", "arr0", "arr1", "arr2"]
-BANKS = ("pw0", "pw1", "pw2", "pw3", "pa", "pb", "pc", "pd")
+CYC = 0.83
+TRIES, PASSES, JITTER, STRETCH, PLAN = 1000, 2, 300.0, 2500.0, []
+TMP = "VS"
+
+
+def v(name, a=0, b=None, s=1):
+    return (name, a, SCRATCH[name][1][1] if b is None else b, s, None)
+
+
+def at(win, off):
+    return win[:4] + (off,)
+
+
+def col(name, a):
+    return v(name, a, a + 1)
+
+
+def span(x):
+    return range(x[1], x[2], x[3]) if x[3] > 0 else range(x[2] - 1, x[1] - 1, x[3])
+
+
+def length(x):
+    return 16 * len(span(x[4])) if x[4] else len(span(x))
 
 
 def rank_program(g, core, T, topo):
@@ -37,372 +61,440 @@ def rank_program(g, core, T, topo):
     queue = {"V": g.vector, "S": g.scalar, "P": g.tensor, "G": g, "Y": g.sync}
     count = {s: 0 for s in SEMAPHORES}
     known = {e: {} for e in queue}
-    calls, first, writer, readers = [], [], {}, {}
+    calls, first = [], []
+    writer = {n: [-1] * d[1][1] for n, d in SCRATCH.items()}
+    readers = {n: [[] for _ in range(d[1][1])] for n, d in SCRATCH.items()}
+    banks = {}
 
-    def record(e, r, w, fn, cost, late, sem, n):
-        r, w = r.split(), w.split()
-        first.append(sum(float(t) for t in r if t[0] == "+") + SOONER.get(w[0] if w else "", 0.0))
-        need = {writer[t] for t in r + w if t in writer}
-        for t in w:
-            need.update(readers.get(t, []))
-        for t in r:
-            if t in BANKS:
-                need.update(i for i in readers.get(t, []) if calls[i][0] != e)
-        for t in r:
-            readers.setdefault(t, []).append(len(calls))
-        for t in w:
-            writer[t], readers[t] = len(calls), []
-        calls.append((e, need, fn, cost, late, sem, n))
+    def ap(x, word=None):
+        if not isinstance(x, tuple):
+            return x
+        name, a, b, s, off = x
+        if s > 0:
+            t = T[name][:, a:b:s] if s > 1 else T[name][:, a:b]
+        else:
+            t = T[name][:, b - 1:a - 1:s] if a else T[name][:, b - 1::s]
+        if word is not None:
+            t = t.bitcast(word)
+        return t.indirect(ap(off)) if off else t
 
-    def op(e, r, w, fn):
-        cost = 55.0
-        if r[:1] == "@":
-            c, r = (r + " ").split(" ", 1)
-            cost = 55 + {"g": 1.3, "s": 3.2}[c[1]] * int(c[2:]) if c[1] in "gs" else max(55.0, 0.87 * int(c[1:]))
-        record(e, r, w, lambda: fn(queue[e]).then_inc(T.sem[e], 1), cost, 0.0, e, 1)
+    def record(e, r, w, fn, cost, late, sem, n, soon=0.0, after=()):
+        me, need = len(calls), set(after)
+        r = [x for x in r if isinstance(x, tuple)]
+        r += [x[4] for x in r + w if x[4]]
+        for x in r + w:
+            need.update(writer[x[0]][c] for c in span(x))
+            if SCRATCH[x[0]][0] == "psum":
+                for b in {c // 512 for c in span(x)}:
+                    users = banks.setdefault((x[0], b), [])
+                    need.update(i for i in users if calls[i][0] != e)
+                    users.append(me)
+        for x in w:
+            for c in span(x):
+                need.update(readers[x[0]][c])
+        for x in r:
+            for c in span(x):
+                readers[x[0]][c].append(me)
+        for x in w:
+            for c in span(x):
+                writer[x[0]][c], readers[x[0]][c] = me, []
+        first.append(soon)
+        calls.append((e, need - {-1, me}, fn, cost, late, sem, n))
+        return me
 
-    def dma(e, sem, r, w, out, in_):
-        record(e, r, w, lambda: queue[e].dma_start(out, in_).then_inc(T.sem[sem], 16), 60.0, 2200.0, sem, 16)
+    def op(e, r, w, fn, rate=None, more=0.0, soon=0.0, after=()):
+        full = [x for x in r + w if isinstance(x, tuple)]
+        n = length(full[0])
+        if rate is None:
+            rate = 0.5 if e == "V" and all(SCRATCH[x[0]][2] in (BF, U16) for x in full) else 1.0
+        cost = max(64.0, n * rate) * CYC
+        if r and r[0][4]:
+            cost = (50 if e == "V" else 65) + 1.56 * CYC * n
+        if w[0][4]:
+            cost = 50 + 3.8 * CYC * n
+        return record(e, r, w, lambda: fn(queue[e]).then_inc(T.sem[e], 1), cost + more, 0.0, e, 1, soon, after)
 
-    def issue():
+    def dma(e, sem, r, w, out, in_, after=()):
+        x = (r + w)[0]
+        size = len(span(x)) * {BF: 2, U8: 1}.get(SCRATCH[x[0]][2], 4)
+        return record(e, r, w, lambda: queue[e].dma_start(out, in_).then_inc(T.sem[sem], 16), 60.0, 2000.0 + 0.64 * size, sem, 16, 0.0, after)
+
+    def lay(turn, before, back):
+        end, taken = [0.0] * len(calls), {e: [] for e in queue}
+        for i in turn:
+            e, _, _, cost, late = calls[i][:5]
+            if back:
+                t = max([end[j] + WAKE for j in before[i]] + [0.0]) + late
+            else:
+                t = max([end[j] + calls[j][4] + WAKE for j in before[i]] + [0.0])
+            line = taken[e]
+            k, hi = 0, len(line)
+            while k < hi:
+                mid = (k + hi) // 2
+                k, hi = (mid + 1, hi) if line[mid][1] <= t else (k, mid)
+            while k < len(line) and line[k][0] < t + cost:
+                t, k = max(t, line[k][1]), k + 1
+            line.insert(k, (t, t + cost))
+            end[i] = t + cost
+        return end
+
+    def plan():
         n = len(calls)
-        after = [[] for _ in calls]
-        for i, c in enumerate(calls):
-            for j in c[1]:
-                after[j].append(i)
-        rest = [0.0] * n
+        need, after, behind = [], [[] for _ in calls], []
+        for i in range(n):
+            mask, keep = 0, []
+            for j in sorted(calls[i][1], reverse=True):
+                if not mask >> j & 1:
+                    keep.append(j)
+                    mask |= behind[j]
+                    after[j].append(i)
+            need.append(keep)
+            behind.append(mask | 1 << i)
+        rest, best = [0.0] * n, None
         for i in range(n - 1, -1, -1):
             rest[i] = first[i] + calls[i][3] + calls[i][4] + max([WAKE + rest[j] for j in after[i]] + [0.0])
-        left, ready, free = [len(c[1]) for c in calls], [0.0] * n, {e: 0.0 for e in queue}
-        can = [i for i in range(n) if not left[i]]
+        rng = np.random.default_rng(0)
+        for trial in range(TRIES):
+            key, mid = list(rest), float(rng.uniform(0.0, best[0])) if best else 0.0
+            if best:
+                key = [-t + (x if abs(t - mid) < STRETCH else 0.0) for t, x in zip(best[2], rng.normal(0.0, JITTER, n).tolist())]
+            for i in range(n - 1, -1, -1):
+                key[i] = max([key[i]] + [key[j] + 1.0 for j in after[i]])
+            turn = sorted(range(n), key=lambda i: (-key[i], i))
+            for _ in range(PASSES):
+                end = lay(turn, need, False)
+                whole = max(end[i] + calls[i][4] for i in range(n))
+                if best is None or whole <= best[0]:
+                    begin = [end[i] - calls[i][3] for i in range(n)]
+                    best = (whole, sorted(range(n), key=lambda i: (begin[i], i)), begin)
+                back = lay(sorted(range(n), key=lambda i: (-end[i] - calls[i][4], -i)), after, True)
+                turn = sorted(range(n), key=lambda i: (-back[i], i))
+        return best[1]
+
+    def issue():
+        if not PLAN:
+            PLAN.extend(plan())
         event, clock = {}, {}
-        while can:
-            i = min(can, key=lambda k: (max(ready[k], free[calls[k][0]]), -rest[k], k))
-            e = calls[i][0]
-            until = max(ready[i], free[e]) + calls[i][3]
-            for k in can:
-                if calls[k][0] == e and rest[k] > rest[i]:
-                    ti, tk = max(ready[i], free[e]), max(ready[k], free[e])
-                    if tk < until and max(tk + rest[k], tk + calls[k][3] + rest[i]) < max(ti + rest[i], ti + calls[i][3] + rest[k]):
-                        i = k
-            can.remove(i)
-            _, need, fn, cost, late, sem, inc = calls[i]
+        for i in PLAN:
+            e, need, fn, cost, late, sem, inc = calls[i]
             for ev in sorted({event[j] for j in need}, key=lambda ev: (-ev[1], ev[0])):
                 if known[e].get(ev[0], 0) < ev[1]:
                     queue[e].wait_ge(T.sem[ev[0]], ev[1])
-                    for s, v in clock[ev].items():
-                        known[e][s] = max(known[e].get(s, 0), v)
+                    for s, c in clock[ev].items():
+                        known[e][s] = max(known[e].get(s, 0), c)
             fn()
             count[sem] += inc
             event[i] = (sem, count[sem])
             clock[event[i]] = dict(known[e]) if sem[:3] != "arr" else {}
             clock[event[i]][sem] = count[sem]
-            free[e] = max(ready[i], free[e]) + cost
-            for j in after[i]:
-                ready[j] = max(ready[j], free[e] + late + WAKE)
-                left[j] -= 1
-                if not left[j]:
-                    can.append(j)
 
-    def ts(r, w, out, in0, s1, op0, s2=None, op1=None):
+    def ts(out, in0, s1, op0, s2=None, op1=None, **kw):
         if op1 is None:
-            op("V", r, w, lambda q: q.tensor_scalar(out, in0, s1, None, op0))
-        else:
-            op("V", r, w, lambda q: q.tensor_scalar(out, in0, s1, s2, op0, op1))
+            return op("V", [in0, s1], [out], lambda q: q.tensor_scalar(ap(out), ap(in0), ap(s1), None, op0), **kw)
+        return op("V", [in0, s1, s2], [out], lambda q: q.tensor_scalar(ap(out), ap(in0), ap(s1), ap(s2), op0, op1), **kw)
 
-    def tt(r, w, out, a, b, o):
-        op("V", r, w, lambda q: q.tensor_tensor(out, a, b, o))
+    def tt(out, a, b, o, **kw):
+        rate = 1.0 if "psum" in (SCRATCH[a[0]][0], SCRATCH[b[0]][0]) else 2.0
+        return op("V", [a, b], [out], lambda q: q.tensor_tensor(ap(out), ap(a), ap(b), o), rate, **kw)
 
-    def cp(r, w, out, a):
-        op("V", r, w, lambda q: q.tensor_copy(out, a))
+    def cp(out, a, **kw):
+        return op("V", [a], [out], lambda q: q.tensor_copy(ap(out), ap(a)), **kw)
 
-    def scan(r, w, out, a, b, init, o0, o1):
-        op("V", r, w, lambda q: q.tensor_tensor_scan(out, a, b, init, o0, o1))
+    def scan(out, a, b, init, o0, o1, **kw):
+        return op("V", [a, b, init], [out], lambda q: q.tensor_tensor_scan(ap(out), ap(a), ap(b), ap(init), o0, o1), **kw)
 
-    def total(r, w, out, src, at, n, init=0.0):
-        scan(r, w, out, src[:, at:at + n // 2], src[:, at + n // 2:at + n], init, A.add, A.add)
+    def total(out, src, a, n, init):
+        return scan(out, v(src, a, a + n // 2), v(src, a + n // 2, a + n), init, A.add, A.add)
 
-    def fill(r, w, out, c):
-        op("V", r, w, lambda q: q.memset(out, c))
+    def fill(out, c, **kw):
+        return op("V", [], [out], lambda q: q.memset(ap(out), c), **kw)
 
-    def act(r, w, out, a, f, **kw):
-        op("S", r, w, lambda q: q.activation(out, a, f, **kw))
+    def act(out, a, f, bias=0.0, scale=1.0, acc=None, **kw):
+        given = {k: x for k, x, usual in (("bias", bias, 0.0), ("scale", scale, 1.0), ("accum_out", acc, None)) if x != usual}
+        return op("S", [a, bias, scale], [out, acc] if acc else [out],
+                  lambda q: q.activation(ap(out), ap(a), f, **{k: ap(x) for k, x in given.items()}), more=20.0 if acc else 0.0, **kw)
 
-    def quant(n, r, w, q_, s_, a):
-        op("V", "@%d " % (n + 20) + r, w, lambda q: q.quantize_mx(q_, s_, a))
+    def quant(q_, s_, a, b, src, **kw):
+        cost = 12 + 0.22 * length(src)
+        return record("V", [src], [v(q_, a, b), v(s_, a, b)],
+                      lambda: g.vector.quantize_mx(ap(v(q_, a, b)), ap(v(s_, a, b)), ap(src)).then_inc(T.sem["V"], 1), cost, 0.0, "V", 1, **kw)
 
-    def mm(r, w, out, lq, ls, l0, rq, rs, r0, n):
-        op("P", "@%d " % (3 * n // 2) + r, w,
-           lambda q: q.matmul_mx(out, lq[:, l0:l0 + 128], ls[:, l0:l0 + 128], rq[:, r0:r0 + n], rs[:, r0:r0 + n], True, True))
+    def mm(out, lq, ls, l0, rq, rs, r0, n):
+        sides = [v(lq, l0, l0 + 128), v(ls, l0, l0 + 128), v(rq, r0, r0 + n), v(rs, r0, r0 + n)]
+        return record("P", sides, [out], lambda: g.tensor.matmul_mx(ap(out), *[ap(x) for x in sides], True, True).then_inc(T.sem["P"], 1),
+                      0.6 * (n + 16), 0.0, "P", 1)
 
-    def table(n, w, out, pat, base):
-        op("G", "@%d" % (150 + 2 * n), w + " gq", lambda q: q.iota(out, pat, base, 0, allow_small_or_imprecise_dtypes=True))
+    def table(out, pat, base, cm=0, after=()):
+        if SCRATCH[out[0]][2] == I32:
+            return op("G", [], [out], lambda q: q.iota(ap(out), pat, base, cm), 2.0, 130.0, after=after)
+        return op("G", [], [out], lambda q: q.iota(ap(out), pat, base, cm, allow_small_or_imprecise_dtypes=True), 2.0, 130.0, after=after)
 
-    def bank(b, n):
-        return T.pw[:, 512 * b:512 * b + n]
+    def select(out, a, pat, x, cm=0):
+        return op("G", [a], [out], lambda q: q.affine_select(ap(out), ap(a), pat, A.not_equal, x, 0, cm), 2.0, 170.0)
 
-    def names(fmt, rows):
-        return " ".join(fmt % i for i in rows)
+    def bank(b, a, n):
+        return v("pw", 512 * b + a, 512 * b + n)
 
-    def pick(e, r, w, out, win):
-        if e == "V":
-            cp(r, w, out, win)
-        else:
-            act(r, w, out, win, F.Copy)
+    def pick(e, out, win, **kw):
+        return cp(out, win, **kw) if e == "V" else act(out, win, F.Copy, **kw)
+
+    def half(x, h, parts=2):
+        n = len(span(x)) // parts
+        return (x[0], x[1] + h * n * x[3], x[1] + (h * n + n - 1) * x[3] + 1, x[3], None)
 
     BIG = 2.0 ** 30
-    XS = "Xh Xm0 Xm1 Xm2 Xm3"
-    T1 = "t1a t1b t1c"
-    dma("S", "ldx", "", XS, T.X[:], T.x[:])
-    dma("Y", "ldu", "", "ub", T.ub[:], T.u[:])
-    dma("Y", "ldn", "", "nbi", T.nbi[:], T.nb[:])
-    dma("Y", "ldw", "ub Xh", "qw", T.qw[:].bitcast(dt.uint8), T.wc[:])
-    dma("Y", "lds", "ub Xh", "sw", T.sw[:], T.ws[:])
-    dma("Y", "ldv", "qw", "vb", T.vb[:], T.v[:])
-    op("G", "@180", "di0", lambda q: q.iota(T.di[:, 0:16], [[1, 16]], 128, -1))
-    op("G", "@180", "di2", lambda q: q.iota(T.di[:, 32:48], [[0, 16]], 0, 1))
-    op("G", "@180", "ln", lambda q: q.iota(T.ln[:], [[16, 16]], 16, 0, allow_small_or_imprecise_dtypes=True))
-    op("G", "@180", "di1 gq", lambda q: q.iota(T.di[:, 16:32], [[4, 16]], 131, -1))
-    table(C, "i1", T.i1[:], [[1, C]], 1)
-    table(C, "i0", T.i0[:], [[1, C]], 0)
-    table(C, "t1a", T.t1[:, 1:C], [[256, C - 1]], 256)
-    op("G", "@4250 di0 di2 ln", "eb gq", lambda q: q.iota(T.eb[:], [[0, 2048]], 0, 0, allow_small_or_imprecise_dtypes=True))
-    op("G", "@4300 eb", "eb gq", lambda q: q.affine_select(T.eb[:], T.eb[:], [[1, 4], [-1, 512]], A.not_equal, 0.5, 0, 4))
-    table(768, "r3f", T.r3f[:], [[512, C], [0, 3]], 2 ** 24 - 1)
-    op("G", "@1750 r3f", "r3f", lambda q: q.affine_select(T.r3f[:], T.r3f[:], [[0, C], [1, 3]], A.is_equal, 1.0, 0, 0))
-    fill("@384", "r3", T.r3[:], 1.0)
-    fill("@128", "r3", T.r3[:, 0:768:3], 2.0 ** 25)
-    fill("", "at15", T.at[:, 15:16], 0.0)
-    fill("@128", "t1b", T.t1[:, C:2 * C], 2.0 ** 17)
-    fill("", "t1c", T.t1[:, 0:1], 1.0)
-    fill("@128", "TTz", T.TT[:, 256:512], 0.0)
-    ts("di0", "dj0", T.dj[:, 0:16], T.di[:, 0:16], 15, A.bitwise_and)
-    ts("di2", "dj2", T.dj[:, 32:48], T.di[:, 32:48], 15, A.bitwise_and)
-    ts("dj0", "cc0", T.cc[:, 0:16], T.dj[:, 0:16], 0.0, A.is_equal)
-    cp("dj2", "oa", T.oa[:], T.dj[:, 32:48])
-    ts("di1", "dj1", T.dj[:, 16:32], T.di[:, 16:32], 2, A.arith_shift_right, 3, A.bitwise_and)
-    ts("ln", "ou", T.ou[:], T.ln[:, 0:8], -16.0, A.add)
-    ts("dj0 dj1", "cc1", T.cc[:, 16:48], T.dj[:, 0:32], 0.0, A.not_equal)
-    ts("di2", "dj3", T.dj[:, 48:49], T.di[:, 32:33], 3, A.bitwise_and)
-    act("@g256 cc0 oa", "mk", T.mk[:], T.cc[:, 0:16].indirect(T.oa[:]), F.Copy)
-    act("@g256 cc1 oa", "nm", T.nm[:], T.cc[:, 16:32].indirect(T.oa[:]), F.Copy)
-    ts("dj0 dj1", "kk", T.kk[:], T.dj[:, 0:32], 1.0, A.is_equal, BIG, A.mult)
-    ts("dj0", "cr0", T.cr[:, 0:1], T.dj[:, 15:16], 0.0, A.is_equal, 1 / BIG, A.max)
-    ts("dj1", "cr1", T.cr[:, 1:2], T.dj[:, 19:20], 0.0, A.is_equal, 1 / BIG, A.max)
-    tt("kk cc1", "cc2", T.cc[:, 48:80], T.kk[:], T.cc[:, 16:48], A.max)
-    ts("dj0", "cr7", T.cr[:, 7:8], T.dj[:, 15:16], 0.0, A.not_equal, BIG, A.mult)
-    ts("dj3", "cr3", T.cr[:, 3:4], T.dj[:, 48:49], -4.0, A.add)
-    ts("dj2", "cr4", T.cr[:, 4:5], T.dj[:, 32:33], -16.0, A.add)
-    ts("cr1", "cr2", T.cr[:, 2:3], T.cr[:, 1:2], 4.0, A.mult)
-    ts("cr7", "cr5", T.cr[:, 5:6], T.cr[:, 7:8], 1.0, A.max)
-    ts("cr7", "cr6", T.cr[:, 6:7], T.cr[:, 7:8], 1.0, A.max, -1.0, A.mult)
-    ts("ln cr4", "pos", T.nlf[:, 64:80], T.ln[:], T.cr[:, 4:5], A.add)
-    act("@g256 cc2 oa", "c16", T.c16[:], T.cc[:, 48:64].indirect(T.oa[:]), F.Copy)
-    act("@g256 cc2 oa", "c4", T.c4[:], T.cc[:, 64:80].indirect(T.oa[:]), F.Copy)
-    act("@512 " + T1, "tp", T.tp[:], T.t1[:], F.Copy, scale=256.0)
-    quant(512, "eb +5000", "qe", T.qe[:], T.se[:], T.eb[:])
-    quant(128, "vb", "qv", T.qv[:], T.sv[:], T.vb[:])
-    cp("nbi", "nbu", T.nbu[:], T.nbi[:])
+    FAR, FARTHER = 2.0 ** 25, 2.0 ** 28
+    MID = 1.0 - 2.0 ** 23
+    SPOT = 258
+    lx = dma("S", "ldx", [], [v("X")], T.X[:], T.x[:])
+    lu = dma("Y", "ldu", [], [v("ub")], T.ub[:], T.u[:])
+    dma("Y", "ldn", [], [v("nbi")], T.nbi[:], T.nb[:])
+    lw = dma("Y", "ldw", [], [v("qw")], T.qw[:].bitcast(dt.uint8), T.wc[:], (lx, lu))
+    dma("Y", "lds", [], [v("sw")], T.sw[:], T.ws[:], (lx, lu))
+    dma("Y", "ldv", [], [v("vb")], T.vb[:], T.v[:], (lw,))
+    table(v("di", 0, 16), [[1, 16]], 128, -1)
+    table(v("di", 32, 48), [[0, 16]], 0, 1)
+    table(v("ln"), [[16, 16]], 16)
+    table(v("lb"), [[-16, 16]], C - 16)
+    table(v("di", 16, 32), [[4, 16]], 131, -1)
+    table(v("i1"), [[1, C]], 1)
+    table(v("i0"), [[1, C]], 0)
+    table(v("cap"), [[1, C]], 2 ** 24 - SPOT)
+    fill(v("one"), 1.0)
+    fill(v("eb"), 0.0)
+    for b in range(4):
+        select(v("eb", 513 * b, 512 * b + 512, 4), v("eb", 513 * b, 512 * b + 512, 4), [[-1, 128]], 0.5, 1)
+    for dd, w, values in (("d2", 4, (FARTHER, 0.0, 0.0)), ("d3", 4, (FARTHER, 0.0, 0.0)), ("d4", 3, (FARTHER, 0.0, MID))):
+        for k, x in enumerate(values):
+            select(v(dd, k, w * C, w), v("one"), [[0, C]], x)
+    fill(v("m4", 768, 784), MID)
+    fill(v("rs"), 0.0)
+    fill(v("rs", 0, 80, 5), FAR)
+    fill(col("at", 15), 0.0)
+    fill(v("t1", C, 2 * C), FAR)
+    fill(v("TT", 256, 512), 0.0)
+    act(v("t1", 0, C), v("i0"), F.Copy, scale=65536.0)
+    ts(v("dj", 0, 16), v("di", 0, 16), 15, A.bitwise_and)
+    ts(v("dj", 32, 48), v("di", 32, 48), 15, A.bitwise_and)
+    ts(v("cc", 0, 16), v("dj", 0, 16), 0.0, A.is_equal)
+    cp(v("oa"), v("dj", 32, 48))
+    ts(v("dj", 16, 32), v("di", 16, 32), 2, A.arith_shift_right, 3, A.bitwise_and)
+    ts(v("ou"), v("ln", 0, 8), -16.0, A.add)
+    ts(v("cc", 16, 48), v("dj", 0, 32), 0.0, A.not_equal)
+    ts(col("dj", 48), col("di", 32), 3, A.bitwise_and)
+    act(v("mk"), at(v("cc", 0, 16), v("oa")), F.Copy)
+    act(v("nm"), at(v("cc", 16, 32), v("oa")), F.Copy)
+    ts(v("kk"), v("dj", 0, 32), 1.0, A.is_equal, BIG, A.mult)
+    ts(col("cr", 0), col("dj", 15), 0.0, A.is_equal, 1 / BIG, A.max)
+    ts(col("cr", 1), col("dj", 19), 0.0, A.is_equal, 1 / BIG, A.max)
+    tt(v("cc", 48, 80), v("kk"), v("cc", 16, 48), A.max)
+    ts(col("cr", 3), col("dj", 48), -4.0, A.add)
+    ts(col("cr", 4), col("dj", 32), -16.0, A.add)
+    ts(col("cr", 2), col("cr", 1), 4.0, A.mult)
+    ts(col("cr", 5), col("cr", 0), 3.0, A.mult)
+    ts(col("cr", 6), col("cr", 0), 4.0, A.mult)
+    ts(v("nlf", 4, 80, 5), v("ln"), col("cr", 4), A.add)
+    act(v("c16"), at(v("cc", 48, 64), v("oa")), F.Copy)
+    act(v("c4"), at(v("cc", 64, 80), v("oa")), F.Copy)
+    for b in range(4):
+        quant("qe", "se", 128 * b, 128 * b + 128, half(v("eb"), b, 4))
+    quant("qv", "sv", 0, 128, v("vb"))
+    cp(v("nbu"), v("nbi"))
     for p in range(4):
-        pick("VSSS"[p], "@g256 i1 nbu", "NR%d" % p, T.NR[:, 256 * p:256 * p + 256], T.i1[:].indirect(T.nbu[:, 16 * p:16 * p + 16]))
-    quant(128, "ub", "qu", T.qu[:], T.su[:], T.ub[:])
-    act("@g128 qu ou", "sur", T.sur[:], T.su[:].indirect(T.ou[:]), F.Copy)
-    op("V", "@g128 qu ou", "qur", lambda q: q.tensor_copy(T.qur[:].bitcast(dt.uint32), T.qu[:].bitcast(dt.uint32).indirect(T.ou[:])))
-    quant(C, XS, "qxh qxo qxm", T.qx[:], T.sx[:], T.X[:])
-    quant(128, XS, "lq", T.lq[:, 0:128], T.ls[:, 0:128], T.X[:, 0:512])
+        pick("VSSS"[p], half(v("NR"), p, 4), at(v("i1"), half(v("nbu"), p, 4)))
+    quant("qu", "su", 0, 128, v("ub"))
+    act(v("sur"), at(v("su"), v("ou")), F.Copy)
+    op("V", [at(v("qu"), v("ou"))], [v("qur")], lambda q: q.tensor_copy(ap(v("qur"), dt.uint32), ap(at(v("qu"), v("ou")), dt.uint32)))
+    quant("qx", "sx", 0, C, v("X"))
+    quant("lq", "ls", 0, 128, v("X", 0, 512))
 
     def names_to_lists():
         for e in range(4):
-            scan("@128 c16 NR0 NR1 NR2 NR3", "NC%d" % e, T.NC[:, C * e:C * e + C], T.c16[:], T.NR[:, e:1024:4], 0.0, A.mult, A.max)
-        ts("NC0 NC1 NC2 NC3 cr0", "nlf", T.nlf[:, 0:64], T.NC[:, 15:1024:16], T.cr[:, 0:1], A.mult, -1.0, A.add)
-        ts("NC0 NC1 NC2 NC3 cr0", "nl", T.nl[:], T.NC[:, 15:1024:16], T.cr[:, 0:1], A.mult, -1.0, A.add)
+            scan(half(v("NC"), e, 4), v("c16"), v("NR", e, 1024, 4), 0.0, A.mult, A.max)
+            ts(v("nlf", e, 80, 5), v("NC", C * e + 15, C * e + C, 16), col("cr", 0), A.mult, -1.0, A.add)
+        ts(v("nl"), v("NC", 15, 1024, 16), col("cr", 0), A.mult, -1.0, A.add)
+        ts(v("nl4"), v("NC", 15, 1024, 16), col("cr", 6), A.mult, -1.0, A.add)
 
-    def own(i):
-        return T.H[:, 16 * i + 15:16 * i + 16]
+    def own(i, src="H"):
+        return col(src, 16 * i + 15)
 
-    def s_rows(rows, src, name, c0, hs):
+    def carried(lo, hi, c0):
+        return v("sg", SG * lo + 15 + c0, SG * (hi - 1) + 16 + c0, SG)
+
+    def s_rows(rows, src, c0, out):
+        lo, hi = rows[0], rows[-1] + 1
         for i in rows:
-            a, b = C * i, 16 * i + 16
-            act("@%d %s %s +%d" % (C - c0, name, hs, 3000 if c0 else 0), "sg%d sh%d sj%d" % (i, i, i) + (" si%d" % i if c0 == 0 else ""),
-                T.sg[:, a + c0:a + C], src[:, 0:C - c0], F.Sign, bias=own(i), scale=-1.0)
+            a, b = SG * i + 16, 16 * i + 16
+            act(v("sg", a + c0, a + C), v(src, 0, C - c0), F.Sign, bias=own(i), scale=-1.0)
             if i < 15:
-                act("@%d sg%d" % (max(64, C - b) + 24, i), "sh%d at%d" % (i, i), T.sg[:, a + b:a + C], T.sg[:, a + b:a + C], F.Relu, scale=-1.0,
-                    accum_out=T.at[:, i:i + 1])
-            act("@%d sg%d" % (max(64, b - c0) + 24, i), "sj%d ag%d" % (i, i), T.sg[:, a + c0:a + b], T.sg[:, a + c0:a + b], F.Relu,
-                accum_out=T.ag[:, i:i + 1])
+                act(v("sg", a + b, a + C), v("sg", a + b, a + C), F.Relu, scale=-1.0, acc=col("at", i))
+        tt(v("e1", lo, hi), v("lb", lo, hi), v("co", 16 * lo + 15, 16 * hi, 16), A.add)
+        tt(carried(lo, hi, c0), v("e1", lo, hi), v("at", lo, hi), A.subtract)
+        for i in rows:
+            a, b = SG * i + 16, 16 * i + 16
+            act(v("sg", a + c0 - 1, a + b), v("sg", a + c0 - 1, a + b), F.Relu, acc=col(out, i))
 
-    def to_list(src, name, c0, n, tag, m):
-        tt("@%d %s mk" % (n, name), "ms" + tag, T.ms[:, c0:c0 + n], src[:, 0:n], T.mk[:, 0:n], A.mult)
-        op("V", "@%d %s" % (n, name), "mx%d" % m, lambda q: q.tensor_reduce(T.mx[:, m:m + 1], src[:, 0:n], AxisListType.X, A.max))
-        scan("@%d nm ms%s" % (n, tag), "H" + tag, T.H[:, c0:c0 + n], T.nm[:, 0:n], T.ms[:, c0:c0 + n], 0.0, A.mult, A.add)
-        tt("@%d H%s %s" % (n, tag, name), "eq" + tag, T.eq[:, c0:c0 + n], T.H[:, c0:c0 + n], src[:, 0:n], A.is_equal)
-        scan("@%d nm eq%s" % (n // 2, tag), "co" + tag, T.co[:, c0:c0 + n], T.nm[:, 0:n], T.eq[:, c0:c0 + n], 0.0, A.mult, A.add)
+    def v_row(i, src, c0, n, to, a, out, init):
+        b = min(16 * i + 16 - c0, n)
+        ts(v(to, a, a + b), v(src, 0, b), own(i), A.is_lt)
+        if b < n:
+            ts(v(to, a + b, a + n), v(src, b, n), own(i), A.is_le)
+        total(out, to, a, n, init)
+
+    def to_list(src, c0, n):
+        tt(v("ms", c0, c0 + n), v(src, 0, n), v("mk", 0, n), A.mult)
+        scan(v("H", c0, c0 + n), v("nm", 0, n), v("ms", c0, c0 + n), 0.0, A.mult, A.add)
+        tt(v("eq", c0, c0 + n), v("H", c0, c0 + n), v(src, 0, n), A.is_equal)
+        scan(v("co", c0, c0 + n), v("nm", 0, n), v("eq", c0, c0 + n), 0.0, A.mult, A.add)
+
+    def start_of(src, src2, c0, n, most, rest):
+        scan(v("mx", c0, c0 + n), v(src, 0, n), v("one", 0, n), most, A.max, A.mult)
+        act(v("nf", c0, c0 + n), v(src2, 0, n), F.Sign, bias=col("mx", c0 + n - 1), scale=-1.0)
+        scan(v("cs", c0, c0 + n), v("one", 0, n), v("nf", c0, c0 + n, -1), rest, A.add, A.mult)
 
     def early():
-        mm("qur sur qxo qxm", "pa", T.pa[:, 0:M], T.qur, T.sur, 0, T.qx, T.sx, K, M)
-        mm("qur sur qxo qxm", "pb", T.pb[:, 0:M], T.qur, T.sur, 0, T.qx, T.sx, K, M)
-        to_list(T.pa, "pa", K, M, "m", 0)
+        mm(v("pa", 0, M), "qur", "sur", 0, "qx", "sx", K, M)
+        mm(v("pb", 0, M), "qur", "sur", 0, "qx", "sx", K, M)
+        to_list("pa", K, M)
+        start_of("pa", "pb", K, M, -BIG ** 3, 0.0)
         lo, h = 4 + NE, M // 2
-        s_rows(range(lo, 16), T.pb, "pb", K, "Hm")
+        s_rows(range(lo, 16), "pb", K, "rb")
         for i in range(4, lo):
-            a, b = M * (i - 4), 16 * i + 16 - K
-            ts("@%d pa Hm" % b, "ce%d" % i, T.ce[:, a:a + b], T.pa[:, 0:b], own(i), A.is_ge)
-            ts("@%d pa Hm" % (M - b), "cf%d" % i, T.ce[:, a + b:a + M], T.pa[:, b:M], own(i), A.is_gt)
-            total("ce%d cf%d" % (i, i), "ceo%d" % i, T.ceo[:, h * (i - 4):h * (i - 3)], T.ce, a, M, float(K))
+            v_row(i, "pa", K, M, "ce", M * (i - 4), v("ceo", h * (i - 4), h * (i - 3)), own(i, "co"))
+        if NL < NE:
+            cp(carried(4 + NL, lo, 0), v("ceo", h * NL + h - 1, h * NE, h))
+        lo = max(lo, 4 + NL)
+        cp(carried(lo, 16, 0), v("rb", lo, 16))
 
     def late(t):
-        nv, n0, lo = (NV, C, NV) if t == 0 else (4, K, 4 + NE)
-        h = M // 2
-        com = "coh" if t == 0 else "com"
-        mm("qur sur qxh qxo qxm", "pc", T.pc[:, 0:C], T.qur, T.sur, 0, T.qx, T.sx, 0, C)
-        mm("qur sur qxh qxo qxm", "pd", T.pd[:, 0:C], T.qur, T.sur, 0, T.qx, T.sx, 0, C)
-        to_list(T.pc, "pc", 0, n0, "h", 1 if t else 2)
-        if t:
-            tt("mx0 mx1", "mx2", T.mx[:, 2:3], T.mx[:, 0:1], T.mx[:, 1:2], A.max)
-            for i in range(4, 16):
-                act("pd Hm", "si%d" % i, T.sg[:, C * i:C * i + K], T.pd[:, 0:K], F.Sign, bias=own(i), scale=-1.0)
-                act("@88 si%d" % i, "si%d al%d" % (i, i), T.sg[:, C * i:C * i + K], T.sg[:, C * i:C * i + K], F.Relu, accum_out=T.al[:, i:i + 1])
-        act("@256 pd mx2", "nf", T.nf[:], T.pd[:, 0:C], F.Sign, bias=T.mx[:, 2:3], scale=-1.0)
-        if t == 0:
-            s_rows(range(nv, 16), T.pd, "pd", 0, "Hh")
-        srows = range(lo, 16)
-        scan("@128 nf", "p1", T.p1[:], T.nf[:], T.nf[:], 1.0, A.mult, A.mult)
-        total("p1", "p2", T.p2[:], T.p1, 0, C)
-        ts("@80 nlf pos p2", "nn", T.nn[:], T.nlf[:], T.p2[:, 127:128], A.not_equal, 256.0, A.mult)
-        tt("nn", "n2a", T.n2[:, 0:32], T.nn[:, 0:32], T.nn[:, 32:64], A.min)
-        tt("n2a", "n2b", T.n2[:, 32:48], T.n2[:, 0:16], T.n2[:, 16:32], A.min)
-        tt("n2b nn", "n2c", T.n2[:, 48:64], T.n2[:, 32:48], T.nn[:, 64:80], A.min)
-        ts("@128 i0 p2", "rt", T.rt[:], T.i0[:], T.p2[:, 127:128], A.not_equal, 2.0 ** 25, A.mult)
+        nv, n0, h = (NV, C, 0) if t == 0 else (4, K, M // 2)
+        mm(v("pc", 0, C), "qur", "sur", 0, "qx", "sx", 0, C)
+        mm(v("pd", 0, C), "qur", "sur", 0, "qx", "sx", 0, C)
+        to_list("pc", 0, n0)
+        start_of("pc", "pd", 0, n0, col("mx", C - 1) if t else -BIG ** 3, col("cs", C - 1) if t else 0.0)
+        start = col("cs", n0 - 1)
+        ts(v("nn"), v("nlf"), start, A.not_equal, 256.0, A.mult)
+        scan(v("n2"), v("rs"), v("nn"), 0.0, A.max, A.min)
+        ts(v("g2", 3, 1024, 4), v("i0"), start, A.not_equal, FAR, A.mult)
+        tt(v("ci", 0, nv), v("co", 15, 16 * nv, 16), v("n2", 4, 5 * nv, 5), A.subtract)
         for i in range(nv):
-            a, b = C * i, 16 * i + 16
-            ts("@%d pc Hh" % b, "cb%d" % i, T.cb[:, a:a + b], T.pc[:, 0:b], own(i), A.is_ge)
-            ts("@%d pc Hh" % (C - b), "cd%d" % i, T.cb[:, a + b:a + C], T.pc[:, b:C], own(i), A.is_gt)
-            total("cb%d cd%d" % (i, i), "cbo%d" % i, T.cbo[:, 128 * i:128 * i + 128], T.cb, a, C)
-        tt("ln " + com, "e2", T.e2[:, lo:16], T.ln[:, lo:16], T.co[:, 16 * lo + 15:C:16], A.subtract)
-        tt(names("cbo%d", range(nv)) + " coh", "byb", T.by[:, 0:nv], T.cbo[:, 127:128 * nv:128], T.co[:, 15:16 * nv:16], A.subtract)
-        tt("e2 " + names("at%d", srows), "e1", T.e1[:, lo:16], T.e2[:, lo:16], T.at[:, lo:16], A.add)
-        if t:
-            tt(names("ceo%d", range(4, lo)) + " com", "eev", T.ee[:, 4:lo], T.ceo[:, h - 1:h * (lo - 4):h], T.co[:, K + 15:16 * lo:16], A.subtract)
-            tt("e1 " + names("ag%d", srows), "ees", T.ee[:, lo:16], T.e1[:, lo:16], T.ag[:, lo:16], A.subtract)
-            tt("eev ees " + names("al%d", range(4, 16)), "bya", T.by[:, 4:16], T.ee[:, 4:16], T.al[:, 4:16], A.subtract)
+            v_row(i, "pc", 0, C, "cb", C * i, v("cbo", 128 * i, 128 * i + 128), col("ci", i))
+        if t == 0:
+            s_rows(range(nv, 16), "pd", 0, "ab")
         else:
-            tt("e1 " + names("ag%d", srows), "bya", T.by[:, lo:16], T.e1[:, lo:16], T.ag[:, lo:16], A.subtract)
-        tt("bya byb n2c", "byc", T.by[:, 16:32], T.by[:, 0:16], T.n2[:, 48:64], A.add)
-        cp("bya byb byc", "byu", T.byu[:], T.by[:])
-        ts("bya byb cr5", "bys", T.bys[:], T.by[:, 0:16], T.cr[:, 5:6], A.mult)
-        cp("bya byb", "byh", T.byh[:], T.by[:, 0:16])
+            for lo, hi, known_ in ((4, 4 + min(NE, NL), v("ceo", h - 1, h * min(NE, NL), h)), (4 + NE, 4 + NL, v("rb", 4 + NE, 4 + NL))):
+                if lo < hi:
+                    tt(v("ci", lo, hi), known_, v("n2", 5 * lo + 4, 5 * hi, 5), A.subtract)
+            nv = 4 + NL
+            for i in range(4, nv):
+                v_row(i, "pc", 0, K, "cb", C * i, v("cbo", 128 * i + 96, 128 * i + 128), col("ci", i))
+            for i in range(nv, 16):
+                a = SG * i + 16
+                act(v("sg", a, a + K), v("pd", 0, K), F.Sign, bias=own(i), scale=-1.0)
+                act(v("sg", a - 1, a + K), v("sg", a - 1, a + K), F.Relu, acc=col("ab", i))
+        ts(v("bcu", 0, nv), v("cbo", 127, 128 * nv, 128), -1.0, A.mult, float(C), A.add)
+        tt(v("bc", 0, nv), v("cbo", 127, 128 * nv, 128), v("n2", 4, 5 * nv, 5), A.add)
+        ts(v("byu", 0, nv), v("bc", 0, nv), -1.0, A.mult, float(C), A.add)
+        tt(v("bc", nv, 16), v("n2", 5 * nv + 4, 80, 5), v("ab", nv, 16), A.subtract)
+        ts(v("bcu", nv, 16), v("bc", nv, 16), float(C), A.add)
+        ts(v("byu", nv, 16), v("ab", nv, 16), -1.0, A.mult, float(C), A.add)
         for p in (1, 0):
-            pick("VS"[p], "@g128 byu " + T1, "q1%d" % p, T.q1[:, 128 * p:128 * p + 128], T.t1[:].indirect(T.byu[:, 16 + 8 * p:24 + 8 * p]))
+            pick("VS"[p], half(v("q1"), p), at(v("t1"), half(v("bcu"), p)))
 
-    def least(tab, name, gg, mo, tmp, rst, rname, cyc):
+    def step(tab, lists, gg, dd, mo, w, tmp, most, shift=0.0):
         for h in range(2):
-            a, b, o, r = 384 * h, 384 * h + 384, 8 * h, "@g128 nl " + name
-            act(r, "g1%d" % h, gg[:, a + 1:b:3], tab[:].indirect(T.nl[:, 32 + o:40 + o]), F.Copy)
-            act(r, "g2%d" % h, gg[:, a + 2:b:3], tab[:].indirect(T.nl[:, 48 + o:56 + o]), F.Copy)
-            tt(r + " rt", "tmp%d" % h, tmp[:, 128 * h:128 * h + 128], tab[:].indirect(T.nl[:, o:o + 8]), T.rt[:, 128 * h:128 * h + 128], A.min)
-            tt(r + " tmp%d" % h, "g0%d" % h, gg[:, a:b:3], tab[:].indirect(T.nl[:, 16 + o:24 + o]), tmp[:, 128 * h:128 * h + 128], A.min)
-            scan("@%d g0%d g1%d g2%d %s" % (cyc, h, h, h, rname), "mo%d" % h, mo[:, a:b], rst[:, a:b], gg[:, a:b], 0.0, A.max, A.min)
-
-    def plus(out, name, tab, tname, mo):
-        for h in range(2):
-            tt("@g128 byu mo%d %s" % (h, tname), name + str(h), out[:, 128 * h:128 * h + 128], tab[:].indirect(T.byu[:, 8 * h:8 * h + 8]),
-               mo[:, 384 * h + 2:384 * h + 384:3], A.add)
-
-    def keys(mo, conv, cyc):
-        for h in range(2):
-            scan("@%d mo%d c16" % (cyc, h), "conv%d" % h, conv[:, 128 * h:128 * h + 128], T.c16[:, 0:128], mo[:, 384 * h + 2:384 * h + 384:3],
-                 0.0, A.mult, A.max)
-        plus(T.kr, "kr", T.i0, "i0", mo)
-        tt("conv0 conv1 bys", "kl", T.kl[:], conv[:, 15:C:16], T.bys[:], A.add)
-
-    def ranking(nb, narrow, out, name, c0, c1, c2):
-        ns = 16 - nb
-        for i in range(ns):
-            act("@280 kr0 kr1 kl cr6", "sg%d sh%d si%d sj%d ab%d" % (i, i, i, i, i), T.sg[:, C * i:C * i + C], T.kr[:], F.Sign,
-                bias=T.kl[:, i:i + 1], scale=T.cr[:, 6:7], accum_out=T.ab[:, i:i + 1])
-        if narrow:
-            ts("conv0 conv1 cr0", "mj", T.mj[:], T.vb2[:, 15:C:16], T.cr[:, 0:1], A.mult)
-            for h in range(2):
-                cp("@128 kr%d" % h, "ku%d" % h, T.ku[:, 128 * h:128 * h + 128], T.kr[:, 128 * h:128 * h + 128])
-        for i in range(ns, 16):
-            if narrow:
-                ts("@128 ku0 ku1 mj byh", "cb%d cd%d" % (i, i), T.cb[:, C * i:C * i + C], T.ku[:], T.mj[:, i:i + 1], A.subtract, T.byh[:, i:i + 1], A.is_lt)
+            a, b = 128 * w * h, 128 * w * (h + 1)
+            e = [at(tab, v(lists, 16 * k + 8 * h, 16 * k + 8 * h + 8)) for k in range(4)]
+            act(v(gg, a + 1, b, w), e[2], F.Copy)
+            act(v(gg, a + 2, b, w), e[3], F.Identity, bias=shift)
+            if most:
+                tt(half(v(tmp), h), e[0], half(v(most), h), A.min)
             else:
-                ts("@256 kr0 kr1 kl cr5", "cb%d cd%d" % (i, i), T.cb[:, C * i:C * i + C], T.kr[:], T.cr[:, 5:6], A.mult, T.kl[:, i:i + 1], A.is_gt)
-            total("cb%d" % i, "cbo%d" % i, T.cbo[:, 128 * i:128 * i + 128], T.cb, C * i, C)
-        ts(names("cbo%d", range(ns, 16)) + " un0", name + "a", out[:, ns:16], T.cbo[:, 128 * ns + 127:2048:128], c0, A.add)
-        ts(names("ab%d", range(ns)) + " un1", name + "b", out[:, 0:ns], T.ab[:, 0:ns], c1, A.mult, c2, A.add)
+                pick(TMP[h], half(v(tmp), h), e[0])
+            tt(v(gg, a, b, w), e[1], half(v(tmp), h), A.min)
+            scan(v(mo, a, b), v(dd, a, b), v(gg, a, b), 0.0, A.add, A.min)
 
     def order():
         for b in range(4):
-            mm("qe qxh qxo qxm", "pw%d" % b, bank(b, C), T.qe, T.se, 128 * b, T.qx, T.sx, 0, C)
-            act("@256 pw%d +1500" % b, "DX%d" % b, T.DX[:, b:1024:4], bank(b, C), F.Copy)
-        least(T.q1, "q10 q11", T.gb, T.mb, T.tb, T.r3, "r3", 192)
-        act("@280 mo0 mo1", "nr un0", T.nr[:], T.mb[:, 2:768:3], F.Relu, bias=-1.0, scale=2.0 ** -16, accum_out=T.un[:, 0:1])
-        act("un0", "un1", T.un[:, 1:2], T.un[:, 0:1], F.Identity, bias=127.5)
-        keys(T.mb, T.vb2, 64)
-        ranking(NB[0], True, T.pl, "pl", T.un[:, 0:1], 0.5, T.un[:, 1:2])
-        for p in (0, 1):
-            pick("SV"[p], "@g128 tp pla plb", "pp%d" % p, T.pp[:, 128 * p:128 * p + 128], T.tp[:].indirect(T.pl[:, 8 * p:8 * p + 8]))
-        least(T.pp, "pp0 pp1", T.gb, T.mb, T.tb, T.r3, "r3", 192)
-        plus(T.k3, "k3", T.t1, T1, T.mb)
-        least(T.k3, "k30 k31", T.gf, T.mf, T.tf, T.r3f, "r3f", 384)
-        keys(T.mf, T.vf, 128)
-        ranking(NB[1], False, T.npl, "npl", 0.0, -0.5, 127.5)
+            mm(bank(b, 0, C), "qe", "se", 128 * b, "qx", "sx", 0, C)
+            act(v("DX", b, 1024, 4), bank(b, 0, C), F.Copy)
+        act(v("d2", 3, 1024, 4), at(v("i0"), v("byu")), F.Copy, scale=256.0)
+        act(v("d3", 3, 1024, 4), at(v("i0"), v("byu")), F.Copy)
+        for p in range(4):
+            cp(at(v("cr2"), half(v("byu"), p, 4)), half(v("i1"), p, 4))
+        scan(v("cl", 1, C), v("c16", 1, C), v("cr2", 1, C), float(SPOT), A.mult, A.max)
+        ts(v("rl"), v("cl", 15, C, 16), col("cr", 5), A.mult, -1.0, A.add)
+        step(v("q1"), "nl", "g2", "d2", "m2", 4, "tf", None)
+        step(v("m2"), "nl4", "g2", "d3", "m3", 4, "tf", None)
+        step(v("m3"), "nl4", "g4", "d4", "m4", 3, "tf", "cap", MID)
+        for h in range(2):
+            tt(half(v("mb"), h), at(v("m4"), half(v("rl"), h)), half(v("mk"), h), A.mult)
+            scan(half(v("Hb"), h), half(v("nm"), h), half(v("mb"), h), 0.0, A.mult, A.add)
+        act(v("W", 0, C), at(v("m4"), v("rl")), F.Identity, bias=0.5)
+        act(v("W", C, 2 * C), at(v("m4"), v("rl")), F.Identity, bias=-0.5)
+        tt(v("eqb"), at(v("m4"), v("rl")), v("Hb"), A.is_equal)
+        scan(v("cob"), v("nm"), v("eqb"), 0.0, A.mult, A.add)
+        ns = 16 - NB
+        for i in range(ns):
+            act(v("sg", SG * i, SG * i + C), v("W", 16 * i + 16, 16 * i + 16 + C), F.Sign, bias=own(i, "Hb"), scale=-1.0, acc=col("ac", i))
+        for i in range(ns, 16):
+            ts(v("cb", C * i, C * i + C), v("W", 16 * i + 16, 16 * i + 16 + C), own(i, "Hb"), A.is_gt)
+            total(v("cbo", 128 * i, 128 * i + 128), "cb", C * i, C, own(i, "cob"))
+        ts(v("npl", ns, 16), v("cbo", 128 * ns + 127, 2048, 128), -1.0, A.add)
+        ts(v("e2", 0, ns), v("cob", 15, 16 * ns, 16), 2.0, A.mult, 254.0, A.add)
+        tt(v("e3", 0, ns), v("e2", 0, ns), v("ac", 0, ns), A.subtract)
+        ts(v("npl", 0, ns), v("e3", 0, ns), 0.5, A.mult)
 
     def move(t):
-        qt, st = T["qt%d" % t], T["st%d" % t]
-        dxs = "@g256 DX0 DX1 DX2 DX3 l4"
-        cut = 16 - NB[1] + NB[1] % 2
-        cp("@s%d i1 npla" % (C - 16 * cut), "lr", T.lr[:].indirect(T.npl[:, cut:16]), T.i1[:, 16 * cut:C])
-        cp("@s%d i1 npla nplb" % (16 * cut), "lr", T.lr[:].indirect(T.npl[:, 0:cut]), T.i1[:, 0:16 * cut])
-        scan("@128 c4 lr", "lc", T.lc[:], T.c4[:], T.lr[:], 0.0, A.mult, A.max)
-        ts("lc cr2 cr3", "l4", T.l4[:], T.lc[:, 3:C:4], T.cr[:, 2:3], A.mult, T.cr[:, 3:4], A.add)
-        if t < R - 1:
-            cp("@g256 l4 " + XS, "TT0 TT1", T.TT[:, 0:256], T.X[:].indirect(T.l4[:, 48:64]))
-        else:
-            for p in (1, 0):
-                pick("VS"[p], "@g128 l4 " + XS, "TT%d" % p, T.TT[:, 128 * p:128 * p + 128], T.X[:].indirect(T.l4[:, 48 + 8 * p:56 + 8 * p]))
-        quant(128, "TT0 TT1 TTz", "qt%d" % t, qt[:], st[:], T.TT[:])
-        at, arr = 128 + K * t, "arr%d" % t
+        qt, st = "qt%d" % t, "st%d" % t
+        cut = 16 - NB + NB % 2
+        cp(at(v("lr"), v("npl", cut, 16)), v("cr2", 16 * cut, C))
+        cp(at(v("lr"), v("npl", 0, cut)), v("cr2", 0, 16 * cut))
+        for a, b in ((M, C), (0, M)):
+            scan(v("lc", a, b), v("c4", a, b), v("lr", a, b), 0.0, A.mult, A.max)
+            ts(v("l4", a // 4, b // 4), v("lc", a + 3, b, 4), col("cr", 2), A.mult, col("cr", 3), A.add)
+        for p in (1, 0):
+            pick("VS"[p], v("TT", 128 * p, 128 * p + 128), at(v("X"), v("l4", 48 + 8 * p, 56 + 8 * p)))
+        quant(qt, st, 0, 128, v("TT"))
+        to, arr = 128 + K * t, "arr%d" % t
 
         def send():
-            g.remote_dma(T.lq[:, at:at + K].bitcast(dt.uint8), qt[:, 0:K].bitcast(dt.uint8), T.sem[arr], T.sem["sent"], pid, rid, topo.mask(core, nxt))
-            g.remote_dma(T.ls[:, at:at + K], st[:, 0:K], T.sem[arr], T.sem["sent"], pid, rid, topo.mask(core, nxt))
+            g.remote_dma(ap(v("lq", to, to + K), dt.uint8), ap(v(qt, 0, K), dt.uint8), T.sem[arr], T.sem["sent"], pid, rid, topo.mask(core, nxt))
+            g.remote_dma(ap(v("ls", to, to + K)), ap(v(st, 0, K)), T.sem[arr], T.sem["sent"], pid, rid, topo.mask(core, nxt))
             count["sent"] += 2 * n_out
 
-        record("G", "qt%d" % t, "land%d" % t, send, 500.0, TRAVEL, arr, 2 * n_in)
+        record("G", [v(qt, 0, K), v(st, 0, K)], [v("lq", to, to + K), v("ls", to, to + K)], send, 500.0, TRAVEL, arr, 2 * n_in)
         for p in range(3):
-            act(dxs, "EH%d" % p, T.EH[:, 256 * p:256 * p + 256], T.DX[:].indirect(T.l4[:, 16 * p:16 * p + 16]), F.Copy)
-            tt(dxs + " EH%d" % p, "Z%d" % (p + 1), T.Z[:, 256 * p + 256:256 * p + 512], T.DX[:].indirect(T.l4[:, 16 * p + 16:16 * p + 32]),
-               T.EH[:, 256 * p:256 * p + 256], A.add)
-        quant(M, "Z1 Z2 Z3", "qz", T.qz[:], T.sz[:], T.Z[:, 256:1024])
+            act(half(v("EH"), p, 3), at(v("DX"), half(v("l4"), p, 4)), F.Copy)
+            tt(half(v("Z"), p + 1, 4), at(v("DX"), half(v("l4"), p + 1, 4)), half(v("EH"), p, 3), A.add)
+        quant("qz", "sz", 0, M, v("Z", 256, 1024))
         for b in range(4):
-            mm("qw sw qz", "pw%d" % b, bank(b, M), T.qw, T.sw, 128 * b, T.qz, T.sz, 0, M)
+            mm(bank(b, 0, M), "qw", "sw", 128 * b, "qz", "sz", 0, M)
             if b % 2:
-                ts("@192 pw%d" % b, "Xm%d" % b, T.X[:, 4 * K + b:1024:4], bank(b, M), 0.0, A.max, 0.03125, A.mult)
+                ts(v("X", 4 * K + b, 1024, 4), bank(b, 0, M), 0.0, A.max, 0.03125, A.mult)
             else:
-                act("@192 pw%d" % b, "Xm%d" % b, T.X[:, 4 * K + b:1024:4], bank(b, M), F.Relu, scale=0.03125)
-        quant(M, "Xm0 Xm1 Xm2 Xm3", "qxo qxm", T.qx[:, K:C], T.sx[:, K:C], T.X[:, 4 * K:1024])
-        act("@g256 i1 npla nplb", "ir", T.ir[:], T.i1[:].indirect(T.npl[:]), F.Copy)
+                act(v("X", 4 * K + b, 1024, 4), bank(b, 0, M), F.Relu, scale=0.03125)
+        quant("qx", "sx", K, C, v("X", 4 * K, 1024))
+        act(v("iq"), at(v("i1"), v("npl")), F.Copy)
+        act(v("ir"), at(v("iq"), v("byu")), F.Copy)
         for e in range(4):
-            act("@g256 ir nl", "NA%d" % e, T.NA[:, e:1024:4], T.ir[:].indirect(T.nl[:, 16 * e:16 * e + 16]), F.Copy)
+            act(v("NA", e, 1024, 4), at(v("ir"), half(v("nl"), e, 4)), F.Copy)
         for p in range(4 if t < R - 1 else 0):
-            pick("VVSS"[p], "@g256 NA0 NA1 NA2 NA3 l4", "NR%d" % p, T.NR[:, 256 * p:256 * p + 256], T.NA[:].indirect(T.l4[:, 16 * p:16 * p + 16]))
+            pick("VSSS"[p], half(v("NR"), p, 4), at(v("NA"), half(v("l4"), p, 4)))
 
     def mix(t):
-        if t == R - 1:
-            to = [(n, T[n][:, 0:128], T[n][:, K:128]) for n in BANKS[4:]]
-        else:
-            to = [(BANKS[b], bank(b, 128), T.pw[:, 512 * b + K:512 * b + 128]) for b in range(4)]
         for b in range(4):
-            mm("qe lq land%d" % t, to[b][0], to[b][1], T.qe, T.se, 128 * b, T.lq, T.ls, K + K * t, 128)
-            tt(to[b][0] + " EH0", "Z0%d" % b, T.Z[:, b:256:4], to[b][2], T.EH[:, b:256:4], A.add)
-        quant(128, "Z00 Z01 Z02 Z03 Z1", "qh", T.qh[:], T.sh[:], T.Z[:, 0:512])
+            name, a = (("pa", "pb", "pc", "pd")[b], 0) if t == R - 1 else ("pw", 512 * b)
+            mm(v(name, a, a + 128), "qe", "se", 128 * b, "lq", "ls", K + K * t, 128)
+            tt(v("Z", b, 256, 4), v(name, a + K, a + 128), v("EH", b, 256, 4), A.add)
+        quant("qh", "sh", 0, 128, v("Z", 0, 512))
         for b in range(4):
-            mm("qw sw qh", "pw%d" % b, bank(b, 128), T.qw, T.sw, 128 * b, T.qh, T.sh, 0, 128)
-            ts("pw%d qt%d lq" % (b, t), "Xh%d" % b, T.X[:, b:4 * K:4], bank(b, K), 0.0, A.max, 0.03125, A.mult)
-        quant(128, "Xh0 Xh1 Xh2 Xh3 Xm0 Xm1 Xm2 Xm3", "qxh qxo Xh", T.qx[:, 0:128], T.sx[:, 0:128], T.X[:, 0:512])
+            mm(bank(b, 0, 128), "qw", "sw", 128 * b, "qh", "sh", 0, 128)
+            if b % 2:
+                ts(v("X", b, 4 * K, 4), bank(b, 0, K), 0.0, A.max, 0.03125, A.mult)
+            else:
+                act(v("X", b, 4 * K, 4), bank(b, 0, K), F.Relu, scale=0.03125)
+        quant("qx", "sx", 0, 128, v("X", 0, 512))
 
     for t in range(R):
         names_to_lists()
@@ -413,19 +505,19 @@ def rank_program(g, core, T, topo):
         order()
         move(t)
 
-    act("@g1024 NA0 NA1 NA2 NA3 l4", "ON", T.ON[:], T.NA[:].indirect(T.l4[:]), F.Identity, bias=-1.0)
-    dma("S", "out", "ON", "", T.on[:], T.ON[0:128:16, :])
+    act(v("ON"), at(v("NA"), v("l4")), F.Identity, bias=-1.0)
+    dma("S", "out", [v("ON")], [], T.on[:], T.ON[0:128:16, :])
+    mm(v("pw", 0, 128), "qv", "sv", 0, "qx", "sx", 128, 128)
+    dma("Y", "out", [v("qx", 128, C)], [], T.oc[:, 512:1024], ap(v("qx", 128, C), dt.uint8))
+    act(v("ys", 128, C), v("pw", 0, 128), F.Copy)
+    dma("S", "out", [v("ys", 128, C)], [], T.y[:, 128:C], T.ys[:, 128:C])
     mix(R - 1)
-    mm("qv qxm", "pa", T.pa[:, 0:128], T.qv, T.sv, 0, T.qx, T.sx, 128, 128)
-    dma("Y", "out", "qxm", "", T.oc[:, 512:1024], T.qx[:, 128:C].bitcast(dt.uint8))
-    act("@128 pa", "ym", T.ys[:, 128:C], T.pa[:, 0:128], F.Copy)
-    dma("S", "out", "ym", "", T.y[:, 128:C], T.ys[:, 128:C])
-    mm("qv qxh qxo", "pc", T.pc[:, 0:128], T.qv, T.sv, 0, T.qx, T.sx, 0, 128)
-    dma("Y", "out", "qxh qxo", "", T.oc[:, 0:512], T.qx[:, 0:128].bitcast(dt.uint8))
+    mm(v("pc", 0, 128), "qv", "sv", 0, "qx", "sx", 0, 128)
+    dma("Y", "out", [v("qx", 0, 128)], [], T.oc[:, 0:512], ap(v("qx", 0, 128), dt.uint8))
     for k in range(4):
-        dma("S" if k else "Y", "out", "qxh qxo qxm", "", T.osc[4 * k:4 * k + 4, :], T.sx[32 * k:32 * k + 4, :])
-    cp("@128 pc", "yh", T.ys[:, 0:128], T.pc[:, 0:128])
-    dma("Y", "out", "yh", "", T.y[:, 0:128], T.ys[:, 0:128])
+        dma("S" if k else "Y", "out", [v("sx")], [], T.osc[4 * k:4 * k + 4, :], T.sx[32 * k:32 * k + 4, :])
+    cp(v("ys", 0, 128), v("pc", 0, 128))
+    dma("Y", "out", [v("ys", 0, 128)], [], T.y[:, 0:128], T.ys[:, 0:128])
     issue()
     for s in SEMAPHORES:
         if count[s]:

@@ -3,30 +3,45 @@ from concourse.mybir import dt, AluOpType as A, ActivationFunctionType as F
 
 C, K, R = 256, 64, 3
 M = C - K
-NV = 10
+NV = 9
 NE = 5
-NL = 2
-NB = 7
-WAKE, TRAVEL = 200.0, 2800.0
+NB = 11
+NRP = 4
+TMP = ((("V", 0, 8), ("V", 8, 16)), (("V", 0, 8), ("S", 8, 16)), (("V", 0, 8), ("S", 8, 16)))
+TTE = "VS"
+RELU = ("SVSV", "SSSS", "SVSV")
+BATCHES = ((12, 16), (0, 8), (8, 12))
+ZCUT = ((16, 24), (24, 32), (32, 48), (0, 8), (8, 16))
+WAKE, TRAVEL = 240.0, 2800.0
+CYC = 0.83
+NODE_AT = ("i1", "na1", "na2", "na1")
+FROM = ("na1", "lr", "lr")
+SOFT = 0
+ROUNDS = 12000
+SEED = 0
+REACH = 20
+SAMPLE = 30
+EVEN = 60.0
+STALE = 800
+RELAY = 20
+PLAN = []
 BF, FP, U16, I32, Q4, U8 = "bfloat16", "float32", "uint16", "int32", "float8_e4m3fn_x4", "uint8"
-SG = 272
+PAD = 96
+SG = PAD + C
 SIZES = {
-    BF: "X 1024 ub 512 vb 512 eb 2048 TT 512 Z 1024 DX 1024 EH 768 kk 32 cc 80 mk 256 nm 256 c16 256 c4 256 i1 256 i0 256 t1 512 "
-        "NR 1024 NA 1024 NC 1024 eq 256 co 256 nf 256 cs 256 one 256 rt 256 ce 2304 ceo 1152 cb 4096 cbo 2048 sg 4352 q1 256 "
-        "d2 1024 d3 1024 tb 256 lr 256 lc 256 ir 256 iq 256 cr2 256 cl 256 eqb 256 cob 256 rs 80",
-    FP: "cr 10 ln 16 nlf 80 ON 1024 ms 256 H 256 mx 256 mh 64 nn 80 n2 80 at 16 ab 16 e1 16 e2 16 e3 16 ac 16 lb 16 ci 16 rb 16 bc 16 "
-        "d4 768 cap 256 g2 1024 g4 768 m2 1024 m3 1024 m4 784 tf 256 mb 256 Hb 256 W 512 ys 256",
-    U16: "nbu 64 oa 16 ou 8 nl 64 nl4 64 bcu 16 byu 16 rl 16 npl 16 l4 64",
+    BF: "X 1024 ub 512 vb 512 eb 2048 TT 512 Z 1024 DX 1024 EH 768 kk 32 cc 80 mk 256 nm 256 c16 256 c4 256 i1 256 t1 512 ci 16 "
+        "NR 1024 NA 1024 NC 1024 eq 256 co 256 nf 256 cs 256 sn 256 one 256 ce 2304 cb 4096 cbo 2048 sg 5632 byw 272 q1 256 "
+        "d2 1024 d3 1024 lr 256 lc 256 iq 256 nr 256 cl 256 kr 256 bn 256 eqb 256 cob 256 rs 96 p4 1040 pl 256 na1 256 na2 256 l16 256 s1 16",
+    FP: "cr 10 ln 16 nlf 96 ON 1024 ms 256 H 256 mx 256 nn 96 n2 96 at 16 ab 16 e1 16 e2 16 e3 16 ac 16 lb 16 bc 16 "
+        "d4 1024 g2 1024 g4 1024 m2 1024 m3 1024 m4 1040 tf 256 mb 256 Hb 256 W 512 ys 256",
+    U16: "nbu 64 oa 16 ou 8 nl 64 nl4 64 byu 16 bcu 16 rl 16 npl 16 l4 64 n4 64 pu 16 pqu 16 bnu 16 lu 16 cu 2",
     I32: "nbi 64 di 48 dj 64",
-    Q4: "qu 128 qur 128 qv 128 qw 512 qe 512 qx 256 qz 192 qh 128 qt0 128 qt1 128 qt2 128 lq 320",
-    U8: "su 128 sur 128 sv 128 sw 512 se 512 sx 256 sz 192 sh 128 st0 128 st1 128 st2 128 ls 320",
+    Q4: "qu 128 qur 128 qv 128 qw 512 qe 512 qx 256 qz 256 qh 128 qf 128 qt0 128 qt1 128 qt2 128 lq 320",
+    U8: "su 128 sur 128 sv 128 sw 512 se 512 sx 256 sz 256 sh 128 sf 128 st0 128 st1 128 st2 128 ls 320",
 }
 SCRATCH = {n: ("sbuf", [128, int(w)], d) for d, s in SIZES.items() for n, w in zip(s.split()[0::2], s.split()[1::2])}
 SCRATCH.update({n: ("psum", [128, w], FP) for n, w in (("pw", 2048), ("pa", 512), ("pb", 512), ("pc", 512), ("pd", 512))})
 SEMAPHORES = ["V", "S", "P", "G", "ldx", "ldu", "ldn", "ldw", "lds", "ldv", "out", "sent", "arr0", "arr1", "arr2"]
-CYC = 0.83
-TRIES, PASSES, JITTER, STRETCH, PLAN = 1000, 2, 300.0, 2500.0, []
-TMP = "VS"
 
 
 def v(name, a=0, b=None, s=1):
@@ -41,12 +56,165 @@ def col(name, a):
     return v(name, a, a + 1)
 
 
+def half(x, h, parts=2):
+    n = len(span(x)) // parts
+    return (x[0], x[1] + h * n * x[3], x[1] + (h * n + n - 1) * x[3] + 1, x[3], None)
+
+
 def span(x):
     return range(x[1], x[2], x[3]) if x[3] > 0 else range(x[2] - 1, x[1] - 1, x[3])
 
 
 def length(x):
     return 16 * len(span(x[4])) if x[4] else len(span(x))
+
+
+def plan(calls):
+    n = len(calls)
+    on, cost, late = [c[0] for c in calls], [c[3] for c in calls], [c[4] for c in calls]
+    need, after, behind = [], [[] for _ in calls], []
+    for i in range(n):
+        mask, keep = 0, [(j, cost[j]) for j in calls[i][7]]
+        for j in sorted(calls[i][1], reverse=True):
+            if not mask >> j & 1:
+                keep.append((j, cost[j] + late[j] + WAKE))
+                mask |= behind[j]
+        for j, lag in keep:
+            after[j].append((i, lag))
+        need.append(keep)
+        behind.append(mask | 1 << i)
+
+    def lay(turn, back):
+        begin, lines = [0.0] * n, {e: ([], []) for e in on}
+        for i in turn:
+            if back:
+                t = max([begin[j] + cost[j] + lag - cost[i] for j, lag in after[i]] + [late[i]])
+            else:
+                t = max([begin[j] + lag for j, lag in need[i]] + [0.0])
+            (a, b), c = lines[on[i]], cost[i]
+            k = len(b)
+            while k and b[k - 1] > t:
+                k -= 1
+            while k < len(a) and a[k] < t + c:
+                t, k = max(t, b[k]), k + 1
+            a.insert(k, t)
+            b.insert(k, t + c)
+            begin[i] = t
+        return begin
+
+    def line_up(begin):
+        last = {}
+        for i in sorted(range(n), key=lambda i: (begin[i], i)):
+            prev[i], nxt[i] = last.get(on[i], -1), -1
+            if prev[i] >= 0:
+                nxt[prev[i]] = i
+            last[on[i]] = i
+
+    def times():
+        left = [len(need[i]) + (prev[i] >= 0) for i in range(n)]
+        turn, free, begin, own, rest = [i for i in range(n) if not left[i]], [0.0] * n, [0.0] * n, [0.0] * n, [0.0] * n
+        for i in turn:
+            p, t = prev[i], free[i]
+            if p >= 0 and begin[p] + cost[p] > t:
+                t = begin[p] + cost[p]
+            begin[i] = t
+            for j, lag in after[i]:
+                if t + lag > free[j]:
+                    free[j] = t + lag
+                left[j] -= 1
+                if not left[j]:
+                    turn.append(j)
+            j = nxt[i]
+            if j >= 0:
+                left[j] -= 1
+                if not left[j]:
+                    turn.append(j)
+        if len(turn) < n:
+            return None
+        for i in reversed(turn):
+            t = cost[i] + late[i]
+            for j, lag in after[i]:
+                if lag + rest[j] > t:
+                    t = lag + rest[j]
+            own[i], j = t, nxt[i]
+            rest[i] = cost[i] + rest[j] if j >= 0 and cost[i] + rest[j] > t else t
+        return max(rest), begin, free, rest, own
+
+    def relaid(begin):
+        back = lay(sorted(range(n), key=lambda i: (-begin[i] - cost[i], -i)), True)
+        return lay(sorted(range(n), key=lambda i: (-back[i] - cost[i], i)), False)
+
+    prev, nxt, rng = [-1] * n, [-1] * n, np.random.default_rng(SEED)
+    rest = times()[3]
+    line_up(relaid(lay(sorted(range(n), key=lambda i: (-rest[i], i)), False)))
+    now = best = times()
+    barred, stale = {}, 0
+    for step in range(ROUNDS):
+        whole, begin, free, rest, own = now
+        i = max(range(n), key=lambda k: rest[k])
+        runs = [[i]]
+        while True:
+            j, on_path = nxt[i], [k for k, lag in after[i] if abs(lag + rest[k] - rest[i]) < 1e-6]
+            if j >= 0 and abs(cost[i] + rest[j] - rest[i]) < 1e-6:
+                runs[-1].append(j)
+            elif on_path:
+                j = on_path[0]
+                runs.append([j])
+            else:
+                break
+            i = j
+        moves = [(b, x, y, back) for b in runs for x in range(len(b) - 1) for y in range(x + 1, min(len(b), x + REACH + 1))
+                 if x == 0 or y == len(b) - 1 or y == x + 1 for back in range(1 + (y > x + 1))]
+        chosen = None
+        for k in rng.integers(len(moves), size=SAMPLE).tolist():
+            b, x, y, back = moves[k]
+            u, w = b[x], b[y]
+            if back:
+                if any(begin[j] + cost[j] > begin[u] + cost[u] or j == u for j, _ in need[w]):
+                    continue
+                new, pairs = [w] + b[x:y], [(w, j) for j in b[x:y]]
+            else:
+                if any(rest[j] > rest[w] or j == w for j, _ in after[u]):
+                    continue
+                new, pairs = b[x + 1:y + 1] + [u], [(j, u) for j in b[x + 1:y + 1]]
+            if any(barred.get(p, -1) > step for p in pairs):
+                continue
+            t, heads = begin[prev[u]] + cost[prev[u]] if prev[u] >= 0 else 0.0, []
+            for j in new:
+                t = max(t, free[j])
+                heads.append(t)
+                t += cost[j]
+            t, longest = rest[nxt[w]] if nxt[w] >= 0 else 0.0, 0.0
+            for j, h in zip(new[::-1], heads[::-1]):
+                t = max(t + cost[j], own[j])
+                longest = max(longest, h + t)
+            d = longest - whole
+            d = d if d < -0.5 else float(rng.exponential(1.0)) * (EVEN if d < 0.5 else d)
+            if chosen is None or d < chosen[0]:
+                chosen = (d, [prev[u]] + new + [nxt[w]], pairs)
+        if chosen is None:
+            continue
+        for j, k in zip(chosen[1], chosen[1][1:]):
+            if j >= 0:
+                nxt[j] = k
+            if k >= 0:
+                prev[k] = j
+        for j, k in chosen[2]:
+            barred[k, j] = step + 8 + int(rng.integers(8))
+        now, stale = times(), stale + 1
+        if now and step % RELAY == 0:
+            line_up(relaid(now[1]))
+            new = times()
+            if new[0] <= now[0]:
+                now = new
+            else:
+                line_up(now[1])
+        if now and now[0] < best[0]:
+            best, stale = now, 0
+        if now is None or stale > STALE:
+            line_up(best[1])
+            now, stale = times(), 0
+    return sorted(range(n), key=lambda i: (best[1][i], i))
 
 
 def rank_program(g, core, T, topo):
@@ -61,7 +229,7 @@ def rank_program(g, core, T, topo):
     queue = {"V": g.vector, "S": g.scalar, "P": g.tensor, "G": g, "Y": g.sync}
     count = {s: 0 for s in SEMAPHORES}
     known = {e: {} for e in queue}
-    calls, first = [], []
+    calls = []
     writer = {n: [-1] * d[1][1] for n, d in SCRATCH.items()}
     readers = {n: [[] for _ in range(d[1][1])] for n, d in SCRATCH.items()}
     banks = {}
@@ -78,12 +246,15 @@ def rank_program(g, core, T, topo):
             t = t.bitcast(word)
         return t.indirect(ap(off)) if off else t
 
-    def record(e, r, w, fn, cost, late, sem, n, soon=0.0, after=()):
-        me, need = len(calls), set(after)
+    def record(e, r, w, fn, cost, late, sem, n, after=()):
+        me, need, turn = len(calls), set(after), set()
         r = [x for x in r if isinstance(x, tuple)]
         r += [x[4] for x in r + w if x[4]]
-        for x in r + w:
+        for x in r:
             need.update(writer[x[0]][c] for c in span(x))
+        for x in w:
+            turn.update(writer[x[0]][c] for c in span(x))
+        for x in r + w:
             if SCRATCH[x[0]][0] == "psum":
                 for b in {c // 512 for c in span(x)}:
                     users = banks.setdefault((x[0], b), [])
@@ -91,18 +262,19 @@ def rank_program(g, core, T, topo):
                     users.append(me)
         for x in w:
             for c in span(x):
-                need.update(readers[x[0]][c])
+                turn.update(readers[x[0]][c])
         for x in r:
             for c in span(x):
                 readers[x[0]][c].append(me)
         for x in w:
             for c in span(x):
                 writer[x[0]][c], readers[x[0]][c] = me, []
-        first.append(soon)
-        calls.append((e, need - {-1, me}, fn, cost, late, sem, n))
+        turn -= need | {-1, me}
+        need.update(i for i in turn if calls[i][0] != e or calls[i][4] or late or not SOFT)
+        calls.append((e, need - {-1, me}, fn, cost, late, sem, n, turn - need))
         return me
 
-    def op(e, r, w, fn, rate=None, more=0.0, soon=0.0, after=()):
+    def op(e, r, w, fn, rate=None, more=0.0):
         full = [x for x in r + w if isinstance(x, tuple)]
         n = length(full[0])
         if rate is None:
@@ -112,71 +284,19 @@ def rank_program(g, core, T, topo):
             cost = (50 if e == "V" else 65) + 1.56 * CYC * n
         if w[0][4]:
             cost = 50 + 3.8 * CYC * n
-        return record(e, r, w, lambda: fn(queue[e]).then_inc(T.sem[e], 1), cost + more, 0.0, e, 1, soon, after)
+        return record(e, r, w, lambda: fn(queue[e]).then_inc(T.sem[e], 1), cost + more, 0.0, e, 1)
 
     def dma(e, sem, r, w, out, in_, after=()):
         x = (r + w)[0]
         size = len(span(x)) * {BF: 2, U8: 1}.get(SCRATCH[x[0]][2], 4)
-        return record(e, r, w, lambda: queue[e].dma_start(out, in_).then_inc(T.sem[sem], 16), 60.0, 2000.0 + 0.64 * size, sem, 16, 0.0, after)
-
-    def lay(turn, before, back):
-        end, taken = [0.0] * len(calls), {e: [] for e in queue}
-        for i in turn:
-            e, _, _, cost, late = calls[i][:5]
-            if back:
-                t = max([end[j] + WAKE for j in before[i]] + [0.0]) + late
-            else:
-                t = max([end[j] + calls[j][4] + WAKE for j in before[i]] + [0.0])
-            line = taken[e]
-            k, hi = 0, len(line)
-            while k < hi:
-                mid = (k + hi) // 2
-                k, hi = (mid + 1, hi) if line[mid][1] <= t else (k, mid)
-            while k < len(line) and line[k][0] < t + cost:
-                t, k = max(t, line[k][1]), k + 1
-            line.insert(k, (t, t + cost))
-            end[i] = t + cost
-        return end
-
-    def plan():
-        n = len(calls)
-        need, after, behind = [], [[] for _ in calls], []
-        for i in range(n):
-            mask, keep = 0, []
-            for j in sorted(calls[i][1], reverse=True):
-                if not mask >> j & 1:
-                    keep.append(j)
-                    mask |= behind[j]
-                    after[j].append(i)
-            need.append(keep)
-            behind.append(mask | 1 << i)
-        rest, best = [0.0] * n, None
-        for i in range(n - 1, -1, -1):
-            rest[i] = first[i] + calls[i][3] + calls[i][4] + max([WAKE + rest[j] for j in after[i]] + [0.0])
-        rng = np.random.default_rng(0)
-        for trial in range(TRIES):
-            key, mid = list(rest), float(rng.uniform(0.0, best[0])) if best else 0.0
-            if best:
-                key = [-t + (x if abs(t - mid) < STRETCH else 0.0) for t, x in zip(best[2], rng.normal(0.0, JITTER, n).tolist())]
-            for i in range(n - 1, -1, -1):
-                key[i] = max([key[i]] + [key[j] + 1.0 for j in after[i]])
-            turn = sorted(range(n), key=lambda i: (-key[i], i))
-            for _ in range(PASSES):
-                end = lay(turn, need, False)
-                whole = max(end[i] + calls[i][4] for i in range(n))
-                if best is None or whole <= best[0]:
-                    begin = [end[i] - calls[i][3] for i in range(n)]
-                    best = (whole, sorted(range(n), key=lambda i: (begin[i], i)), begin)
-                back = lay(sorted(range(n), key=lambda i: (-end[i] - calls[i][4], -i)), after, True)
-                turn = sorted(range(n), key=lambda i: (-back[i], i))
-        return best[1]
+        return record(e, r, w, lambda: queue[e].dma_start(out, in_).then_inc(T.sem[sem], 16), 60.0, 2000.0 + 0.64 * size, sem, 16, after)
 
     def issue():
         if not PLAN:
-            PLAN.extend(plan())
+            PLAN.extend(plan(calls))
         event, clock = {}, {}
         for i in PLAN:
-            e, need, fn, cost, late, sem, inc = calls[i]
+            e, need, fn, cost, late, sem, inc, _ = calls[i]
             for ev in sorted({event[j] for j in need}, key=lambda ev: (-ev[1], ev[0])):
                 if known[e].get(ev[0], 0) < ev[1]:
                     queue[e].wait_ge(T.sem[ev[0]], ev[1])
@@ -188,46 +308,46 @@ def rank_program(g, core, T, topo):
             clock[event[i]] = dict(known[e]) if sem[:3] != "arr" else {}
             clock[event[i]][sem] = count[sem]
 
-    def ts(out, in0, s1, op0, s2=None, op1=None, **kw):
+    def ts(out, in0, s1, op0, s2=None, op1=None):
         if op1 is None:
-            return op("V", [in0, s1], [out], lambda q: q.tensor_scalar(ap(out), ap(in0), ap(s1), None, op0), **kw)
-        return op("V", [in0, s1, s2], [out], lambda q: q.tensor_scalar(ap(out), ap(in0), ap(s1), ap(s2), op0, op1), **kw)
+            return op("V", [in0, s1], [out], lambda q: q.tensor_scalar(ap(out), ap(in0), ap(s1), None, op0))
+        return op("V", [in0, s1, s2], [out], lambda q: q.tensor_scalar(ap(out), ap(in0), ap(s1), ap(s2), op0, op1))
 
-    def tt(out, a, b, o, **kw):
+    def tt(out, a, b, o):
         rate = 1.0 if "psum" in (SCRATCH[a[0]][0], SCRATCH[b[0]][0]) else 2.0
-        return op("V", [a, b], [out], lambda q: q.tensor_tensor(ap(out), ap(a), ap(b), o), rate, **kw)
+        return op("V", [a, b], [out], lambda q: q.tensor_tensor(ap(out), ap(a), ap(b), o), rate)
 
-    def cp(out, a, **kw):
-        return op("V", [a], [out], lambda q: q.tensor_copy(ap(out), ap(a)), **kw)
+    def cp(out, a):
+        return op("V", [a], [out], lambda q: q.tensor_copy(ap(out), ap(a)))
 
-    def scan(out, a, b, init, o0, o1, **kw):
-        return op("V", [a, b, init], [out], lambda q: q.tensor_tensor_scan(ap(out), ap(a), ap(b), ap(init), o0, o1), **kw)
+    def scan(out, a, b, init, o0, o1):
+        return op("V", [a, b, init], [out], lambda q: q.tensor_tensor_scan(ap(out), ap(a), ap(b), ap(init), o0, o1))
 
     def total(out, src, a, n, init):
         return scan(out, v(src, a, a + n // 2), v(src, a + n // 2, a + n), init, A.add, A.add)
 
-    def fill(out, c, **kw):
-        return op("V", [], [out], lambda q: q.memset(ap(out), c), **kw)
+    def fill(out, c):
+        return op("V", [], [out], lambda q: q.memset(ap(out), c))
 
-    def act(out, a, f, bias=0.0, scale=1.0, acc=None, **kw):
+    def act(out, a, f, bias=0.0, scale=1.0, acc=None):
         given = {k: x for k, x, usual in (("bias", bias, 0.0), ("scale", scale, 1.0), ("accum_out", acc, None)) if x != usual}
         return op("S", [a, bias, scale], [out, acc] if acc else [out],
-                  lambda q: q.activation(ap(out), ap(a), f, **{k: ap(x) for k, x in given.items()}), more=20.0 if acc else 0.0, **kw)
+                  lambda q: q.activation(ap(out), ap(a), f, **{k: ap(x) for k, x in given.items()}), more=20.0 if acc else 0.0)
 
-    def quant(q_, s_, a, b, src, **kw):
-        cost = 12 + 0.22 * length(src)
+    def quant(q_, s_, a, b, src):
         return record("V", [src], [v(q_, a, b), v(s_, a, b)],
-                      lambda: g.vector.quantize_mx(ap(v(q_, a, b)), ap(v(s_, a, b)), ap(src)).then_inc(T.sem["V"], 1), cost, 0.0, "V", 1, **kw)
+                      lambda: g.vector.quantize_mx(ap(v(q_, a, b)), ap(v(s_, a, b)), ap(src)).then_inc(T.sem["V"], 1),
+                      12 + 0.22 * length(src), 0.0, "V", 1)
 
     def mm(out, lq, ls, l0, rq, rs, r0, n):
         sides = [v(lq, l0, l0 + 128), v(ls, l0, l0 + 128), v(rq, r0, r0 + n), v(rs, r0, r0 + n)]
         return record("P", sides, [out], lambda: g.tensor.matmul_mx(ap(out), *[ap(x) for x in sides], True, True).then_inc(T.sem["P"], 1),
                       0.6 * (n + 16), 0.0, "P", 1)
 
-    def table(out, pat, base, cm=0, after=()):
+    def table(out, pat, base, cm=0):
         if SCRATCH[out[0]][2] == I32:
-            return op("G", [], [out], lambda q: q.iota(ap(out), pat, base, cm), 2.0, 130.0, after=after)
-        return op("G", [], [out], lambda q: q.iota(ap(out), pat, base, cm, allow_small_or_imprecise_dtypes=True), 2.0, 130.0, after=after)
+            return op("G", [], [out], lambda q: q.iota(ap(out), pat, base, cm), 2.0, 130.0)
+        return op("G", [], [out], lambda q: q.iota(ap(out), pat, base, cm, allow_small_or_imprecise_dtypes=True), 2.0, 130.0)
 
     def select(out, a, pat, x, cm=0):
         return op("G", [a], [out], lambda q: q.affine_select(ap(out), ap(a), pat, A.not_equal, x, 0, cm), 2.0, 170.0)
@@ -235,19 +355,22 @@ def rank_program(g, core, T, topo):
     def bank(b, a, n):
         return v("pw", 512 * b + a, 512 * b + n)
 
-    def pick(e, out, win, **kw):
-        return cp(out, win, **kw) if e == "V" else act(out, win, F.Copy, **kw)
+    def pick(e, out, win):
+        return cp(out, win) if e == "V" else act(out, win, F.Copy)
 
-    def half(x, h, parts=2):
-        n = len(span(x)) // parts
-        return (x[0], x[1] + h * n * x[3], x[1] + (h * n + n - 1) * x[3] + 1, x[3], None)
+    def listed(tmp, row):
+        scan(v(tmp), v("c16"), row, 0.0, A.mult, A.max)
+        return v(tmp, 15, C, 16)
+
+    def last(name):
+        return v(name, 3, 4 * C, 4)
 
     BIG = 2.0 ** 30
     FAR, FARTHER = 2.0 ** 25, 2.0 ** 28
     MID = 1.0 - 2.0 ** 23
     SPOT = 258
-    lx = dma("S", "ldx", [], [v("X")], T.X[:], T.x[:])
     lu = dma("Y", "ldu", [], [v("ub")], T.ub[:], T.u[:])
+    lx = dma("S", "ldx", [], [v("X")], T.X[:], T.x[:])
     dma("Y", "ldn", [], [v("nbi")], T.nbi[:], T.nb[:])
     lw = dma("Y", "ldw", [], [v("qw")], T.qw[:].bitcast(dt.uint8), T.wc[:], (lx, lu))
     dma("Y", "lds", [], [v("sw")], T.sw[:], T.ws[:], (lx, lu))
@@ -258,22 +381,23 @@ def rank_program(g, core, T, topo):
     table(v("lb"), [[-16, 16]], C - 16)
     table(v("di", 16, 32), [[4, 16]], 131, -1)
     table(v("i1"), [[1, C]], 1)
-    table(v("i0"), [[1, C]], 0)
-    table(v("cap"), [[1, C]], 2 ** 24 - SPOT)
+    table(v("p4"), [[1, 260], [0, 4]], 1)
     fill(v("one"), 1.0)
     fill(v("eb"), 0.0)
     for b in range(4):
         select(v("eb", 513 * b, 512 * b + 512, 4), v("eb", 513 * b, 512 * b + 512, 4), [[-1, 128]], 0.5, 1)
-    for dd, w, values in (("d2", 4, (FARTHER, 0.0, 0.0)), ("d3", 4, (FARTHER, 0.0, 0.0)), ("d4", 3, (FARTHER, 0.0, MID))):
+    for dd, values in (("d2", (FARTHER, 0.0, 0.0)), ("d3", (FARTHER, 0.0, 0.0)), ("d4", (FARTHER, 0.0, 0.0, MID))):
         for k, x in enumerate(values):
-            select(v(dd, k, w * C, w), v("one"), [[0, C]], x)
-    fill(v("m4", 768, 784), MID)
+            select(v(dd, k, 4 * C, 4), v("one"), [[0, C]], x)
+    select(v("TT", 256, 512), v("one"), [[0, C]], 0.0)
+    fill(v("byw", C, 272), FAR)
+    fill(v("m4", 1024, 1040), MID)
     fill(v("rs"), 0.0)
-    fill(v("rs", 0, 80, 5), FAR)
+    fill(v("rs", 0, 96, 6), FAR)
+    fill(v("nlf", 5, 96, 6), -1.0)
     fill(col("at", 15), 0.0)
-    fill(v("t1", C, 2 * C), FAR)
-    fill(v("TT", 256, 512), 0.0)
-    act(v("t1", 0, C), v("i0"), F.Copy, scale=65536.0)
+    select(v("t1", C, 2 * C), v("one"), [[0, C]], FAR)
+    act(v("t1", 0, C), v("i1"), F.Identity, bias=-65536.0, scale=65536.0)
     ts(v("dj", 0, 16), v("di", 0, 16), 15, A.bitwise_and)
     ts(v("dj", 32, 48), v("di", 32, 48), 15, A.bitwise_and)
     ts(v("cc", 0, 16), v("dj", 0, 16), 0.0, A.is_equal)
@@ -289,11 +413,11 @@ def rank_program(g, core, T, topo):
     ts(col("cr", 1), col("dj", 19), 0.0, A.is_equal, 1 / BIG, A.max)
     tt(v("cc", 48, 80), v("kk"), v("cc", 16, 48), A.max)
     ts(col("cr", 3), col("dj", 48), -4.0, A.add)
-    ts(col("cr", 4), col("dj", 32), -16.0, A.add)
+    ts(col("cr", 4), col("dj", 32), -15.0, A.add)
     ts(col("cr", 2), col("cr", 1), 4.0, A.mult)
-    ts(col("cr", 5), col("cr", 0), 3.0, A.mult)
     ts(col("cr", 6), col("cr", 0), 4.0, A.mult)
-    ts(v("nlf", 4, 80, 5), v("ln"), col("cr", 4), A.add)
+    ts(col("cr", 7), col("cr", 0), 1.0 / C, A.mult)
+    ts(v("nlf", 4, 96, 6), v("ln"), col("cr", 4), A.add)
     act(v("c16"), at(v("cc", 48, 64), v("oa")), F.Copy)
     act(v("c4"), at(v("cc", 64, 80), v("oa")), F.Copy)
     for b in range(4):
@@ -302,159 +426,200 @@ def rank_program(g, core, T, topo):
     cp(v("nbu"), v("nbi"))
     for p in range(4):
         pick("VSSS"[p], half(v("NR"), p, 4), at(v("i1"), half(v("nbu"), p, 4)))
+    for e in range(4):
+        scan(half(v("NC"), e, 4), v("c16"), v("NR", e, 1024, 4), 0.0, A.mult, A.max)
+        ts(v("nlf", e, 96, 6), v("NC", C * e + 15, C * e + C, 16), col("cr", 0), A.mult)
+    ts(v("nl"), v("NC", 15, 1024, 16), col("cr", 0), A.mult, -1.0, A.add)
+    ts(v("nl4"), v("NC", 15, 1024, 16), col("cr", 6), A.mult, -1.0, A.add)
     quant("qu", "su", 0, 128, v("ub"))
     act(v("sur"), at(v("su"), v("ou")), F.Copy)
     op("V", [at(v("qu"), v("ou"))], [v("qur")], lambda q: q.tensor_copy(ap(v("qur"), dt.uint32), ap(at(v("qu"), v("ou")), dt.uint32)))
     quant("qx", "sx", 0, C, v("X"))
     quant("lq", "ls", 0, 128, v("X", 0, 512))
 
-    def names_to_lists():
-        for e in range(4):
-            scan(half(v("NC"), e, 4), v("c16"), v("NR", e, 1024, 4), 0.0, A.mult, A.max)
-            ts(v("nlf", e, 80, 5), v("NC", C * e + 15, C * e + C, 16), col("cr", 0), A.mult, -1.0, A.add)
-        ts(v("nl"), v("NC", 15, 1024, 16), col("cr", 0), A.mult, -1.0, A.add)
-        ts(v("nl4"), v("NC", 15, 1024, 16), col("cr", 6), A.mult, -1.0, A.add)
-
     def own(i, src="H"):
         return col(src, 16 * i + 15)
 
     def carried(lo, hi, c0):
-        return v("sg", SG * lo + 15 + c0, SG * (hi - 1) + 16 + c0, SG)
+        return v("sg", SG * lo + PAD - 1 + c0, SG * (hi - 1) + PAD + c0, SG)
 
-    def s_rows(rows, src, c0, out):
-        lo, hi = rows[0], rows[-1] + 1
-        for i in rows:
-            a, b = SG * i + 16, 16 * i + 16
-            act(v("sg", a + c0, a + C), v(src, 0, C - c0), F.Sign, bias=own(i), scale=-1.0)
+    def scores(c0, c1, one, two):
+        n = max(c1 - c0, 128)
+        for x in (one, two):
+            mm(v(x[0], x[1], x[1] + n), "qur", "sur", 0, "qx", "sx", c1 - n, n)
+        return c0, c1, (one[0], one[1] + n - c1), (two[0], two[1] + n - c1)
+
+    def part(x, a, b):
+        return v(x[0], x[1] + a, x[1] + b)
+
+    def s_rows(lo, hi, pieces, out):
+        first = min(p[0] for p in pieces)
+        for i in range(lo, hi):
+            a, b = SG * i + PAD, 16 * i + 16
+            for c0, c1, _, x in pieces:
+                act(v("sg", a + c0, a + c1), part(x, c0, c1), F.Sign, bias=own(i), scale=-1.0)
             if i < 15:
                 act(v("sg", a + b, a + C), v("sg", a + b, a + C), F.Relu, scale=-1.0, acc=col("at", i))
         tt(v("e1", lo, hi), v("lb", lo, hi), v("co", 16 * lo + 15, 16 * hi, 16), A.add)
-        tt(carried(lo, hi, c0), v("e1", lo, hi), v("at", lo, hi), A.subtract)
-        for i in rows:
-            a, b = SG * i + 16, 16 * i + 16
-            act(v("sg", a + c0 - 1, a + b), v("sg", a + c0 - 1, a + b), F.Relu, acc=col(out, i))
+        tt(carried(lo, hi, first), v("e1", lo, hi), v("at", lo, hi), A.subtract)
+        for i in range(lo, hi):
+            a, b = SG * i + PAD, 16 * i + 16
+            act(v("sg", a + first - 1, a + b), v("sg", a + first - 1, a + b), F.Relu, acc=col(out, i))
 
-    def v_row(i, src, c0, n, to, a, out, init):
-        b = min(16 * i + 16 - c0, n)
-        ts(v(to, a, a + b), v(src, 0, b), own(i), A.is_lt)
-        if b < n:
-            ts(v(to, a + b, a + n), v(src, b, n), own(i), A.is_le)
-        total(out, to, a, n, init)
+    def v_row(i, pieces, to, a, out, init):
+        first, end = min(p[0] for p in pieces), max(p[1] for p in pieces)
+        for c0, c1, x, _ in pieces:
+            b = min(max(16 * i + 16, c0), c1)
+            for p, q, o in ((c0, b, A.is_lt), (b, c1, A.is_le)):
+                if p < q:
+                    ts(v(to, a + p - first, a + q - first), part(x, p, q), own(i), o)
+        total(out, to, a, end - first, init)
 
-    def to_list(src, c0, n):
-        tt(v("ms", c0, c0 + n), v(src, 0, n), v("mk", 0, n), A.mult)
-        scan(v("H", c0, c0 + n), v("nm", 0, n), v("ms", c0, c0 + n), 0.0, A.mult, A.add)
-        tt(v("eq", c0, c0 + n), v("H", c0, c0 + n), v(src, 0, n), A.is_equal)
-        scan(v("co", c0, c0 + n), v("nm", 0, n), v("eq", c0, c0 + n), 0.0, A.mult, A.add)
-
-    def start_of(src, src2, c0, n, most, rest):
-        scan(v("mx", c0, c0 + n), v(src, 0, n), v("one", 0, n), most, A.max, A.mult)
-        act(v("nf", c0, c0 + n), v(src2, 0, n), F.Sign, bias=col("mx", c0 + n - 1), scale=-1.0)
-        scan(v("cs", c0, c0 + n), v("one", 0, n), v("nf", c0, c0 + n, -1), rest, A.add, A.mult)
+    def prepare(piece, behind):
+        c0, c1, one, two = piece
+        src, n = part(one, c0, c1), c1 - c0
+        tt(v("ms", c0, c1), src, v("mk", 0, n), A.mult)
+        scan(v("H", c0, c1), v("nm", 0, n), v("ms", c0, c1), 0.0, A.mult, A.add)
+        tt(v("eq", c0, c1), v("H", c0, c1), src, A.is_equal)
+        scan(v("co", c0, c1), v("nm", 0, n), v("eq", c0, c1), 0.0, A.mult, A.add)
+        scan(v("mx", c0, c1), src, v("one", 0, n), col("mx", behind) if behind else -BIG ** 3, A.max, A.mult)
+        act(v("nf", c0, c1), part(two, c0, c1), F.Sign, bias=col("mx", c1 - 1), scale=-1.0)
+        scan(v("cs", c0, c1), v("nf", c0, c1, -1), v("one", 0, n), col("cs", behind) if behind else 0.0, A.mult, A.add)
 
     def early():
-        mm(v("pa", 0, M), "qur", "sur", 0, "qx", "sx", K, M)
-        mm(v("pb", 0, M), "qur", "sur", 0, "qx", "sx", K, M)
-        to_list("pa", K, M)
-        start_of("pa", "pb", K, M, -BIG ** 3, 0.0)
-        lo, h = 4 + NE, M // 2
-        s_rows(range(lo, 16), "pb", K, "rb")
-        for i in range(4, lo):
-            v_row(i, "pa", K, M, "ce", M * (i - 4), v("ceo", h * (i - 4), h * (i - 3)), own(i, "co"))
-        if NL < NE:
-            cp(carried(4 + NL, lo, 0), v("ceo", h * NL + h - 1, h * NE, h))
-        lo = max(lo, 4 + NL)
-        cp(carried(lo, 16, 0), v("rb", lo, 16))
+        pieces = [scores(128, C, ("pa", 0), ("pb", 0)), scores(K, 128, ("pc", 0), ("pd", 0))]
+        prepare(pieces[0], 0)
+        prepare(pieces[1], C - 1)
+        s_rows(4 + NE, 16, pieces, "ab")
+        cp(carried(4 + NE, 16, 0), v("ab", 4 + NE, 16))
+        for i in range(4, 4 + NE):
+            v_row(i, pieces, "ce", M * (i - 4), v("sg", SG * i, SG * i + PAD), own(i, "co"))
 
     def late(t):
-        nv, n0, h = (NV, C, 0) if t == 0 else (4, K, M // 2)
-        mm(v("pc", 0, C), "qur", "sur", 0, "qx", "sx", 0, C)
-        mm(v("pd", 0, C), "qur", "sur", 0, "qx", "sx", 0, C)
-        to_list("pc", 0, n0)
-        start_of("pc", "pd", 0, n0, col("mx", C - 1) if t else -BIG ** 3, col("cs", C - 1) if t else 0.0)
+        nv, n0 = (NV, C) if t == 0 else (4, K)
+        whole = scores(0, C, ("pw", 0), ("pw", 512))
+        if t:
+            mm(bank(2, 0, 128), "qur", "sur", 0, "qx", "sx", 0, 128)
+        prepare((0, n0, ("pw", 1024) if t else whole[2], whole[3]), 127 if t else 0)
         start = col("cs", n0 - 1)
-        ts(v("nn"), v("nlf"), start, A.not_equal, 256.0, A.mult)
-        scan(v("n2"), v("rs"), v("nn"), 0.0, A.max, A.min)
-        ts(v("g2", 3, 1024, 4), v("i0"), start, A.not_equal, FAR, A.mult)
-        tt(v("ci", 0, nv), v("co", 15, 16 * nv, 16), v("n2", 4, 5 * nv, 5), A.subtract)
-        for i in range(nv):
-            v_row(i, "pc", 0, C, "cb", C * i, v("cbo", 128 * i, 128 * i + 128), col("ci", i))
+        if t:
+            act(col("p4", 4 * SPOT - 1), start, F.Copy)
+            ts(col("cu", 0), start, -1.0, A.add)
+            act(v("s1"), at(v(NODE_AT[t]), col("cu", 0)), F.Copy)
+            start = col("s1", 0)
+        act(v("sn"), v("i1"), F.Sign, bias=start, scale=-1.0)
+        act(last("g2"), v("sn"), F.Abs, scale=FAR)
+        ts(v("nn"), v("nlf"), start, A.not_equal, 1.0 if t else float(C), A.mult)
+        scan(v("n2"), v("rs"), v("nn"), 0.0, A.add, A.min)
+        counts = v("cbo", 127, 128 * nv, 128)
         if t == 0:
-            s_rows(range(nv, 16), "pd", 0, "ab")
-        else:
-            for lo, hi, known_ in ((4, 4 + min(NE, NL), v("ceo", h - 1, h * min(NE, NL), h)), (4 + NE, 4 + NL, v("rb", 4 + NE, 4 + NL))):
-                if lo < hi:
-                    tt(v("ci", lo, hi), known_, v("n2", 5 * lo + 4, 5 * hi, 5), A.subtract)
-            nv = 4 + NL
-            for i in range(4, nv):
-                v_row(i, "pc", 0, K, "cb", C * i, v("cbo", 128 * i + 96, 128 * i + 128), col("ci", i))
-            for i in range(nv, 16):
-                a = SG * i + 16
-                act(v("sg", a, a + K), v("pd", 0, K), F.Sign, bias=own(i), scale=-1.0)
-                act(v("sg", a - 1, a + K), v("sg", a - 1, a + K), F.Relu, acc=col("ab", i))
-        ts(v("bcu", 0, nv), v("cbo", 127, 128 * nv, 128), -1.0, A.mult, float(C), A.add)
-        tt(v("bc", 0, nv), v("cbo", 127, 128 * nv, 128), v("n2", 4, 5 * nv, 5), A.add)
-        ts(v("byu", 0, nv), v("bc", 0, nv), -1.0, A.mult, float(C), A.add)
-        tt(v("bc", nv, 16), v("n2", 5 * nv + 4, 80, 5), v("ab", nv, 16), A.subtract)
-        ts(v("bcu", nv, 16), v("bc", nv, 16), float(C), A.add)
+            tt(v("ci", 0, nv), v("co", 15, 16 * nv, 16), v("n2", 5, 6 * nv, 6), A.subtract)
+            for i in range(nv):
+                v_row(i, [whole], "cb", C * i, v("cbo", 128 * i, 128 * i + 128), col("ci", i))
+            s_rows(nv, 16, [whole], "ab")
+            ts(v("bcu", 0, nv), counts, -1.0, A.mult, float(C), A.add)
+            tt(v("bc", 0, nv), counts, v("n2", 5, 6 * nv, 6), A.add)
+            ts(v("byu", 0, nv), v("bc", 0, nv), -1.0, A.mult, float(C), A.add)
+            tt(v("bc", nv, 16), v("n2", 6 * nv + 5, 96, 6), v("ab", nv, 16), A.subtract)
+            ts(v("bcu", nv, 16), v("bc", nv, 16), float(C), A.add)
+            ts(v("byu", nv, 16), v("ab", nv, 16), -1.0, A.mult, float(C), A.add)
+            for p in (1, 0):
+                pick("VS"[p], half(v("q1"), p), at(v("t1"), half(v("bcu"), p)))
+            return
+        ts(v("pqu"), v("n2", 5, 96, 6), float(C), A.mult)
+        for i in range(nv):
+            v_row(i, [whole], "cb", C * i, v("cbo", 128 * i, 128 * i + 128), own(i, "co"))
+        for i in range(nv, 16):
+            a = SG * i + PAD
+            act(v("sg", a, a + K), part(whole[3], 0, K), F.Sign, bias=own(i), scale=-1.0)
+            act(v("sg", a - 1, a + K), v("sg", a - 1, a + K), F.Relu, acc=col("ab", i))
+        ts(v("byu", 0, nv), counts, -1.0, A.mult, float(C), A.add)
         ts(v("byu", nv, 16), v("ab", nv, 16), -1.0, A.mult, float(C), A.add)
         for p in (1, 0):
-            pick("VS"[p], half(v("q1"), p), at(v("t1"), half(v("bcu"), p)))
+            pick("VS"[p], half(v("byw", 0, C), p), at(v("t1", 0, C), half(v("byu"), p)))
+        for p in (1, 0):
+            pick("VS"[p], half(v("q1"), p), at(v("byw"), half(v("pqu"), p)))
 
-    def step(tab, lists, gg, dd, mo, w, tmp, most, shift=0.0):
-        for h in range(2):
-            a, b = 128 * w * h, 128 * w * (h + 1)
-            e = [at(tab, v(lists, 16 * k + 8 * h, 16 * k + 8 * h + 8)) for k in range(4)]
-            act(v(gg, a + 1, b, w), e[2], F.Copy)
-            act(v(gg, a + 2, b, w), e[3], F.Identity, bias=shift)
-            if most:
-                tt(half(v(tmp), h), e[0], half(v(most), h), A.min)
-            else:
-                pick(TMP[h], half(v(tmp), h), e[0])
-            tt(v(gg, a, b, w), e[1], half(v(tmp), h), A.min)
+    def step(tab, lists, gg, dd, mo, who):
+        for one, lo, hi in who:
+            a, b = 64 * lo, 64 * hi
+            e = [at(tab, v(lists, 16 * k + lo, 16 * k + hi)) for k in range(4)]
+            act(v(gg, a + 1, b, 4), e[2], F.Copy)
+            act(v(gg, a + 2, b, 4), e[3], F.Copy)
+            pick(one, v("tf", 16 * lo, 16 * hi), e[0])
+            tt(v(gg, a, b, 4), e[1], v("tf", 16 * lo, 16 * hi), A.min)
             scan(v(mo, a, b), v(dd, a, b), v(gg, a, b), 0.0, A.add, A.min)
 
-    def order():
+    def order(t):
         for b in range(4):
-            mm(bank(b, 0, C), "qe", "se", 128 * b, "qx", "sx", 0, C)
-            act(v("DX", b, 1024, 4), bank(b, 0, C), F.Copy)
-        act(v("d2", 3, 1024, 4), at(v("i0"), v("byu")), F.Copy, scale=256.0)
-        act(v("d3", 3, 1024, 4), at(v("i0"), v("byu")), F.Copy)
-        for p in range(4):
-            cp(at(v("cr2"), half(v("byu"), p, 4)), half(v("i1"), p, 4))
-        scan(v("cl", 1, C), v("c16", 1, C), v("cr2", 1, C), float(SPOT), A.mult, A.max)
-        ts(v("rl"), v("cl", 15, C, 16), col("cr", 5), A.mult, -1.0, A.add)
-        step(v("q1"), "nl", "g2", "d2", "m2", 4, "tf", None)
-        step(v("m2"), "nl4", "g2", "d3", "m3", 4, "tf", None)
-        step(v("m3"), "nl4", "g4", "d4", "m4", 3, "tf", "cap", MID)
+            mm(bank(2 + b % 2, 0, C), "qe", "se", 128 * b, "qx", "sx", 0, C)
+            act(v("DX", b, 1024, 4), bank(2 + b % 2, 0, C), F.Copy)
+        by = at(v("byw", 0, C), v("pu")) if t else at(v("t1", 0, C), v("byu"))
+        act(last("d2"), by, F.Copy, scale=2.0 ** -8)
+        act(last("d3"), by, F.Identity, bias=1.0, scale=2.0 ** -16)
+        act(last("g4"), last("p4"), F.Identity, bias=2.0 ** 24 - SPOT + MID)
+        rank_of = "bnu" if t else "byu"
+        if t:
+            ts(v("bnu"), listed("bn", last("d3")), col("cr", 0), A.mult, -1.0, A.add)
+        for p in range(NRP):
+            cp(at(v("nr"), half(v("byu"), p, NRP)), half(v(NODE_AT[t]), p, NRP))
+        scan(v("cl", 1, C), v("c16", 1, C), v("nr", 1, C), float(SPOT), A.mult, A.max)
+        ts(v("rl"), v("cl", 15, C, 16), col("cr", 6), A.mult, -1.0, A.add)
+        if t:
+            act(v("kr"), at(v("p4"), v("rl")), F.Copy)
+        step(v("q1"), "nl", "g2", "d2", "m2", TMP[0])
+        step(v("m2"), "nl4", "g2", "d3", "m3", TMP[1])
+        step(v("m3"), "nl4", "g4", "d4", "m4", TMP[2])
         for h in range(2):
             tt(half(v("mb"), h), at(v("m4"), half(v("rl"), h)), half(v("mk"), h), A.mult)
             scan(half(v("Hb"), h), half(v("nm"), h), half(v("mb"), h), 0.0, A.mult, A.add)
-        act(v("W", 0, C), at(v("m4"), v("rl")), F.Identity, bias=0.5)
-        act(v("W", C, 2 * C), at(v("m4"), v("rl")), F.Identity, bias=-0.5)
-        tt(v("eqb"), at(v("m4"), v("rl")), v("Hb"), A.is_equal)
+            act(half(v("W"), h, 4), at(v("m4"), half(v("rl"), h)), F.Identity, bias=0.5)
+            act(half(v("W"), 2 + h, 4), half(v("W"), h, 4), F.Identity, bias=-1.0)
+            tt(half(v("eqb"), h), at(v("m4"), half(v("rl"), h)), half(v("Hb"), h), A.is_equal)
         scan(v("cob"), v("nm"), v("eqb"), 0.0, A.mult, A.add)
-        ns = 16 - NB
-        for i in range(ns):
-            act(v("sg", SG * i, SG * i + C), v("W", 16 * i + 16, 16 * i + 16 + C), F.Sign, bias=own(i, "Hb"), scale=-1.0, acc=col("ac", i))
-        for i in range(ns, 16):
-            ts(v("cb", C * i, C * i + C), v("W", 16 * i + 16, 16 * i + 16 + C), own(i, "Hb"), A.is_gt)
-            total(v("cbo", 128 * i, 128 * i + 128), "cb", C * i, C, own(i, "cob"))
-        ts(v("npl", ns, 16), v("cbo", 128 * ns + 127, 2048, 128), -1.0, A.add)
-        ts(v("e2", 0, ns), v("cob", 15, 16 * ns, 16), 2.0, A.mult, 254.0, A.add)
-        tt(v("e3", 0, ns), v("e2", 0, ns), v("ac", 0, ns), A.subtract)
-        ts(v("npl", 0, ns), v("e3", 0, ns), 0.5, A.mult)
+        for i in range(16):
+            if i < NB:
+                act(v("sg", SG * i, SG * i + C), v("W", 16 * i + 16, 16 * i + 16 + C), F.Sign, bias=own(i, "Hb"), scale=-1.0, acc=col("ac", i))
+            else:
+                ts(v("cb", C * i, C * i + C), v("W", 16 * i + 16, 16 * i + 16 + C), own(i, "Hb"), A.is_gt)
+                total(v("cbo", 128 * i, 128 * i + 128), "cb", C * i, C, own(i, "cob"))
+        for first, end in BATCHES:
+            lo, hi = max(first, NB), end
+            if lo < hi:
+                ts(v("npl", lo, hi), v("cbo", 128 * lo + 127, 128 * hi, 128), -1.0, A.add)
+            lo, hi = first, min(end, NB)
+            ties = v("cob", 16 * lo + 15, 16 * hi, 16)
+            if hi - lo > 3:
+                ts(v("e2", lo, hi), ties, 2.0, A.mult, 254.0, A.add)
+                tt(v("e3", lo, hi), v("e2", lo, hi), v("ac", lo, hi), A.subtract)
+                ts(v("npl", lo, hi), v("e3", lo, hi), 0.5, A.mult)
+            elif lo < hi:
+                ts(v("e2", lo, hi), ties, 127.0, A.add)
+                for i in range(lo, hi):
+                    ts(col("npl", i), col("ac", i), -0.5, A.mult, col("e2", i), A.add)
+            cp(at(v(FROM[t]), v("npl", first, end)), v("kr" if t else "nr", 16 * first, 16 * end))
+        return rank_of
 
-    def move(t):
+    def fourfold(out, row, a, b):
+        scan(v("lc", a, b), v("c4", a, b), v(row, a, b), 0.0, A.mult, A.max)
+        ts(v(out, a // 4, b // 4), v("lc", a + 3, b, 4), col("cr", 2), A.mult, col("cr", 3), A.add)
+
+    def layer(q_, s_, o, skip, a, b, who, to=("qx", "sx")):
+        for k in range(4):
+            mm(bank(k, 0, 128), "qw", "sw", 128 * k, q_, s_, o, 128)
+            if who[k] == "V":
+                ts(v("X", 4 * a + k, 4 * b, 4), bank(k, skip, skip + b - a), 0.0, A.max, 0.03125, A.mult)
+            else:
+                act(v("X", 4 * a + k, 4 * b, 4), bank(k, skip, skip + b - a), F.Relu, scale=0.03125)
+        a = a // 128 * 128
+        quant(*to, a, a + 128, v("X", 4 * a, 4 * a + 512))
+
+    def move(t, rank_of):
         qt, st = "qt%d" % t, "st%d" % t
-        cut = 16 - NB + NB % 2
-        cp(at(v("lr"), v("npl", cut, 16)), v("cr2", 16 * cut, C))
-        cp(at(v("lr"), v("npl", 0, cut)), v("cr2", 0, 16 * cut))
-        for a, b in ((M, C), (0, M)):
-            scan(v("lc", a, b), v("c4", a, b), v("lr", a, b), 0.0, A.mult, A.max)
-            ts(v("l4", a // 4, b // 4), v("lc", a + 3, b, 4), col("cr", 2), A.mult, col("cr", 3), A.add)
+        fourfold("l4", FROM[t], M, C)
+        fourfold("l4", FROM[t], 0, M)
         for p in (1, 0):
-            pick("VS"[p], v("TT", 128 * p, 128 * p + 128), at(v("X"), v("l4", 48 + 8 * p, 56 + 8 * p)))
+            pick(TTE[p], v("TT", 128 * p, 128 * p + 128), at(v("X"), v("l4", 48 + 8 * p, 56 + 8 * p)))
         quant(qt, st, 0, 128, v("TT"))
         to, arr = 128 + K * t, "arr%d" % t
 
@@ -464,23 +629,33 @@ def rank_program(g, core, T, topo):
             count["sent"] += 2 * n_out
 
         record("G", [v(qt, 0, K), v(st, 0, K)], [v("lq", to, to + K), v("ls", to, to + K)], send, 500.0, TRAVEL, arr, 2 * n_in)
-        for p in range(3):
-            act(half(v("EH"), p, 3), at(v("DX"), half(v("l4"), p, 4)), F.Copy)
-            tt(half(v("Z"), p + 1, 4), at(v("DX"), half(v("l4"), p + 1, 4)), half(v("EH"), p, 3), A.add)
-        quant("qz", "sz", 0, M, v("Z", 256, 1024))
-        for b in range(4):
-            mm(bank(b, 0, M), "qw", "sw", 128 * b, "qz", "sz", 0, M)
-            if b % 2:
-                ts(v("X", 4 * K + b, 1024, 4), bank(b, 0, M), 0.0, A.max, 0.03125, A.mult)
-            else:
-                act(v("X", 4 * K + b, 1024, 4), bank(b, 0, M), F.Relu, scale=0.03125)
-        quant("qx", "sx", K, C, v("X", 4 * K, 1024))
+        for a, b in ZCUT:
+            act(v("EH", 16 * a, 16 * b), at(v("DX"), v("l4", a, b)), F.Copy)
+            if a < 32:
+                tt(v("Z", 16 * a + 256, 16 * b + 256), at(v("DX"), v("l4", a + 16, b + 16)), v("EH", 16 * a, 16 * b), A.add)
+        for k, name in enumerate(("pa", "pb", "pc", "pd")):
+            mm(v(name, 0, 128), "qe", "se", 128 * k, qt, st, 0, 128)
+            tt(v("Z", 768 + k, 1024, 4), v(name, 0, K), v("EH", 512 + k, 768, 4), A.add)
+        quant("qz", "sz", 0, 128, v("Z", 512, 1024))
+        layer("qz", "sz", 0, 0, 128, C, RELU[0])
+        quant("qz", "sz", 128, C, v("Z", 256, 768))
+        layer("qz", "sz", 128, 0, K, 128, RELU[1])
         act(v("iq"), at(v("i1"), v("npl")), F.Copy)
-        act(v("ir"), at(v("iq"), v("byu")), F.Copy)
-        for e in range(4):
-            act(v("NA", e, 1024, 4), at(v("ir"), half(v("nl"), e, 4)), F.Copy)
-        for p in range(4 if t < R - 1 else 0):
-            pick("VSSS"[p], half(v("NR"), p, 4), at(v("NA"), half(v("l4"), p, 4)))
+        act(last("p4"), at(v("iq"), v(rank_of)), F.Copy)
+        if t:
+            ts(v("lu"), listed("l16", v(FROM[t])), col("cr", 0), A.mult, -1.0, A.add)
+            act(v(NODE_AT[t + 1]), at(v(NODE_AT[t]), v("lu")), F.Copy)
+        if t < R - 1:
+            now = listed("pl", last("p4"))
+            ts(v("pu"), now, col("cr", 0), A.mult, -1.0, A.add)
+            ts(v("rs", 5, 96, 6), now, col("cr", 7), A.mult, -1.0 / C, A.add)
+        else:
+            for e in range(4):
+                act(v("NA", e, 1024, 4), at(v("p4"), half(v("nl4"), e, 4)), F.Copy)
+            fourfold("n4", NODE_AT[R], 0, C)
+            for p in range(2):
+                act(half(v("ON"), p), at(v("NA"), half(v("n4"), p)), F.Identity, bias=-1.0)
+            dma("S", "out", [v("ON")], [], T.on[:], T.ON[0:128:16, :])
 
     def mix(t):
         for b in range(4):
@@ -488,36 +663,27 @@ def rank_program(g, core, T, topo):
             mm(v(name, a, a + 128), "qe", "se", 128 * b, "lq", "ls", K + K * t, 128)
             tt(v("Z", b, 256, 4), v(name, a + K, a + 128), v("EH", b, 256, 4), A.add)
         quant("qh", "sh", 0, 128, v("Z", 0, 512))
-        for b in range(4):
-            mm(bank(b, 0, 128), "qw", "sw", 128 * b, "qh", "sh", 0, 128)
-            if b % 2:
-                ts(v("X", b, 4 * K, 4), bank(b, 0, K), 0.0, A.max, 0.03125, A.mult)
-            else:
-                act(v("X", b, 4 * K, 4), bank(b, 0, K), F.Relu, scale=0.03125)
-        quant("qx", "sx", 0, 128, v("X", 0, 512))
+        layer("qh", "sh", 0, 0, 0, K, RELU[2], ("qf", "sf") if t == R - 1 else ("qx", "sx"))
 
     for t in range(R):
-        names_to_lists()
         if t:
             early()
             mix(t - 1)
         late(t)
-        order()
-        move(t)
+        move(t, order(t))
 
-    act(v("ON"), at(v("NA"), v("l4")), F.Identity, bias=-1.0)
-    dma("S", "out", [v("ON")], [], T.on[:], T.ON[0:128:16, :])
-    mm(v("pw", 0, 128), "qv", "sv", 0, "qx", "sx", 128, 128)
-    dma("Y", "out", [v("qx", 128, C)], [], T.oc[:, 512:1024], ap(v("qx", 128, C), dt.uint8))
-    act(v("ys", 128, C), v("pw", 0, 128), F.Copy)
-    dma("S", "out", [v("ys", 128, C)], [], T.y[:, 128:C], T.ys[:, 128:C])
+    def leave(q_, s_, a, b, name, e, first, second):
+        n = max(b - a, 128)
+        mm(v(name, 0, n), "qv", "sv", 0, q_, s_, a, n)
+        dma(first, "out", [v(q_, a, b)], [], T.oc[:, 4 * a:4 * b], ap(v(q_, a, b), dt.uint8))
+        for k in range(4):
+            dma(second if k else first, "out", [v(s_, a, b)], [], T.osc[4 * k:4 * k + 4, a:b], T[s_][32 * k:32 * k + 4, a:b])
+        pick(e, v("ys", a, b), v(name, 0, b - a))
+        dma(first, "out", [v("ys", a, b)], [], T.y[:, a:b], T.ys[:, a:b])
+
     mix(R - 1)
-    mm(v("pc", 0, 128), "qv", "sv", 0, "qx", "sx", 0, 128)
-    dma("Y", "out", [v("qx", 0, 128)], [], T.oc[:, 0:512], ap(v("qx", 0, 128), dt.uint8))
-    for k in range(4):
-        dma("S" if k else "Y", "out", [v("sx")], [], T.osc[4 * k:4 * k + 4, :], T.sx[32 * k:32 * k + 4, :])
-    cp(v("ys", 0, 128), v("pc", 0, 128))
-    dma("Y", "out", [v("ys", 0, 128)], [], T.y[:, 0:128], T.ys[:, 0:128])
+    leave("qx", "sx", K, C, "pc", "S", "Y", "Y")
+    leave("qf", "sf", 0, K, "pd", "V", "Y", "S")
     issue()
     for s in SEMAPHORES:
         if count[s]:

@@ -3,22 +3,24 @@ from concourse.mybir import dt, AluOpType as A, ActivationFunctionType as F
 
 C, K, R = 256, 64, 3
 M = C - K
-NV = 9
-NE = 5
+SROWS = ((9, 16), (4, 12))
+NAMES = ("SSVV", "SSVV")
 NB = 11
-NRP = 4
+CUTS = (0, 2, 4, 6, 10, 16)
 TMP = ((("V", 0, 8), ("V", 8, 16)), (("V", 0, 8), ("S", 8, 16)), (("V", 0, 8), ("S", 8, 16)))
 TTE = "VS"
 RELU = ("SVSV", "SSSS", "SVSV")
 BATCHES = ((12, 16), (0, 8), (8, 12))
-ZCUT = ((16, 24), (24, 32), (32, 48), (0, 8), (8, 16))
-WAKE, TRAVEL = 240.0, 2800.0
+ZCUT = ((0, 8), (8, 16), (16, 24), (24, 32), (32, 48))
+WAKE, TRAVEL = 220.0, (2000.0, 2000.0, 1500.0)
+ENGINES = 8
+WIDE, SINGLE = [("pw", 512 * k) for k in range(4)], [(n, 0) for n in ("pa", "pb", "pc", "pd")]
 CYC = 0.83
-NODE_AT = ("i1", "na1", "na2", "na1")
+NODE_AT = ("i1", "na1", "na2")
 FROM = ("na1", "lr", "lr")
 SOFT = 0
-ROUNDS = 12000
-SEED = 0
+ROUNDS = 16000
+SEED = 1
 REACH = 20
 SAMPLE = 30
 EVEN = 60.0
@@ -26,13 +28,13 @@ STALE = 800
 RELAY = 20
 PLAN = []
 BF, FP, U16, I32, Q4, U8 = "bfloat16", "float32", "uint16", "int32", "float8_e4m3fn_x4", "uint8"
-PAD = 96
+PAD = 16
 SG = PAD + C
 SIZES = {
-    BF: "X 1024 ub 512 vb 512 eb 2048 TT 512 Z 1024 DX 1024 EH 768 kk 32 cc 80 mk 256 nm 256 c16 256 c4 256 i1 256 t1 512 ci 16 "
-        "NR 1024 NA 1024 NC 1024 eq 256 co 256 nf 256 cs 256 sn 256 one 256 ce 2304 cb 4096 cbo 2048 sg 5632 byw 272 q1 256 "
+    BF: "X 1024 ub 512 vb 512 eb 2048 TT 512 ZH 512 Z 1024 DX 1024 EH 768 kk 32 cc 80 mk 256 nm 256 c16 256 c4 256 i1 256 t1 512 ci 16 "
+        "NR 1024 NA 1024 NC 1024 eq 256 co 256 nf 256 cs 256 sn 256 one 256 cb 4096 cbo 2048 sg 4352 byw 272 q1 256 "
         "d2 1024 d3 1024 lr 256 lc 256 iq 256 nr 256 cl 256 kr 256 bn 256 eqb 256 cob 256 rs 96 p4 1040 pl 256 na1 256 na2 256 l16 256 s1 16",
-    FP: "cr 10 ln 16 nlf 96 ON 1024 ms 256 H 256 mx 256 nn 96 n2 96 at 16 ab 16 e1 16 e2 16 e3 16 ac 16 lb 16 bc 16 "
+    FP: "cr 10 ln 16 nlf 96 ON 1024 ms 256 H 256 mx 256 nn 96 n2 96 at 16 ab 16 e1 16 e2 16 ac 16 lb 16 bc 16 "
         "d4 1024 g2 1024 g4 1024 m2 1024 m3 1024 m4 1040 tf 256 mb 256 Hb 256 W 512 ys 256",
     U16: "nbu 64 oa 16 ou 8 nl 64 nl4 64 byu 16 bcu 16 rl 16 npl 16 l4 64 n4 64 pu 16 pqu 16 bnu 16 lu 16 cu 2",
     I32: "nbi 64 di 48 dj 64",
@@ -41,7 +43,7 @@ SIZES = {
 }
 SCRATCH = {n: ("sbuf", [128, int(w)], d) for d, s in SIZES.items() for n, w in zip(s.split()[0::2], s.split()[1::2])}
 SCRATCH.update({n: ("psum", [128, w], FP) for n, w in (("pw", 2048), ("pa", 512), ("pb", 512), ("pc", 512), ("pd", 512))})
-SEMAPHORES = ["V", "S", "P", "G", "ldx", "ldu", "ldn", "ldw", "lds", "ldv", "out", "sent", "arr0", "arr1", "arr2"]
+SEMAPHORES = ["V", "S", "P", "G", "ldx", "ldy", "ldt", "ldu", "ldn", "ldw", "lds", "ldv", "out", "sent", "arr0", "arr1", "arr2"]
 
 
 def v(name, a=0, b=None, s=1):
@@ -224,7 +226,13 @@ def rank_program(g, core, T, topo):
     n_ranks = len(T.cores)
     nxt, prv = T.cores[(rank + 1) % n_ranks], T.cores[(rank - 1) % n_ranks]
     rid, pid = topo.addr(nxt)[:2]
-    n_out, n_in = len(topo.engines(core, nxt)), len(topo.engines(prv, core))
+
+
+    def engines(src, dst):
+        e = topo.engines(src, dst)
+        return e[::max(1, len(e) // ENGINES)]
+
+    n_out, n_in, mask = len(engines(core, nxt)), len(engines(prv, core)), sum(1 << e for e in engines(core, nxt))
 
     queue = {"V": g.vector, "S": g.scalar, "P": g.tensor, "G": g, "Y": g.sync}
     count = {s: 0 for s in SEMAPHORES}
@@ -286,10 +294,10 @@ def rank_program(g, core, T, topo):
             cost = 50 + 3.8 * CYC * n
         return record(e, r, w, lambda: fn(queue[e]).then_inc(T.sem[e], 1), cost + more, 0.0, e, 1)
 
-    def dma(e, sem, r, w, out, in_, after=()):
+    def dma(e, sem, r, w, out, in_, after=(), rows=128):
         x = (r + w)[0]
         size = len(span(x)) * {BF: 2, U8: 1}.get(SCRATCH[x[0]][2], 4)
-        return record(e, r, w, lambda: queue[e].dma_start(out, in_).then_inc(T.sem[sem], 16), 60.0, 2000.0 + 0.64 * size, sem, 16, after)
+        return record(e, r, w, lambda: queue[e].dma_start(out, in_).then_inc(T.sem[sem], 16), 60.0, 2000.0 + 0.005 * rows * size, sem, 16, after)
 
     def issue():
         if not PLAN:
@@ -369,9 +377,13 @@ def rank_program(g, core, T, topo):
     FAR, FARTHER = 2.0 ** 25, 2.0 ** 28
     MID = 1.0 - 2.0 ** 23
     SPOT = 258
-    lu = dma("Y", "ldu", [], [v("ub")], T.ub[:], T.u[:])
-    lx = dma("S", "ldx", [], [v("X")], T.X[:], T.x[:])
-    dma("Y", "ldn", [], [v("nbi")], T.nbi[:], T.nb[:])
+    lt = dma("S", "ldt", [], [v("ub", 256, 512)], T.ub[:, 256:512], T.u[:, 256:512])
+    calls[dma("S", "ldn", [], [v("nbi")], T.nbi[:], T.nb[:])][7].add(lt)
+    lu = dma("Y", "ldu", [], [v("ub", 0, 256)], T.ub[:, 0:256], T.u[:, 0:256])
+    lz = dma("Y", "ldx", [], [v("X", 512, 1024)], T.X[:, 512:1024], T.x[:, 512:1024])
+    lx = dma("Y", "ldy", [], [v("X", 0, 512)], T.X[:, 0:512], T.x[:, 0:512])
+    calls[lz][7].add(lu)
+    calls[lx][7].add(lz)
     lw = dma("Y", "ldw", [], [v("qw")], T.qw[:].bitcast(dt.uint8), T.wc[:], (lx, lu))
     dma("Y", "lds", [], [v("sw")], T.sw[:], T.ws[:], (lx, lu))
     dma("Y", "ldv", [], [v("vb")], T.vb[:], T.v[:], (lw,))
@@ -389,7 +401,8 @@ def rank_program(g, core, T, topo):
     for dd, values in (("d2", (FARTHER, 0.0, 0.0)), ("d3", (FARTHER, 0.0, 0.0)), ("d4", (FARTHER, 0.0, 0.0, MID))):
         for k, x in enumerate(values):
             select(v(dd, k, 4 * C, 4), v("one"), [[0, C]], x)
-    select(v("TT", 256, 512), v("one"), [[0, C]], 0.0)
+    for name in ("TT", "ZH"):
+        select(v(name, 256, 512), v("one"), [[0, C]], 0.0)
     fill(v("byw", C, 272), FAR)
     fill(v("m4", 1024, 1040), MID)
     fill(v("rs"), 0.0)
@@ -424,17 +437,19 @@ def rank_program(g, core, T, topo):
         quant("qe", "se", 128 * b, 128 * b + 128, half(v("eb"), b, 4))
     quant("qv", "sv", 0, 128, v("vb"))
     cp(v("nbu"), v("nbi"))
-    for p in range(4):
-        pick("VSSS"[p], half(v("NR"), p, 4), at(v("i1"), half(v("nbu"), p, 4)))
+    for p in range(8):
+        pick("VSSSSSSS"[p], half(v("NR"), p, 8), at(v("i1"), half(v("nbu"), p, 8)))
     for e in range(4):
-        scan(half(v("NC"), e, 4), v("c16"), v("NR", e, 1024, 4), 0.0, A.mult, A.max)
+        for h in range(2):
+            scan(half(v("NC"), 2 * e + h, 8), v("c16", 0, 128), half(v("NR", e, 1024, 4), h), 0.0, A.mult, A.max)
         ts(v("nlf", e, 96, 6), v("NC", C * e + 15, C * e + C, 16), col("cr", 0), A.mult)
     ts(v("nl"), v("NC", 15, 1024, 16), col("cr", 0), A.mult, -1.0, A.add)
     ts(v("nl4"), v("NC", 15, 1024, 16), col("cr", 6), A.mult, -1.0, A.add)
     quant("qu", "su", 0, 128, v("ub"))
     act(v("sur"), at(v("su"), v("ou")), F.Copy)
     op("V", [at(v("qu"), v("ou"))], [v("qur")], lambda q: q.tensor_copy(ap(v("qur"), dt.uint32), ap(at(v("qu"), v("ou")), dt.uint32)))
-    quant("qx", "sx", 0, C, v("X"))
+    for a in (128, 0):
+        quant("qx", "sx", a, a + 128, v("X", 4 * a, 4 * a + 512))
     quant("lq", "ls", 0, 128, v("X", 0, 512))
 
     def own(i, src="H"):
@@ -443,11 +458,11 @@ def rank_program(g, core, T, topo):
     def carried(lo, hi, c0):
         return v("sg", SG * lo + PAD - 1 + c0, SG * (hi - 1) + PAD + c0, SG)
 
-    def scores(c0, c1, one, two):
-        n = max(c1 - c0, 128)
+    def scores(c0, c1, one, two, first=None):
+        first = c1 - 128 if first is None else first
         for x in (one, two):
-            mm(v(x[0], x[1], x[1] + n), "qur", "sur", 0, "qx", "sx", c1 - n, n)
-        return c0, c1, (one[0], one[1] + n - c1), (two[0], two[1] + n - c1)
+            mm(v(x[0], x[1], x[1] + 128), "qur", "sur", 0, "qx", "sx", first, 128)
+        return c0, c1, (one[0], one[1] - first), (two[0], two[1] - first)
 
     def part(x, a, b):
         return v(x[0], x[1] + a, x[1] + b)
@@ -466,14 +481,13 @@ def rank_program(g, core, T, topo):
             a, b = SG * i + PAD, 16 * i + 16
             act(v("sg", a + first - 1, a + b), v("sg", a + first - 1, a + b), F.Relu, acc=col(out, i))
 
-    def v_row(i, pieces, to, a, out, init):
-        first, end = min(p[0] for p in pieces), max(p[1] for p in pieces)
+    def v_row(i, pieces, init):
         for c0, c1, x, _ in pieces:
             b = min(max(16 * i + 16, c0), c1)
             for p, q, o in ((c0, b, A.is_lt), (b, c1, A.is_le)):
                 if p < q:
-                    ts(v(to, a + p - first, a + q - first), part(x, p, q), own(i), o)
-        total(out, to, a, end - first, init)
+                    ts(v("cb", C * i + p, C * i + q), part(x, p, q), own(i), o)
+        total(v("cbo", 128 * i, 128 * i + 128), "cb", C * i, C, init)
 
     def prepare(piece, behind):
         c0, c1, one, two = piece
@@ -486,21 +500,20 @@ def rank_program(g, core, T, topo):
         act(v("nf", c0, c1), part(two, c0, c1), F.Sign, bias=col("mx", c1 - 1), scale=-1.0)
         scan(v("cs", c0, c1), v("nf", c0, c1, -1), v("one", 0, n), col("cs", behind) if behind else 0.0, A.mult, A.add)
 
-    def early():
-        pieces = [scores(128, C, ("pa", 0), ("pb", 0)), scores(K, 128, ("pc", 0), ("pd", 0))]
+    middle = []
+
+    def ranking(t):
+        n0 = K if t else 128
+        pieces = [scores(M if t else 128, C, ("pa", 0), ("pb", 0)), middle.pop() if t else scores(0, 128, ("pc", 0), ("pd", 0))]
         prepare(pieces[0], 0)
         prepare(pieces[1], C - 1)
-        s_rows(4 + NE, 16, pieces, "ab")
-        cp(carried(4 + NE, 16, 0), v("ab", 4 + NE, 16))
-        for i in range(4, 4 + NE):
-            v_row(i, pieces, "ce", M * (i - 4), v("sg", SG * i, SG * i + PAD), own(i, "co"))
-
-    def late(t):
-        nv, n0 = (NV, C) if t == 0 else (4, K)
-        whole = scores(0, C, ("pw", 0), ("pw", 512))
         if t:
-            mm(bank(2, 0, 128), "qur", "sur", 0, "qx", "sx", 0, 128)
-        prepare((0, n0, ("pw", 1024) if t else whole[2], whole[3]), 127 if t else 0)
+            mix(t - 1)
+            pieces.append(scores(0, K, ("pw", 1024), ("pw", 1536), 0))
+            prepare(pieces[2], M - 1)
+            mm(bank(0, 0, C), "qur", "sur", 0, "qx", "sx", 0, C)
+        lo, hi = SROWS[t > 0]
+        mine = [(a, b) for a, b in ((0, lo), (hi, 16)) if a < b]
         start = col("cs", n0 - 1)
         if t:
             act(col("p4", 4 * SPOT - 1), start, F.Copy)
@@ -511,30 +524,28 @@ def rank_program(g, core, T, topo):
         act(last("g2"), v("sn"), F.Abs, scale=FAR)
         ts(v("nn"), v("nlf"), start, A.not_equal, 1.0 if t else float(C), A.mult)
         scan(v("n2"), v("rs"), v("nn"), 0.0, A.add, A.min)
-        counts = v("cbo", 127, 128 * nv, 128)
+        s_rows(lo, hi, pieces, "ab")
         if t == 0:
-            tt(v("ci", 0, nv), v("co", 15, 16 * nv, 16), v("n2", 5, 6 * nv, 6), A.subtract)
-            for i in range(nv):
-                v_row(i, [whole], "cb", C * i, v("cbo", 128 * i, 128 * i + 128), col("ci", i))
-            s_rows(nv, 16, [whole], "ab")
-            ts(v("bcu", 0, nv), counts, -1.0, A.mult, float(C), A.add)
-            tt(v("bc", 0, nv), counts, v("n2", 5, 6 * nv, 6), A.add)
-            ts(v("byu", 0, nv), v("bc", 0, nv), -1.0, A.mult, float(C), A.add)
-            tt(v("bc", nv, 16), v("n2", 6 * nv + 5, 96, 6), v("ab", nv, 16), A.subtract)
-            ts(v("bcu", nv, 16), v("bc", nv, 16), float(C), A.add)
-            ts(v("byu", nv, 16), v("ab", nv, 16), -1.0, A.mult, float(C), A.add)
+            for a, b in mine:
+                counts, marks = v("cbo", 128 * a + 127, 128 * b, 128), v("n2", 6 * a + 5, 6 * b, 6)
+                tt(v("ci", a, b), v("co", 16 * a + 15, 16 * b, 16), marks, A.subtract)
+                for i in range(a, b):
+                    v_row(i, pieces, col("ci", i))
+                ts(v("bcu", a, b), counts, -1.0, A.mult, float(C), A.add)
+                tt(v("bc", a, b), counts, marks, A.add)
+                ts(v("byu", a, b), v("bc", a, b), -1.0, A.mult, float(C), A.add)
+            tt(v("bc", lo, hi), v("n2", 6 * lo + 5, 6 * hi, 6), v("ab", lo, hi), A.subtract)
+            ts(v("bcu", lo, hi), v("bc", lo, hi), float(C), A.add)
+            ts(v("byu", lo, hi), v("ab", lo, hi), -1.0, A.mult, float(C), A.add)
             for p in (1, 0):
                 pick("VS"[p], half(v("q1"), p), at(v("t1"), half(v("bcu"), p)))
             return
         ts(v("pqu"), v("n2", 5, 96, 6), float(C), A.mult)
-        for i in range(nv):
-            v_row(i, [whole], "cb", C * i, v("cbo", 128 * i, 128 * i + 128), own(i, "co"))
-        for i in range(nv, 16):
-            a = SG * i + PAD
-            act(v("sg", a, a + K), part(whole[3], 0, K), F.Sign, bias=own(i), scale=-1.0)
-            act(v("sg", a - 1, a + K), v("sg", a - 1, a + K), F.Relu, acc=col("ab", i))
-        ts(v("byu", 0, nv), counts, -1.0, A.mult, float(C), A.add)
-        ts(v("byu", nv, 16), v("ab", nv, 16), -1.0, A.mult, float(C), A.add)
+        for a, b in mine:
+            for i in range(a, b):
+                v_row(i, pieces if i >= 4 else [(0, C, ("pw", 0), None)], own(i, "co"))
+            ts(v("byu", a, b), v("cbo", 128 * a + 127, 128 * b, 128), -1.0, A.mult, float(C), A.add)
+        ts(v("byu", lo, hi), v("ab", lo, hi), -1.0, A.mult, float(C), A.add)
         for p in (1, 0):
             pick("VS"[p], half(v("byw", 0, C), p), at(v("t1", 0, C), half(v("byu"), p)))
         for p in (1, 0):
@@ -552,17 +563,17 @@ def rank_program(g, core, T, topo):
 
     def order(t):
         for b in range(4):
-            mm(bank(2 + b % 2, 0, C), "qe", "se", 128 * b, "qx", "sx", 0, C)
-            act(v("DX", b, 1024, 4), bank(2 + b % 2, 0, C), F.Copy)
+            mm(bank(1, 0, C), "qe", "se", 128 * b, "qx", "sx", 0, C)
+            act(v("DX", b, 1024, 4), bank(1, 0, C), F.Copy)
         by = at(v("byw", 0, C), v("pu")) if t else at(v("t1", 0, C), v("byu"))
         act(last("d2"), by, F.Copy, scale=2.0 ** -8)
-        act(last("d3"), by, F.Identity, bias=1.0, scale=2.0 ** -16)
+        act(last("d3"), last("d2"), F.Identity, bias=1.0, scale=2.0 ** -8)
         act(last("g4"), last("p4"), F.Identity, bias=2.0 ** 24 - SPOT + MID)
         rank_of = "bnu" if t else "byu"
         if t:
             ts(v("bnu"), listed("bn", last("d3")), col("cr", 0), A.mult, -1.0, A.add)
-        for p in range(NRP):
-            cp(at(v("nr"), half(v("byu"), p, NRP)), half(v(NODE_AT[t]), p, NRP))
+        for a, b in zip(CUTS, CUTS[1:]):
+            cp(at(v("nr"), v("byu", a, b)), v(NODE_AT[t], 16 * a, 16 * b))
         scan(v("cl", 1, C), v("c16", 1, C), v("nr", 1, C), float(SPOT), A.mult, A.max)
         ts(v("rl"), v("cl", 15, C, 16), col("cr", 6), A.mult, -1.0, A.add)
         if t:
@@ -591,8 +602,8 @@ def rank_program(g, core, T, topo):
             ties = v("cob", 16 * lo + 15, 16 * hi, 16)
             if hi - lo > 3:
                 ts(v("e2", lo, hi), ties, 2.0, A.mult, 254.0, A.add)
-                tt(v("e3", lo, hi), v("e2", lo, hi), v("ac", lo, hi), A.subtract)
-                ts(v("npl", lo, hi), v("e3", lo, hi), 0.5, A.mult)
+                tt(v("e1", lo, hi), v("e2", lo, hi), v("ac", lo, hi), A.subtract)
+                ts(v("npl", lo, hi), v("e1", lo, hi), 0.5, A.mult)
             elif lo < hi:
                 ts(v("e2", lo, hi), ties, 127.0, A.add)
                 for i in range(lo, hi):
@@ -604,15 +615,18 @@ def rank_program(g, core, T, topo):
         scan(v("lc", a, b), v("c4", a, b), v(row, a, b), 0.0, A.mult, A.max)
         ts(v(out, a // 4, b // 4), v("lc", a + 3, b, 4), col("cr", 2), A.mult, col("cr", 3), A.add)
 
-    def layer(q_, s_, o, skip, a, b, who, to=("qx", "sx")):
-        for k in range(4):
-            mm(bank(k, 0, 128), "qw", "sw", 128 * k, q_, s_, o, 128)
+    def layer(q_, s_, o, a, b, who, banks=WIDE, tile="X", to=("qx", "sx"), between=None):
+        first = max(b - 128, 0)
+        for k, (name, c) in enumerate(banks):
+            mm(v(name, c, c + 128), "qw", "sw", 128 * k, q_, s_, o, 128)
+            c += a - first
             if who[k] == "V":
-                ts(v("X", 4 * a + k, 4 * b, 4), bank(k, skip, skip + b - a), 0.0, A.max, 0.03125, A.mult)
+                ts(v(tile, 4 * a + k, 4 * b, 4), v(name, c, c + b - a), 0.0, A.max, 0.03125, A.mult)
             else:
-                act(v("X", 4 * a + k, 4 * b, 4), bank(k, skip, skip + b - a), F.Relu, scale=0.03125)
-        a = a // 128 * 128
-        quant(*to, a, a + 128, v("X", 4 * a, 4 * a + 512))
+                act(v(tile, 4 * a + k, 4 * b, 4), v(name, c, c + b - a), F.Relu, scale=0.03125)
+        if between:
+            between()
+        quant(*to, first, first + 128, v(tile, 4 * first, 4 * first + 512))
 
     def move(t, rank_of):
         qt, st = "qt%d" % t, "st%d" % t
@@ -624,52 +638,60 @@ def rank_program(g, core, T, topo):
         to, arr = 128 + K * t, "arr%d" % t
 
         def send():
-            g.remote_dma(ap(v("lq", to, to + K), dt.uint8), ap(v(qt, 0, K), dt.uint8), T.sem[arr], T.sem["sent"], pid, rid, topo.mask(core, nxt))
-            g.remote_dma(ap(v("ls", to, to + K)), ap(v(st, 0, K)), T.sem[arr], T.sem["sent"], pid, rid, topo.mask(core, nxt))
+            g.remote_dma(ap(v("lq", to, to + K), dt.uint8), ap(v(qt, 0, K), dt.uint8), T.sem[arr], T.sem["sent"], pid, rid, mask)
+            g.remote_dma(ap(v("ls", to, to + K)), ap(v(st, 0, K)), T.sem[arr], T.sem["sent"], pid, rid, mask)
             count["sent"] += 2 * n_out
 
-        record("G", [v(qt, 0, K), v(st, 0, K)], [v("lq", to, to + K), v("ls", to, to + K)], send, 500.0, TRAVEL, arr, 2 * n_in)
+        record("G", [v(qt, 0, K), v(st, 0, K)], [v("lq", to, to + K), v("ls", to, to + K)], send, 500.0, TRAVEL[t], arr, 2 * n_in)
         for a, b in ZCUT:
-            act(v("EH", 16 * a, 16 * b), at(v("DX"), v("l4", a, b)), F.Copy)
+            pick("S" if a else "V", v("EH", 16 * a, 16 * b), at(v("DX"), v("l4", a, b)))
             if a < 32:
                 tt(v("Z", 16 * a + 256, 16 * b + 256), at(v("DX"), v("l4", a + 16, b + 16)), v("EH", 16 * a, 16 * b), A.add)
         for k, name in enumerate(("pa", "pb", "pc", "pd")):
             mm(v(name, 0, 128), "qe", "se", 128 * k, qt, st, 0, 128)
             tt(v("Z", 768 + k, 1024, 4), v(name, 0, K), v("EH", 512 + k, 768, 4), A.add)
-        quant("qz", "sz", 0, 128, v("Z", 512, 1024))
-        layer("qz", "sz", 0, 0, 128, C, RELU[0])
-        quant("qz", "sz", 128, C, v("Z", 256, 768))
-        layer("qz", "sz", 128, 0, K, 128, RELU[1])
+        quant("qz", "sz", 0, 128, v("Z", 256, 768))
+        layer("qz", "sz", 0, K, M, RELU[0])
+        quant("qz", "sz", 128, C, v("Z", 512, 1024))
+        layer("qz", "sz", 128, M, C, RELU[1], SINGLE, between=(lambda: middle.append(scores(K, M, ("pc", 0), ("pd", 0)))) if t < R - 1 else None)
         act(v("iq"), at(v("i1"), v("npl")), F.Copy)
         act(last("p4"), at(v("iq"), v(rank_of)), F.Copy)
-        if t:
+        if 0 < t < R - 1:
             ts(v("lu"), listed("l16", v(FROM[t])), col("cr", 0), A.mult, -1.0, A.add)
             act(v(NODE_AT[t + 1]), at(v(NODE_AT[t]), v("lu")), F.Copy)
         if t < R - 1:
             now = listed("pl", last("p4"))
             ts(v("pu"), now, col("cr", 0), A.mult, -1.0, A.add)
             ts(v("rs", 5, 96, 6), now, col("cr", 7), A.mult, -1.0 / C, A.add)
+            if t == R - 2:
+                fourfold("n4", NODE_AT[t + 1], 0, C)
+                for p in range(4):
+                    act(half(v("NA"), p, 4), at(v("NR"), half(v("n4"), p, 4)), F.Copy)
+                for e in range(4):
+                    scan(half(v("NC"), e, 4), v("c16"), v("NA", e, 1024, 4), 0.0, A.mult, A.max)
+                ts(v("n4"), v("NC", 15, 1024, 16), col("cr", 6), A.mult, -1.0, A.add)
         else:
             for e in range(4):
-                act(v("NA", e, 1024, 4), at(v("p4"), half(v("nl4"), e, 4)), F.Copy)
-            fourfold("n4", NODE_AT[R], 0, C)
-            for p in range(2):
-                act(half(v("ON"), p), at(v("NA"), half(v("n4"), p)), F.Identity, bias=-1.0)
-            dma("S", "out", [v("ON")], [], T.on[:], T.ON[0:128:16, :])
+                pick(NAMES[0][e], v("NA", e, 1024, 4), at(v("p4"), half(v("n4"), e, 4)))
+            for p in range(4):
+                if NAMES[1][p] == "V":
+                    ts(half(v("ON"), p, 4), at(v("NA"), half(v("l4"), p, 4)), -1.0, A.add)
+                else:
+                    act(half(v("ON"), p, 4), at(v("NA"), half(v("l4"), p, 4)), F.Identity, bias=-1.0)
+            dma("S", "out", [v("ON")], [], T.on[:], T.ON[0:128:16, :], rows=8)
 
     def mix(t):
-        for b in range(4):
-            name, a = (("pa", "pb", "pc", "pd")[b], 0) if t == R - 1 else ("pw", 512 * b)
+        for b, (name, a) in enumerate(WIDE):
             mm(v(name, a, a + 128), "qe", "se", 128 * b, "lq", "ls", K + K * t, 128)
-            tt(v("Z", b, 256, 4), v(name, a + K, a + 128), v("EH", b, 256, 4), A.add)
-        quant("qh", "sh", 0, 128, v("Z", 0, 512))
-        layer("qh", "sh", 0, 0, 0, K, RELU[2], ("qf", "sf") if t == R - 1 else ("qx", "sx"))
+            tt(v("ZH", b, 256, 4), v(name, a + K, a + 128), v("EH", b, 256, 4), A.add)
+        quant("qh", "sh", 0, 128, v("ZH"))
+        if t == R - 1:
+            layer("qh", "sh", 0, 0, K, RELU[2], WIDE, "TT", ("qf", "sf"))
+        else:
+            layer("qh", "sh", 0, 0, K, RELU[2])
 
     for t in range(R):
-        if t:
-            early()
-            mix(t - 1)
-        late(t)
+        ranking(t)
         move(t, order(t))
 
     def leave(q_, s_, a, b, name, e, first, second):

import numpy as np
from concourse.mybir import dt, AluOpType as A, ActivationFunctionType as F

C, K, R = 256, 64, 3
M = C - K
SROWS = ((9, 16), (4, 12))
NAMES = ("SSVV", "SSVV")
NB = 11
CUTS = (0, 2, 4, 6, 10, 16)
TMP = ((("V", 0, 8), ("V", 8, 16)), (("V", 0, 8), ("S", 8, 16)), (("V", 0, 8), ("S", 8, 16)))
TTE = "VS"
RELU = ("SVSV", "SSSS", "SVSV")
BATCHES = ((12, 16), (0, 8), (8, 12))
ZCUT = ((0, 8), (8, 16), (16, 24), (24, 32), (32, 48))
WAKE, TRAVEL = 220.0, (2000.0, 2000.0, 1500.0)
ENGINES = 8
WIDE, SINGLE = [("pw", 512 * k) for k in range(4)], [(n, 0) for n in ("pa", "pb", "pc", "pd")]
CYC = 0.83
NODE_AT = ("i1", "na1", "na2")
FROM = ("na1", "lr", "lr")
SOFT = 0
ROUNDS = 16000
SEED = 1
REACH = 20
SAMPLE = 30
EVEN = 60.0
STALE = 800
RELAY = 20
PLAN = []
BF, FP, U16, I32, Q4, U8 = "bfloat16", "float32", "uint16", "int32", "float8_e4m3fn_x4", "uint8"
PAD = 16
SG = PAD + C
SIZES = {
    BF: "X 1024 ub 512 vb 512 eb 2048 TT 512 ZH 512 Z 1024 DX 1024 EH 768 kk 32 cc 80 mk 256 nm 256 c16 256 c4 256 i1 256 t1 512 ci 16 "
        "NR 1024 NA 1024 NC 1024 eq 256 co 256 nf 256 cs 256 sn 256 one 256 cb 4096 cbo 2048 sg 4352 byw 272 q1 256 "
        "d2 1024 d3 1024 lr 256 lc 256 iq 256 nr 256 cl 256 kr 256 bn 256 eqb 256 cob 256 rs 96 p4 1040 pl 256 na1 256 na2 256 l16 256 s1 16",
    FP: "cr 10 ln 16 nlf 96 ON 1024 ms 256 H 256 mx 256 nn 96 n2 96 at 16 ab 16 e1 16 e2 16 ac 16 lb 16 bc 16 "
        "d4 1024 g2 1024 g4 1024 m2 1024 m3 1024 m4 1040 tf 256 mb 256 Hb 256 W 512 ys 256",
    U16: "nbu 64 oa 16 ou 8 nl 64 nl4 64 byu 16 bcu 16 rl 16 npl 16 l4 64 n4 64 pu 16 pqu 16 bnu 16 lu 16 cu 2",
    I32: "nbi 64 di 48 dj 64",
    Q4: "qu 128 qur 128 qv 128 qw 512 qe 512 qx 256 qz 256 qh 128 qf 128 qt0 128 qt1 128 qt2 128 lq 320",
    U8: "su 128 sur 128 sv 128 sw 512 se 512 sx 256 sz 256 sh 128 sf 128 st0 128 st1 128 st2 128 ls 320",
}
SCRATCH = {n: ("sbuf", [128, int(w)], d) for d, s in SIZES.items() for n, w in zip(s.split()[0::2], s.split()[1::2])}
SCRATCH.update({n: ("psum", [128, w], FP) for n, w in (("pw", 2048), ("pa", 512), ("pb", 512), ("pc", 512), ("pd", 512))})
SEMAPHORES = ["V", "S", "P", "G", "ldx", "ldy", "ldt", "ldu", "ldn", "ldw", "lds", "ldv", "out", "sent", "arr0", "arr1", "arr2"]


def v(name, a=0, b=None, s=1):
    return (name, a, SCRATCH[name][1][1] if b is None else b, s, None)


def at(win, off):
    return win[:4] + (off,)


def col(name, a):
    return v(name, a, a + 1)


def half(x, h, parts=2):
    n = len(span(x)) // parts
    return (x[0], x[1] + h * n * x[3], x[1] + (h * n + n - 1) * x[3] + 1, x[3], None)


def span(x):
    return range(x[1], x[2], x[3]) if x[3] > 0 else range(x[2] - 1, x[1] - 1, x[3])


def length(x):
    return 16 * len(span(x[4])) if x[4] else len(span(x))


def plan(calls):
    n = len(calls)
    on, cost, late = [c[0] for c in calls], [c[3] for c in calls], [c[4] for c in calls]
    need, after, behind = [], [[] for _ in calls], []
    for i in range(n):
        mask, keep = 0, [(j, cost[j]) for j in calls[i][7]]
        for j in sorted(calls[i][1], reverse=True):
            if not mask >> j & 1:
                keep.append((j, cost[j] + late[j] + WAKE))
                mask |= behind[j]
        for j, lag in keep:
            after[j].append((i, lag))
        need.append(keep)
        behind.append(mask | 1 << i)

    def lay(turn, back):
        begin, lines = [0.0] * n, {e: ([], []) for e in on}
        for i in turn:
            if back:
                t = max([begin[j] + cost[j] + lag - cost[i] for j, lag in after[i]] + [late[i]])
            else:
                t = max([begin[j] + lag for j, lag in need[i]] + [0.0])
            (a, b), c = lines[on[i]], cost[i]
            k = len(b)
            while k and b[k - 1] > t:
                k -= 1
            while k < len(a) and a[k] < t + c:
                t, k = max(t, b[k]), k + 1
            a.insert(k, t)
            b.insert(k, t + c)
            begin[i] = t
        return begin

    def line_up(begin):
        last = {}
        for i in sorted(range(n), key=lambda i: (begin[i], i)):
            prev[i], nxt[i] = last.get(on[i], -1), -1
            if prev[i] >= 0:
                nxt[prev[i]] = i
            last[on[i]] = i

    def times():
        left = [len(need[i]) + (prev[i] >= 0) for i in range(n)]
        turn, free, begin, own, rest = [i for i in range(n) if not left[i]], [0.0] * n, [0.0] * n, [0.0] * n, [0.0] * n
        for i in turn:
            p, t = prev[i], free[i]
            if p >= 0 and begin[p] + cost[p] > t:
                t = begin[p] + cost[p]
            begin[i] = t
            for j, lag in after[i]:
                if t + lag > free[j]:
                    free[j] = t + lag
                left[j] -= 1
                if not left[j]:
                    turn.append(j)
            j = nxt[i]
            if j >= 0:
                left[j] -= 1
                if not left[j]:
                    turn.append(j)
        if len(turn) < n:
            return None
        for i in reversed(turn):
            t = cost[i] + late[i]
            for j, lag in after[i]:
                if lag + rest[j] > t:
                    t = lag + rest[j]
            own[i], j = t, nxt[i]
            rest[i] = cost[i] + rest[j] if j >= 0 and cost[i] + rest[j] > t else t
        return max(rest), begin, free, rest, own

    def relaid(begin):
        back = lay(sorted(range(n), key=lambda i: (-begin[i] - cost[i], -i)), True)
        return lay(sorted(range(n), key=lambda i: (-back[i] - cost[i], i)), False)

    prev, nxt, rng = [-1] * n, [-1] * n, np.random.default_rng(SEED)
    rest = times()[3]
    line_up(relaid(lay(sorted(range(n), key=lambda i: (-rest[i], i)), False)))
    now = best = times()
    barred, stale = {}, 0
    for step in range(ROUNDS):
        whole, begin, free, rest, own = now
        i = max(range(n), key=lambda k: rest[k])
        runs = [[i]]
        while True:
            j, on_path = nxt[i], [k for k, lag in after[i] if abs(lag + rest[k] - rest[i]) < 1e-6]
            if j >= 0 and abs(cost[i] + rest[j] - rest[i]) < 1e-6:
                runs[-1].append(j)
            elif on_path:
                j = on_path[0]
                runs.append([j])
            else:
                break
            i = j
        moves = [(b, x, y, back) for b in runs for x in range(len(b) - 1) for y in range(x + 1, min(len(b), x + REACH + 1))
                 if x == 0 or y == len(b) - 1 or y == x + 1 for back in range(1 + (y > x + 1))]
        chosen = None
        for k in rng.integers(len(moves), size=SAMPLE).tolist():
            b, x, y, back = moves[k]
            u, w = b[x], b[y]
            if back:
                if any(begin[j] + cost[j] > begin[u] + cost[u] or j == u for j, _ in need[w]):
                    continue
                new, pairs = [w] + b[x:y], [(w, j) for j in b[x:y]]
            else:
                if any(rest[j] > rest[w] or j == w for j, _ in after[u]):
                    continue
                new, pairs = b[x + 1:y + 1] + [u], [(j, u) for j in b[x + 1:y + 1]]
            if any(barred.get(p, -1) > step for p in pairs):
                continue
            t, heads = begin[prev[u]] + cost[prev[u]] if prev[u] >= 0 else 0.0, []
            for j in new:
                t = max(t, free[j])
                heads.append(t)
                t += cost[j]
            t, longest = rest[nxt[w]] if nxt[w] >= 0 else 0.0, 0.0
            for j, h in zip(new[::-1], heads[::-1]):
                t = max(t + cost[j], own[j])
                longest = max(longest, h + t)
            d = longest - whole
            d = d if d < -0.5 else float(rng.exponential(1.0)) * (EVEN if d < 0.5 else d)
            if chosen is None or d < chosen[0]:
                chosen = (d, [prev[u]] + new + [nxt[w]], pairs)
        if chosen is None:
            continue
        for j, k in zip(chosen[1], chosen[1][1:]):
            if j >= 0:
                nxt[j] = k
            if k >= 0:
                prev[k] = j
        for j, k in chosen[2]:
            barred[k, j] = step + 8 + int(rng.integers(8))
        now, stale = times(), stale + 1
        if now and step % RELAY == 0:
            line_up(relaid(now[1]))
            new = times()
            if new[0] <= now[0]:
                now = new
            else:
                line_up(now[1])
        if now and now[0] < best[0]:
            best, stale = now, 0
        if now is None or stale > STALE:
            line_up(best[1])
            now, stale = times(), 0
    return sorted(range(n), key=lambda i: (best[1][i], i))


def rank_program(g, core, T, topo):
    rank = T.rank_of(core)
    if rank is None:
        return
    n_ranks = len(T.cores)
    nxt, prv = T.cores[(rank + 1) % n_ranks], T.cores[(rank - 1) % n_ranks]
    rid, pid = topo.addr(nxt)[:2]


    def engines(src, dst):
        e = topo.engines(src, dst)
        return e[::max(1, len(e) // ENGINES)]

    n_out, n_in, mask = len(engines(core, nxt)), len(engines(prv, core)), sum(1 << e for e in engines(core, nxt))

    queue = {"V": g.vector, "S": g.scalar, "P": g.tensor, "G": g, "Y": g.sync}
    count = {s: 0 for s in SEMAPHORES}
    known = {e: {} for e in queue}
    calls = []
    writer = {n: [-1] * d[1][1] for n, d in SCRATCH.items()}
    readers = {n: [[] for _ in range(d[1][1])] for n, d in SCRATCH.items()}
    banks = {}

    def ap(x, word=None):
        if not isinstance(x, tuple):
            return x
        name, a, b, s, off = x
        if s > 0:
            t = T[name][:, a:b:s] if s > 1 else T[name][:, a:b]
        else:
            t = T[name][:, b - 1:a - 1:s] if a else T[name][:, b - 1::s]
        if word is not None:
            t = t.bitcast(word)
        return t.indirect(ap(off)) if off else t

    def record(e, r, w, fn, cost, late, sem, n, after=()):
        me, need, turn = len(calls), set(after), set()
        r = [x for x in r if isinstance(x, tuple)]
        r += [x[4] for x in r + w if x[4]]
        for x in r:
            need.update(writer[x[0]][c] for c in span(x))
        for x in w:
            turn.update(writer[x[0]][c] for c in span(x))
        for x in r + w:
            if SCRATCH[x[0]][0] == "psum":
                for b in {c // 512 for c in span(x)}:
                    users = banks.setdefault((x[0], b), [])
                    need.update(i for i in users if calls[i][0] != e)
                    users.append(me)
        for x in w:
            for c in span(x):
                turn.update(readers[x[0]][c])
        for x in r:
            for c in span(x):
                readers[x[0]][c].append(me)
        for x in w:
            for c in span(x):
                writer[x[0]][c], readers[x[0]][c] = me, []
        turn -= need | {-1, me}
        need.update(i for i in turn if calls[i][0] != e or calls[i][4] or late or not SOFT)
        calls.append((e, need - {-1, me}, fn, cost, late, sem, n, turn - need))
        return me

    def op(e, r, w, fn, rate=None, more=0.0):
        full = [x for x in r + w if isinstance(x, tuple)]
        n = length(full[0])
        if rate is None:
            rate = 0.5 if e == "V" and all(SCRATCH[x[0]][2] in (BF, U16) for x in full) else 1.0
        cost = max(64.0, n * rate) * CYC
        if r and r[0][4]:
            cost = (50 if e == "V" else 65) + 1.56 * CYC * n
        if w[0][4]:
            cost = 50 + 3.8 * CYC * n
        return record(e, r, w, lambda: fn(queue[e]).then_inc(T.sem[e], 1), cost + more, 0.0, e, 1)

    def dma(e, sem, r, w, out, in_, after=(), rows=128):
        x = (r + w)[0]
        size = len(span(x)) * {BF: 2, U8: 1}.get(SCRATCH[x[0]][2], 4)
        return record(e, r, w, lambda: queue[e].dma_start(out, in_).then_inc(T.sem[sem], 16), 60.0, 2000.0 + 0.005 * rows * size, sem, 16, after)

    def issue():
        if not PLAN:
            PLAN.extend(plan(calls))
        event, clock = {}, {}
        for i in PLAN:
            e, need, fn, cost, late, sem, inc, _ = calls[i]
            for ev in sorted({event[j] for j in need}, key=lambda ev: (-ev[1], ev[0])):
                if known[e].get(ev[0], 0) < ev[1]:
                    queue[e].wait_ge(T.sem[ev[0]], ev[1])
                    for s, c in clock[ev].items():
                        known[e][s] = max(known[e].get(s, 0), c)
            fn()
            count[sem] += inc
            event[i] = (sem, count[sem])
            clock[event[i]] = dict(known[e]) if sem[:3] != "arr" else {}
            clock[event[i]][sem] = count[sem]

    def ts(out, in0, s1, op0, s2=None, op1=None):
        if op1 is None:
            return op("V", [in0, s1], [out], lambda q: q.tensor_scalar(ap(out), ap(in0), ap(s1), None, op0))
        return op("V", [in0, s1, s2], [out], lambda q: q.tensor_scalar(ap(out), ap(in0), ap(s1), ap(s2), op0, op1))

    def tt(out, a, b, o):
        rate = 1.0 if "psum" in (SCRATCH[a[0]][0], SCRATCH[b[0]][0]) else 2.0
        return op("V", [a, b], [out], lambda q: q.tensor_tensor(ap(out), ap(a), ap(b), o), rate)

    def cp(out, a):
        return op("V", [a], [out], lambda q: q.tensor_copy(ap(out), ap(a)))

    def scan(out, a, b, init, o0, o1):
        return op("V", [a, b, init], [out], lambda q: q.tensor_tensor_scan(ap(out), ap(a), ap(b), ap(init), o0, o1))

    def total(out, src, a, n, init):
        return scan(out, v(src, a, a + n // 2), v(src, a + n // 2, a + n), init, A.add, A.add)

    def fill(out, c):
        return op("V", [], [out], lambda q: q.memset(ap(out), c))

    def act(out, a, f, bias=0.0, scale=1.0, acc=None):
        given = {k: x for k, x, usual in (("bias", bias, 0.0), ("scale", scale, 1.0), ("accum_out", acc, None)) if x != usual}
        return op("S", [a, bias, scale], [out, acc] if acc else [out],
                  lambda q: q.activation(ap(out), ap(a), f, **{k: ap(x) for k, x in given.items()}), more=20.0 if acc else 0.0)

    def quant(q_, s_, a, b, src):
        return record("V", [src], [v(q_, a, b), v(s_, a, b)],
                      lambda: g.vector.quantize_mx(ap(v(q_, a, b)), ap(v(s_, a, b)), ap(src)).then_inc(T.sem["V"], 1),
                      12 + 0.22 * length(src), 0.0, "V", 1)

    def mm(out, lq, ls, l0, rq, rs, r0, n):
        sides = [v(lq, l0, l0 + 128), v(ls, l0, l0 + 128), v(rq, r0, r0 + n), v(rs, r0, r0 + n)]
        return record("P", sides, [out], lambda: g.tensor.matmul_mx(ap(out), *[ap(x) for x in sides], True, True).then_inc(T.sem["P"], 1),
                      0.6 * (n + 16), 0.0, "P", 1)

    def table(out, pat, base, cm=0):
        if SCRATCH[out[0]][2] == I32:
            return op("G", [], [out], lambda q: q.iota(ap(out), pat, base, cm), 2.0, 130.0)
        return op("G", [], [out], lambda q: q.iota(ap(out), pat, base, cm, allow_small_or_imprecise_dtypes=True), 2.0, 130.0)

    def select(out, a, pat, x, cm=0):
        return op("G", [a], [out], lambda q: q.affine_select(ap(out), ap(a), pat, A.not_equal, x, 0, cm), 2.0, 170.0)

    def bank(b, a, n):
        return v("pw", 512 * b + a, 512 * b + n)

    def pick(e, out, win):
        return cp(out, win) if e == "V" else act(out, win, F.Copy)

    def listed(tmp, row):
        scan(v(tmp), v("c16"), row, 0.0, A.mult, A.max)
        return v(tmp, 15, C, 16)

    def last(name):
        return v(name, 3, 4 * C, 4)

    BIG = 2.0 ** 30
    FAR, FARTHER = 2.0 ** 25, 2.0 ** 28
    MID = 1.0 - 2.0 ** 23
    SPOT = 258
    lt = dma("S", "ldt", [], [v("ub", 256, 512)], T.ub[:, 256:512], T.u[:, 256:512])
    calls[dma("S", "ldn", [], [v("nbi")], T.nbi[:], T.nb[:])][7].add(lt)
    lu = dma("Y", "ldu", [], [v("ub", 0, 256)], T.ub[:, 0:256], T.u[:, 0:256])
    lz = dma("Y", "ldx", [], [v("X", 512, 1024)], T.X[:, 512:1024], T.x[:, 512:1024])
    lx = dma("Y", "ldy", [], [v("X", 0, 512)], T.X[:, 0:512], T.x[:, 0:512])
    calls[lz][7].add(lu)
    calls[lx][7].add(lz)
    lw = dma("Y", "ldw", [], [v("qw")], T.qw[:].bitcast(dt.uint8), T.wc[:], (lx, lu))
    dma("Y", "lds", [], [v("sw")], T.sw[:], T.ws[:], (lx, lu))
    dma("Y", "ldv", [], [v("vb")], T.vb[:], T.v[:], (lw,))
    table(v("di", 0, 16), [[1, 16]], 128, -1)
    table(v("di", 32, 48), [[0, 16]], 0, 1)
    table(v("ln"), [[16, 16]], 16)
    table(v("lb"), [[-16, 16]], C - 16)
    table(v("di", 16, 32), [[4, 16]], 131, -1)
    table(v("i1"), [[1, C]], 1)
    table(v("p4"), [[1, 260], [0, 4]], 1)
    fill(v("one"), 1.0)
    fill(v("eb"), 0.0)
    for b in range(4):
        select(v("eb", 513 * b, 512 * b + 512, 4), v("eb", 513 * b, 512 * b + 512, 4), [[-1, 128]], 0.5, 1)
    for dd, values in (("d2", (FARTHER, 0.0, 0.0)), ("d3", (FARTHER, 0.0, 0.0)), ("d4", (FARTHER, 0.0, 0.0, MID))):
        for k, x in enumerate(values):
            select(v(dd, k, 4 * C, 4), v("one"), [[0, C]], x)
    for name in ("TT", "ZH"):
        select(v(name, 256, 512), v("one"), [[0, C]], 0.0)
    fill(v("byw", C, 272), FAR)
    fill(v("m4", 1024, 1040), MID)
    fill(v("rs"), 0.0)
    fill(v("rs", 0, 96, 6), FAR)
    fill(v("nlf", 5, 96, 6), -1.0)
    fill(col("at", 15), 0.0)
    select(v("t1", C, 2 * C), v("one"), [[0, C]], FAR)
    act(v("t1", 0, C), v("i1"), F.Identity, bias=-65536.0, scale=65536.0)
    ts(v("dj", 0, 16), v("di", 0, 16), 15, A.bitwise_and)
    ts(v("dj", 32, 48), v("di", 32, 48), 15, A.bitwise_and)
    ts(v("cc", 0, 16), v("dj", 0, 16), 0.0, A.is_equal)
    cp(v("oa"), v("dj", 32, 48))
    ts(v("dj", 16, 32), v("di", 16, 32), 2, A.arith_shift_right, 3, A.bitwise_and)
    ts(v("ou"), v("ln", 0, 8), -16.0, A.add)
    ts(v("cc", 16, 48), v("dj", 0, 32), 0.0, A.not_equal)
    ts(col("dj", 48), col("di", 32), 3, A.bitwise_and)
    act(v("mk"), at(v("cc", 0, 16), v("oa")), F.Copy)
    act(v("nm"), at(v("cc", 16, 32), v("oa")), F.Copy)
    ts(v("kk"), v("dj", 0, 32), 1.0, A.is_equal, BIG, A.mult)
    ts(col("cr", 0), col("dj", 15), 0.0, A.is_equal, 1 / BIG, A.max)
    ts(col("cr", 1), col("dj", 19), 0.0, A.is_equal, 1 / BIG, A.max)
    tt(v("cc", 48, 80), v("kk"), v("cc", 16, 48), A.max)
    ts(col("cr", 3), col("dj", 48), -4.0, A.add)
    ts(col("cr", 4), col("dj", 32), -15.0, A.add)
    ts(col("cr", 2), col("cr", 1), 4.0, A.mult)
    ts(col("cr", 6), col("cr", 0), 4.0, A.mult)
    ts(col("cr", 7), col("cr", 0), 1.0 / C, A.mult)
    ts(v("nlf", 4, 96, 6), v("ln"), col("cr", 4), A.add)
    act(v("c16"), at(v("cc", 48, 64), v("oa")), F.Copy)
    act(v("c4"), at(v("cc", 64, 80), v("oa")), F.Copy)
    for b in range(4):
        quant("qe", "se", 128 * b, 128 * b + 128, half(v("eb"), b, 4))
    quant("qv", "sv", 0, 128, v("vb"))
    cp(v("nbu"), v("nbi"))
    for p in range(8):
        pick("VSSSSSSS"[p], half(v("NR"), p, 8), at(v("i1"), half(v("nbu"), p, 8)))
    for e in range(4):
        for h in range(2):
            scan(half(v("NC"), 2 * e + h, 8), v("c16", 0, 128), half(v("NR", e, 1024, 4), h), 0.0, A.mult, A.max)
        ts(v("nlf", e, 96, 6), v("NC", C * e + 15, C * e + C, 16), col("cr", 0), A.mult)
    ts(v("nl"), v("NC", 15, 1024, 16), col("cr", 0), A.mult, -1.0, A.add)
    ts(v("nl4"), v("NC", 15, 1024, 16), col("cr", 6), A.mult, -1.0, A.add)
    quant("qu", "su", 0, 128, v("ub"))
    act(v("sur"), at(v("su"), v("ou")), F.Copy)
    op("V", [at(v("qu"), v("ou"))], [v("qur")], lambda q: q.tensor_copy(ap(v("qur"), dt.uint32), ap(at(v("qu"), v("ou")), dt.uint32)))
    for a in (128, 0):
        quant("qx", "sx", a, a + 128, v("X", 4 * a, 4 * a + 512))
    quant("lq", "ls", 0, 128, v("X", 0, 512))

    def own(i, src="H"):
        return col(src, 16 * i + 15)

    def carried(lo, hi, c0):
        return v("sg", SG * lo + PAD - 1 + c0, SG * (hi - 1) + PAD + c0, SG)

    def scores(c0, c1, one, two, first=None):
        first = c1 - 128 if first is None else first
        for x in (one, two):
            mm(v(x[0], x[1], x[1] + 128), "qur", "sur", 0, "qx", "sx", first, 128)
        return c0, c1, (one[0], one[1] - first), (two[0], two[1] - first)

    def part(x, a, b):
        return v(x[0], x[1] + a, x[1] + b)

    def s_rows(lo, hi, pieces, out):
        first = min(p[0] for p in pieces)
        for i in range(lo, hi):
            a, b = SG * i + PAD, 16 * i + 16
            for c0, c1, _, x in pieces:
                act(v("sg", a + c0, a + c1), part(x, c0, c1), F.Sign, bias=own(i), scale=-1.0)
            if i < 15:
                act(v("sg", a + b, a + C), v("sg", a + b, a + C), F.Relu, scale=-1.0, acc=col("at", i))
        tt(v("e1", lo, hi), v("lb", lo, hi), v("co", 16 * lo + 15, 16 * hi, 16), A.add)
        tt(carried(lo, hi, first), v("e1", lo, hi), v("at", lo, hi), A.subtract)
        for i in range(lo, hi):
            a, b = SG * i + PAD, 16 * i + 16
            act(v("sg", a + first - 1, a + b), v("sg", a + first - 1, a + b), F.Relu, acc=col(out, i))

    def v_row(i, pieces, init):
        for c0, c1, x, _ in pieces:
            b = min(max(16 * i + 16, c0), c1)
            for p, q, o in ((c0, b, A.is_lt), (b, c1, A.is_le)):
                if p < q:
                    ts(v("cb", C * i + p, C * i + q), part(x, p, q), own(i), o)
        total(v("cbo", 128 * i, 128 * i + 128), "cb", C * i, C, init)

    def prepare(piece, behind):
        c0, c1, one, two = piece
        src, n = part(one, c0, c1), c1 - c0
        tt(v("ms", c0, c1), src, v("mk", 0, n), A.mult)
        scan(v("H", c0, c1), v("nm", 0, n), v("ms", c0, c1), 0.0, A.mult, A.add)
        tt(v("eq", c0, c1), v("H", c0, c1), src, A.is_equal)
        scan(v("co", c0, c1), v("nm", 0, n), v("eq", c0, c1), 0.0, A.mult, A.add)
        scan(v("mx", c0, c1), src, v("one", 0, n), col("mx", behind) if behind else -BIG ** 3, A.max, A.mult)
        act(v("nf", c0, c1), part(two, c0, c1), F.Sign, bias=col("mx", c1 - 1), scale=-1.0)
        scan(v("cs", c0, c1), v("nf", c0, c1, -1), v("one", 0, n), col("cs", behind) if behind else 0.0, A.mult, A.add)

    middle = []

    def ranking(t):
        n0 = K if t else 128
        pieces = [scores(M if t else 128, C, ("pa", 0), ("pb", 0)), middle.pop() if t else scores(0, 128, ("pc", 0), ("pd", 0))]
        prepare(pieces[0], 0)
        prepare(pieces[1], C - 1)
        if t:
            mix(t - 1)
            pieces.append(scores(0, K, ("pw", 1024), ("pw", 1536), 0))
            prepare(pieces[2], M - 1)
            mm(bank(0, 0, C), "qur", "sur", 0, "qx", "sx", 0, C)
        lo, hi = SROWS[t > 0]
        mine = [(a, b) for a, b in ((0, lo), (hi, 16)) if a < b]
        start = col("cs", n0 - 1)
        if t:
            act(col("p4", 4 * SPOT - 1), start, F.Copy)
            ts(col("cu", 0), start, -1.0, A.add)
            act(v("s1"), at(v(NODE_AT[t]), col("cu", 0)), F.Copy)
            start = col("s1", 0)
        act(v("sn"), v("i1"), F.Sign, bias=start, scale=-1.0)
        act(last("g2"), v("sn"), F.Abs, scale=FAR)
        ts(v("nn"), v("nlf"), start, A.not_equal, 1.0 if t else float(C), A.mult)
        scan(v("n2"), v("rs"), v("nn"), 0.0, A.add, A.min)
        s_rows(lo, hi, pieces, "ab")
        if t == 0:
            for a, b in mine:
                counts, marks = v("cbo", 128 * a + 127, 128 * b, 128), v("n2", 6 * a + 5, 6 * b, 6)
                tt(v("ci", a, b), v("co", 16 * a + 15, 16 * b, 16), marks, A.subtract)
                for i in range(a, b):
                    v_row(i, pieces, col("ci", i))
                ts(v("bcu", a, b), counts, -1.0, A.mult, float(C), A.add)
                tt(v("bc", a, b), counts, marks, A.add)
                ts(v("byu", a, b), v("bc", a, b), -1.0, A.mult, float(C), A.add)
            tt(v("bc", lo, hi), v("n2", 6 * lo + 5, 6 * hi, 6), v("ab", lo, hi), A.subtract)
            ts(v("bcu", lo, hi), v("bc", lo, hi), float(C), A.add)
            ts(v("byu", lo, hi), v("ab", lo, hi), -1.0, A.mult, float(C), A.add)
            for p in (1, 0):
                pick("VS"[p], half(v("q1"), p), at(v("t1"), half(v("bcu"), p)))
            return
        ts(v("pqu"), v("n2", 5, 96, 6), float(C), A.mult)
        for a, b in mine:
            for i in range(a, b):
                v_row(i, pieces if i >= 4 else [(0, C, ("pw", 0), None)], own(i, "co"))
            ts(v("byu", a, b), v("cbo", 128 * a + 127, 128 * b, 128), -1.0, A.mult, float(C), A.add)
        ts(v("byu", lo, hi), v("ab", lo, hi), -1.0, A.mult, float(C), A.add)
        for p in (1, 0):
            pick("VS"[p], half(v("byw", 0, C), p), at(v("t1", 0, C), half(v("byu"), p)))
        for p in (1, 0):
            pick("VS"[p], half(v("q1"), p), at(v("byw"), half(v("pqu"), p)))

    def step(tab, lists, gg, dd, mo, who):
        for one, lo, hi in who:
            a, b = 64 * lo, 64 * hi
            e = [at(tab, v(lists, 16 * k + lo, 16 * k + hi)) for k in range(4)]
            act(v(gg, a + 1, b, 4), e[2], F.Copy)
            act(v(gg, a + 2, b, 4), e[3], F.Copy)
            pick(one, v("tf", 16 * lo, 16 * hi), e[0])
            tt(v(gg, a, b, 4), e[1], v("tf", 16 * lo, 16 * hi), A.min)
            scan(v(mo, a, b), v(dd, a, b), v(gg, a, b), 0.0, A.add, A.min)

    def order(t):
        for b in range(4):
            mm(bank(1, 0, C), "qe", "se", 128 * b, "qx", "sx", 0, C)
            act(v("DX", b, 1024, 4), bank(1, 0, C), F.Copy)
        by = at(v("byw", 0, C), v("pu")) if t else at(v("t1", 0, C), v("byu"))
        act(last("d2"), by, F.Copy, scale=2.0 ** -8)
        act(last("d3"), last("d2"), F.Identity, bias=1.0, scale=2.0 ** -8)
        act(last("g4"), last("p4"), F.Identity, bias=2.0 ** 24 - SPOT + MID)
        rank_of = "bnu" if t else "byu"
        if t:
            ts(v("bnu"), listed("bn", last("d3")), col("cr", 0), A.mult, -1.0, A.add)
        for a, b in zip(CUTS, CUTS[1:]):
            cp(at(v("nr"), v("byu", a, b)), v(NODE_AT[t], 16 * a, 16 * b))
        scan(v("cl", 1, C), v("c16", 1, C), v("nr", 1, C), float(SPOT), A.mult, A.max)
        ts(v("rl"), v("cl", 15, C, 16), col("cr", 6), A.mult, -1.0, A.add)
        if t:
            act(v("kr"), at(v("p4"), v("rl")), F.Copy)
        step(v("q1"), "nl", "g2", "d2", "m2", TMP[0])
        step(v("m2"), "nl4", "g2", "d3", "m3", TMP[1])
        step(v("m3"), "nl4", "g4", "d4", "m4", TMP[2])
        for h in range(2):
            tt(half(v("mb"), h), at(v("m4"), half(v("rl"), h)), half(v("mk"), h), A.mult)
            scan(half(v("Hb"), h), half(v("nm"), h), half(v("mb"), h), 0.0, A.mult, A.add)
            act(half(v("W"), h, 4), at(v("m4"), half(v("rl"), h)), F.Identity, bias=0.5)
            act(half(v("W"), 2 + h, 4), half(v("W"), h, 4), F.Identity, bias=-1.0)
            tt(half(v("eqb"), h), at(v("m4"), half(v("rl"), h)), half(v("Hb"), h), A.is_equal)
        scan(v("cob"), v("nm"), v("eqb"), 0.0, A.mult, A.add)
        for i in range(16):
            if i < NB:
                act(v("sg", SG * i, SG * i + C), v("W", 16 * i + 16, 16 * i + 16 + C), F.Sign, bias=own(i, "Hb"), scale=-1.0, acc=col("ac", i))
            else:
                ts(v("cb", C * i, C * i + C), v("W", 16 * i + 16, 16 * i + 16 + C), own(i, "Hb"), A.is_gt)
                total(v("cbo", 128 * i, 128 * i + 128), "cb", C * i, C, own(i, "cob"))
        for first, end in BATCHES:
            lo, hi = max(first, NB), end
            if lo < hi:
                ts(v("npl", lo, hi), v("cbo", 128 * lo + 127, 128 * hi, 128), -1.0, A.add)
            lo, hi = first, min(end, NB)
            ties = v("cob", 16 * lo + 15, 16 * hi, 16)
            if hi - lo > 3:
                ts(v("e2", lo, hi), ties, 2.0, A.mult, 254.0, A.add)
                tt(v("e1", lo, hi), v("e2", lo, hi), v("ac", lo, hi), A.subtract)
                ts(v("npl", lo, hi), v("e1", lo, hi), 0.5, A.mult)
            elif lo < hi:
                ts(v("e2", lo, hi), ties, 127.0, A.add)
                for i in range(lo, hi):
                    ts(col("npl", i), col("ac", i), -0.5, A.mult, col("e2", i), A.add)
            cp(at(v(FROM[t]), v("npl", first, end)), v("kr" if t else "nr", 16 * first, 16 * end))
        return rank_of

    def fourfold(out, row, a, b):
        scan(v("lc", a, b), v("c4", a, b), v(row, a, b), 0.0, A.mult, A.max)
        ts(v(out, a // 4, b // 4), v("lc", a + 3, b, 4), col("cr", 2), A.mult, col("cr", 3), A.add)

    def layer(q_, s_, o, a, b, who, banks=WIDE, tile="X", to=("qx", "sx"), between=None):
        first = max(b - 128, 0)
        for k, (name, c) in enumerate(banks):
            mm(v(name, c, c + 128), "qw", "sw", 128 * k, q_, s_, o, 128)
            c += a - first
            if who[k] == "V":
                ts(v(tile, 4 * a + k, 4 * b, 4), v(name, c, c + b - a), 0.0, A.max, 0.03125, A.mult)
            else:
                act(v(tile, 4 * a + k, 4 * b, 4), v(name, c, c + b - a), F.Relu, scale=0.03125)
        if between:
            between()
        quant(*to, first, first + 128, v(tile, 4 * first, 4 * first + 512))

    def move(t, rank_of):
        qt, st = "qt%d" % t, "st%d" % t
        fourfold("l4", FROM[t], M, C)
        fourfold("l4", FROM[t], 0, M)
        for p in (1, 0):
            pick(TTE[p], v("TT", 128 * p, 128 * p + 128), at(v("X"), v("l4", 48 + 8 * p, 56 + 8 * p)))
        quant(qt, st, 0, 128, v("TT"))
        to, arr = 128 + K * t, "arr%d" % t

        def send():
            g.remote_dma(ap(v("lq", to, to + K), dt.uint8), ap(v(qt, 0, K), dt.uint8), T.sem[arr], T.sem["sent"], pid, rid, mask)
            g.remote_dma(ap(v("ls", to, to + K)), ap(v(st, 0, K)), T.sem[arr], T.sem["sent"], pid, rid, mask)
            count["sent"] += 2 * n_out

        record("G", [v(qt, 0, K), v(st, 0, K)], [v("lq", to, to + K), v("ls", to, to + K)], send, 500.0, TRAVEL[t], arr, 2 * n_in)
        for a, b in ZCUT:
            pick("S" if a else "V", v("EH", 16 * a, 16 * b), at(v("DX"), v("l4", a, b)))
            if a < 32:
                tt(v("Z", 16 * a + 256, 16 * b + 256), at(v("DX"), v("l4", a + 16, b + 16)), v("EH", 16 * a, 16 * b), A.add)
        for k, name in enumerate(("pa", "pb", "pc", "pd")):
            mm(v(name, 0, 128), "qe", "se", 128 * k, qt, st, 0, 128)
            tt(v("Z", 768 + k, 1024, 4), v(name, 0, K), v("EH", 512 + k, 768, 4), A.add)
        quant("qz", "sz", 0, 128, v("Z", 256, 768))
        layer("qz", "sz", 0, K, M, RELU[0])
        quant("qz", "sz", 128, C, v("Z", 512, 1024))
        layer("qz", "sz", 128, M, C, RELU[1], SINGLE, between=(lambda: middle.append(scores(K, M, ("pc", 0), ("pd", 0)))) if t < R - 1 else None)
        act(v("iq"), at(v("i1"), v("npl")), F.Copy)
        act(last("p4"), at(v("iq"), v(rank_of)), F.Copy)
        if 0 < t < R - 1:
            ts(v("lu"), listed("l16", v(FROM[t])), col("cr", 0), A.mult, -1.0, A.add)
            act(v(NODE_AT[t + 1]), at(v(NODE_AT[t]), v("lu")), F.Copy)
        if t < R - 1:
            now = listed("pl", last("p4"))
            ts(v("pu"), now, col("cr", 0), A.mult, -1.0, A.add)
            ts(v("rs", 5, 96, 6), now, col("cr", 7), A.mult, -1.0 / C, A.add)
            if t == R - 2:
                fourfold("n4", NODE_AT[t + 1], 0, C)
                for p in range(4):
                    act(half(v("NA"), p, 4), at(v("NR"), half(v("n4"), p, 4)), F.Copy)
                for e in range(4):
                    scan(half(v("NC"), e, 4), v("c16"), v("NA", e, 1024, 4), 0.0, A.mult, A.max)
                ts(v("n4"), v("NC", 15, 1024, 16), col("cr", 6), A.mult, -1.0, A.add)
        else:
            for e in range(4):
                pick(NAMES[0][e], v("NA", e, 1024, 4), at(v("p4"), half(v("n4"), e, 4)))
            for p in range(4):
                if NAMES[1][p] == "V":
                    ts(half(v("ON"), p, 4), at(v("NA"), half(v("l4"), p, 4)), -1.0, A.add)
                else:
                    act(half(v("ON"), p, 4), at(v("NA"), half(v("l4"), p, 4)), F.Identity, bias=-1.0)
            dma("S", "out", [v("ON")], [], T.on[:], T.ON[0:128:16, :], rows=8)

    def mix(t):
        for b, (name, a) in enumerate(WIDE):
            mm(v(name, a, a + 128), "qe", "se", 128 * b, "lq", "ls", K + K * t, 128)
            tt(v("ZH", b, 256, 4), v(name, a + K, a + 128), v("EH", b, 256, 4), A.add)
        quant("qh", "sh", 0, 128, v("ZH"))
        if t == R - 1:
            layer("qh", "sh", 0, 0, K, RELU[2], WIDE, "TT", ("qf", "sf"))
        else:
            layer("qh", "sh", 0, 0, K, RELU[2])

    for t in range(R):
        ranking(t)
        move(t, order(t))

    def leave(q_, s_, a, b, name, e, first, second):
        n = max(b - a, 128)
        mm(v(name, 0, n), "qv", "sv", 0, q_, s_, a, n)
        dma(first, "out", [v(q_, a, b)], [], T.oc[:, 4 * a:4 * b], ap(v(q_, a, b), dt.uint8))
        for k in range(4):
            dma(second if k else first, "out", [v(s_, a, b)], [], T.osc[4 * k:4 * k + 4, a:b], T[s_][32 * k:32 * k + 4, a:b])
        pick(e, v("ys", a, b), v(name, 0, b - a))
        dma(first, "out", [v("ys", a, b)], [], T.y[:, a:b], T.ys[:, a:b])

    mix(R - 1)
    leave("qx", "sx", K, C, "pc", "S", "Y", "Y")
    leave("qf", "sf", 0, K, "pd", "V", "Y", "S")
    issue()
    for s in SEMAPHORES:
        if count[s]:
            g.wait_ge(T.sem[s], count[s])
